import numpy as np, ml_dtypes
CORES = [35,38,43,46]
N = 4
BF = ml_dtypes.bfloat16
W, L, M, P, Q, F, RO = 4096, 32, 4, 16, 32, 4, 2
CAP = (N - 1) * Q
def look(u, m):
    return (u * (u >> 5) + (2 * m + 1) * u) & (W - 1)
def pick(x, ix):
    return np.take_along_axis(x, ix[..., None, :], -1)
def pack(x, w, th):
    return {"x0": np.ascontiguousarray(x.reshape(N, 128, W)).astype(np.float32).astype(BF), "wt": np.ascontiguousarray(w).reshape(N, 128, 1).astype(np.float32).astype(BF),
            "th": np.repeat(th, 16, axis=1).astype(np.int32)}
def texture(rng):
    x = np.empty((N, 8, 16, W), np.int64); stock = rng.permutation(np.array([8, 24, 60, 120, 200, 300, 400, 600]))
    for g in range(8):
        n = int(stock[g]); base = rng.integers(0, 256, (n, 16))
        for q in range(N):
            e = 1.5 + rng.random()
            x[q, g] = (base[np.minimum((n * rng.random(W) ** e).astype(np.int64), n - 1)] + rng.integers(-2, 3, (W, 16))).T
    return np.clip(x, 0, 255)
def far(rng):
    return rng.integers(0, 256, (N, 8, 16, W))
def weights(rng):
    w = rng.integers(0, 256, (8, 16)); w[:, 0] = 1; w[:, 1] = 16; w[:, 13:] = 0
    return w
def with_hash(rng, w, u):
    k = rng.integers(0, 256, (len(u), 16)); v = (u - k[:, 2:] @ w[2:]) & (W - 1)
    k[:, 0] = v & 15; k[:, 1] = v >> 4
    return k
def odd(rng, m, n):
    u = np.arange(1, W, 2); u = rng.permutation(u[((u >> 5) & 1) == 0])
    i = np.unique(look(u, m), return_index=True)[1]
    assert len(i) >= n
    return rng.permutation(u[i])[:n]
def runs(rng):
    r = W // (L + F); n = min(r, CAP + 12)
    return L * np.sort(rng.permutation(r)[:n]) + L - 2
def setup_inputs(rng):
    return pack(texture(rng), rng.integers(0, 256, (N, 8, 16)), rng.integers(20, 41, (N, 8, 2)))
def setup_inputs_room(rng):
    x = far(rng); w = weights(rng); th = np.stack([rng.integers(1, 60, (N, 8)), rng.choice(np.array([1, 2, 40]), (N, 8))], axis=-1)
    th[rng.integers(0, N), rng.integers(4, 6), 1] = 0
    for g in range(8):
        m = g % M; p = runs(rng); n = len(p); u = odd(rng, m, n); c = look(u, m); k = with_hash(rng, w[g], u)
        for q in range(N):
            a = int(rng.choice(np.array([0, 1, CAP - 1, CAP, CAP + 1, n])))
            if q == 0: a = (CAP, CAP + 1, n, CAP - 1, 1, 0, CAP, CAP + 1)[g]
            i = rng.permutation(n)[:a]
            x[q, g][:, c] = k.T; x[q, g][:, p[i]] = k[i].T
    return pack(x, np.broadcast_to(w, (N, 8, 16)), th)
def setup_inputs_ties(rng):
    x = far(rng); w = weights(rng); t = rng.integers(2, 250, 8); t2 = t + rng.integers(-1, 2, (N, 8))
    for g in range(1, 8, 2):
        a = 4 * int(rng.integers(65, 124)) + g % 4; t2[:, g] = a; t[g] = a + int(rng.integers(0, 2))
    th = np.stack([np.broadcast_to(t, (N, 8)), t2], axis=-1)
    for g in range(8):
        m = g % M; p = runs(rng); n = len(p); u = odd(rng, m, n); k = with_hash(rng, w[g], u); k[:, 13:] = 0; more = 255 * (g % 2)
        for q in range(N):
            for c in (look(u, m + 1), look(u, m)):
                z = k + 0; z[:, 14] = rng.integers(0, 3, n); x[q, g][:, c] = z.T
            z = k + 0; z[:, 13] = more; z[:, 15] = t[g] - more + rng.integers(-2, 1, n); x[q, g][:, p] = z.T
    return pack(x, np.broadcast_to(w, (N, 8, 16)), th)
def over_the_end(rng, x, w, g):
    p = W - L - 2; every = np.arange(W); first = look(every, 0); later = look(every, np.arange(1, P)[:, None])
    good = (first >= L) & (first < p - L)
    j, uk = np.nonzero((later > W - F) & good & ~np.any(later == p, axis=0))
    i = int(rng.integers(0, len(uk))); u = int(uk[i]); c1 = int(first[u]); c2 = int(later[j[i], u])
    a = int(rng.choice(every[good & (first != c1)])); ca = int(first[a])
    k = with_hash(rng, w[g], np.array([u]))[0]; k[15] = 0; near = k + 0; near[15] = 3
    ka = with_hash(rng, w[g], np.full(N, a))
    for q in range(N):
        x[q, g][:, [0, ca]] = ka[q][:, None]; x[q, g][:, c1] = near; x[q, g][:, [p, c2 - F]] = k[:, None]
def setup_inputs_ends(rng):
    x = far(rng); w = weights(rng); th = rng.integers(1, 60, (N, 8, 2))
    mm, uu = np.nonzero(look(np.arange(W), np.arange(M)[:, None]) >= W - L // 2)
    for g in range(8):
        if g % 4 == 3:
            over_the_end(rng, x, w, g); th[:, g] = rng.integers(4, 60, (N, 2))
            continue
        if g % 2 == 0:
            o = rng.permutation(len(uu)); c, i = np.unique(look(uu[o], mm[o]), return_index=True); u = uu[o][i]; p = L * rng.permutation(len(u))
        else:
            u = odd(rng, g % M, 1); c = look(u, g % M); p = np.array([W - 2])
        k = with_hash(rng, w[g], u)
        for q in range(N):
            x[q, g][:, c] = k.T; x[q, g][:, p] = k.T
    return pack(x, np.broadcast_to(w, (N, 8, 16)), th)
def setup_inputs_alike(rng):
    x = texture(rng); w = rng.integers(0, 256, (N, 8, 16)); th = rng.integers(20, 41, (N, 8, 2))
    for g in range(0, 8, 2):
        base = rng.integers(0, 256, (4, 16)); x[:, g] = base[rng.integers(0, 4, (N, W))].transpose(0, 2, 1)
    th[:, 0] = 1; th[:, 2] = 4096; th[:, 4, 0] = 0; th[:, 1, 0] = 4096; th[:, 1, 1] = 0; th[:, 3, 1] = 4096
    w[:, 6] = 0; w[:, 5] = 255
    x[:, 1, :, 0] = 255
    w[:, 7] = rng.integers(230, 256, (N, 16))
    up = rng.random((N, 1, W)) < 0.5; up[::2] = False
    x[:, 7] = np.where(up, 255 - rng.integers(0, 40, (N, 16, W)), rng.integers(0, 40, (N, 16, W)))
    for q in range(N):
        x[q, 1][:, L * (1 + rng.permutation(W // L - 1)[:W // L // 2])] = 0
        if q % 2 == 0:
            th[q, 7, 0] = rng.integers(150, 260); th[q, 7, 1] = rng.integers(3100, 3600)
        else:
            th[q, 7, 0] = rng.integers(2048, 3000); th[q, 7, 1] = rng.integers(100, 4097)
            c = look((255 * int(np.sum(w[q, 7]))) & (W - 1), 0); x[q, 7][:, [0, L, c]] = 255
    th[0, 7, 1] = 4096
    return pack(x, w, th)
def setup_inputs_spread(rng):
    x = np.minimum((np.exp2(8 * rng.random((N, 8, 1, W))) * rng.random((N, 8, 16, W))).astype(np.int64), 255)
    w = np.minimum(np.exp2(8 * rng.random((N, 8, 16))).astype(np.int64), 255) * (rng.random((N, 8, 16)) > 0.0625)
    return pack(x, w, np.minimum(np.exp2(12 * rng.random((N, 8, 2))).astype(np.int64), 4096))
def check_inputs(d):
    bad = []
    for k in ("x0", "wt"):
        v = np.asarray(d[k]).astype(np.float32)
        if not np.all((v >= 0) & (v <= 255) & (v == np.floor(v))): bad.append("whole numbers of " + k)
    v = np.asarray(d["th"])
    if np.min(v) < 0 or np.max(v) > 4096: bad.append("range of th")
    v = v.reshape(N, 8, 16, 2)
    if np.any(v != v[:, :, :1]): bad.append("rows of th alike in a group")
    return bad
def reference(x0, wt, th):
    x = x0.astype(np.float32).astype(np.int64).reshape(N, 8, 16, W); w = wt.astype(np.float32).astype(np.int64).reshape(N, 8, 16, 1)
    t = th.astype(np.int64).reshape(N, 8, 16, 2)[:, :, 0]; here = np.arange(W)
    for rnd in range(RO):
        u = np.add.reduce(w * x, axis=2) & (W - 1)
        nx = np.zeros_like(u) + ((here + 1) & (W - 1))
        for m in range(M - 1, -1, -1):
            c = look(u, m); near = np.add.reduce(np.abs(pick(x, c) - x), axis=2) < t[..., :1]
            nx = np.where(near, (c + 1) & (W - 1), nx)
        s = np.zeros((N, 8, W // L, L), np.int64); s[..., 0] = L * np.arange(W // L)
        for k in range(1, L): s[..., k] = np.take_along_axis(nx, s[..., k - 1], -1)
        jump = np.zeros(s.shape, bool); jump[..., :-1] = s[..., 1:] != ((s[..., :-1] + 1) & (W - 1))
        s = s.reshape(N, 8, W); jump = jump.reshape(N, 8, W)
        site = np.argsort(~jump, axis=-1, kind="stable")[..., :CAP]
        live = np.take_along_axis(jump, site, -1); ask = pick(x, np.take_along_axis(s, site, -1))
        found = np.zeros((N, 8, CAP), bool); fill = np.zeros((N, 8, 16, CAP, F), np.int64)
        for q in range(N):
            for d in range(1, N):
                b = (q + d) % N; cut = slice((d - 1) * Q, d * Q); a = ask[q][:, :, cut]
                v = np.add.reduce(w[b] * a, axis=1) & (W - 1); c = look(v[..., None], np.arange(P))
                off = np.add.reduce(np.abs(pick(x[b], c.reshape(8, -1)).reshape(8, 16, Q, P) - a[..., None]), axis=1)
                best = np.take_along_axis(c, np.argmin(off, axis=-1)[..., None], -1)
                found[q][:, cut] = np.min(off, axis=-1) < t[b][:, 1:]
                fill[q][:, :, cut] = pick(x[b], ((best + 1 + np.arange(F)) & (W - 1)).reshape(8, -1)).reshape(8, 16, Q, F)
        found = found & live
        more = np.zeros((N, 8, W), np.int64); np.put_along_axis(more, site, found.astype(np.int64) * F, -1)
        place = here + np.add.accumulate(more, axis=-1) - more
        z = np.zeros((N, 8, 16, W + F * CAP + 1), np.int64)
        np.put_along_axis(z, place[:, :, None], pick(x, s), -1)
        at = np.take_along_axis(place, site, -1)[..., None] + 1 + np.arange(F)
        at = np.where(found[..., None], at, W + F * CAP).reshape(N, 8, 1, CAP * F)
        np.put_along_axis(z, at, fill.reshape(N, 8, 16, CAP * F), -1)
        x = np.ascontiguousarray(z[..., :W])
    return {"y": x.reshape(N, 128, W).astype(np.float32).astype(BF)}

@@ -1,0 +1,773 @@
+import numpy as np
+from concourse.bass import DstId, RemoteDMATransfer
+from concourse.mybir import dt, AluOpType as OP, AxisListType, ActivationFunctionType as AF
+
+W = 4096
+RO = 2
+XW = 5184
+F32, BF, I32, U16, F16 = "float32", "bfloat16", "int32", "uint16", "float16"
+SEGS = [(0, 192), (192, 256)]
+ON_SCALAR = ((1, 3),)
+TEN = ((0, 5), (5, 5))
+VEC = ((10, 3), (13, 3))
+WAKE = 0.06
+CY = 0.00083
+
+SCRATCH = {}
+PLACE = {}
+
+
+def _buf(where, cols, dtype, *names):
+    for n in names:
+        SCRATCH[n] = (where, [128, cols], dtype)
+        PLACE[n] = (n, 0, cols)
+
+
+def _pack(cols, dtype, host, *names):
+    SCRATCH[host] = ("sbuf", [128, cols * len(names)], dtype)
+    for i, n in enumerate(names):
+        PLACE[n] = (host, cols * i, cols)
+
+
+_buf("sbuf", XW, BF, "XA", "XB")
+_buf("sbuf", W, BF, "Y0", "XR00", "XR01", "XR02", "XR10", "XR11", "XR12")
+_buf("sbuf", W, F32, "NX1", "NX2")
+_buf("sbuf", 1024, BF, "DD0", "DD1", "DD2", "DD3", "GA0", "GA1", "AB0", "AB1")
+_pack(256, I32, "hI", "CC3", "QI", "DI", "KI", "NXI", "UI", "HI")
+_pack(256, U16, "hU", "CL3", "NXL", "SRL")
+_pack(256, F32, "hF", "CN0", "CN1", "CN2", "CN3", "QF", "DEF", "K2", "SB", "FF", "CU", "WD", "SR", "KEY0", "KEY1")
+_pack(768, I32, "kI", "CCX", "TM")
+_buf("sbuf", 768, U16, "CLX")
+_buf("sbuf", 256, F16, "NXH")
+_pack(128, I32, "gI", "J15", "JG", "J7")
+_pack(128, F32, "gF", "MASK", "KEEP", "KP8", "R0", "R1", "Z0", "Z1", "Z2", "Z3", "TT0", "TT1")
+_pack(128, U16, "gU", "LE", "LO")
+_buf("sbuf", 640, F32, "RO0", "RO1")
+_buf("sbuf", 384, F32, "ROV0", "ROV1", "ZOV0", "ZOV1", "MASK3", "KEEP3")
+_buf("sbuf", 512, F32, "IDV", "WTS")
+_buf("sbuf", 512, I32, "JI", "PB8")
+_buf("sbuf", 4608, F32, "SW")
+_buf("sbuf", 1312, F32, "WA", "WB")
+_buf("sbuf", 144, BF, "EZ", "EW", "EX")
+_buf("sbuf", 144, F32, "EZF")
+_buf("sbuf", 128, BF, "BB", "IDN", "NID", "LT", "UT", "LT4", "BB4", "WB0", "WB1", "WB2")
+_buf("sbuf", 2048, F16, "SEL")
+_buf("sbuf", 16, I32, "TH", "IC")
+_buf("sbuf", 16, F32, "FC")
+_buf("sbuf", 16, BF, "WT")
+_buf("sbuf", 4, F32, "PAR", "PR0", "PR1", "PR2")
+_pack(40, BF, "sB", "EB", "CX", "CS", "FB6")
+_buf("sbuf", 32, F16, "W16")
+_pack(32, F32, "sF", "TRJ", "ZE", "OF", "TR6", "M2", "F4", "F41", "T0F", "UF", "UF2", "I6", "IT6", "LV", "KM", "FD", "FS",
+      "CBF", "P1", "XF", "Q6", "FIF", "FPF")
+_pack(32, U16, "sU", "OL", "JL", "PL", "FL", "FP", "SL")
+_pack(48, I32, "sI", "BI", "VI", "JX", "RX", "PX", "WI", "U6", "H6", "M6", "CB", "FI", "PI6", "SI6", "X6")
+_pack(48, F32, "tF", "BF8", "CM8", "IN8")
+_pack(96, F32, "uF", "KN", "CD", "RR", "VM", "ZV")
+_pack(96, I32, "uI", "TI")
+_pack(96, U16, "uU", "TL")
+_pack(96, BF, "uB", "AQ", "MK", "EXB")
+_buf("sbuf", 1536, BF, "AR", "AD")
+_buf("sbuf", 384, BF, "FB")
+_buf("psum", 512, F32, "P0", "P7")
+_buf("psum", 1024, F32, "P12", "P34", "P56")
+
+NDMA = 20
+SEMAPHORES = ["sV", "sA", "sT", "sG", "par", "lpar"] + ["d%d" % i for i in range(NDMA)]
+SEMAPHORES += ["%s%d%d" % (k, r, h) for k in ("am", "ap", "aq", "lx", "lf") for r in range(RO) for h in range(2)]
+
+
+def rank_program(g, core, T, topo):
+    rank = T.rank_of(core)
+    if rank is None:
+        return
+    cores = list(T.cores)
+    N = len(cores)
+    queue = {"V": g.vector, "A": g.scalar, "P": g.tensor, "G": g, "S": g.sync}
+    qsem = {"V": "sV", "A": "sA", "P": "sT", "G": "sG"}
+    count = {}
+    known = {q: {} for q in queue}
+    snap = {}
+    log = {}
+    ndma, now = [0], [0]
+
+    def v(name, lo=0, hi=None, st=1):
+        host, base, cols = PLACE[name]
+        return (host, base + lo, base + (cols if hi is None else hi), st)
+
+    def ap(x):
+        n, lo, hi, st = x
+        return T[n][:, lo:hi] if st == 1 else T[n][:, lo:hi:st]
+
+    def arg(x):
+        return ap(x) if isinstance(x, tuple) else x
+
+    def ind(win, off):
+        return ("ind", win, off)
+
+    def opnd(x):
+        if x[0] == "ind":
+            return ap(x[1]).indirect(ap(x[2]))
+        return ap(x)
+
+    def hits(a, b):
+        if a[1] <= b[0] or b[1] <= a[0]:
+            return False
+        if a[2] == b[2] and a[2] > 1 and (a[0] - b[0]) % a[2]:
+            return False
+        return True
+
+    def inside(a, lo, hi, st):
+        return a[0] >= lo and a[1] <= hi and (st == 1 or (a[2] == st and (a[0] - lo) % st == 0))
+
+    def bank(x):
+        n, lo, hi, st = x
+        if SCRATCH[n][0] == "psum":
+            return n, lo // 512 * 512, (hi + 511) // 512 * 512, 1
+        return x
+
+    def wait(q, sem, n):
+        if known[q].get(sem, 0) >= n:
+            return
+        queue[q].wait_ge(T.sem[sem], n)
+        known[q][sem] = n
+        for k, c in snap.get((sem, n), {}).items():
+            if known[q].get(k, 0) < c:
+                known[q][k] = c
+
+    def order(q, reads, writes):
+        need = {}
+        for lst, wr in ((reads, False), (writes, True)):
+            for x in lst:
+                n, lo, hi, st = bank(x)
+                ps = SCRATCH[n][0] == "psum"
+                for a in log.get(n, ()):
+                    aq, aw = a[3], a[4]
+                    if not hits((lo, hi, st), a):
+                        continue
+                    if aq == q and q in qsem:
+                        if not (aw or wr) or (ps and q == "P"):
+                            continue
+                    elif not (aw or wr or ps):
+                        continue
+                    if need.get(a[5], 0) < a[6]:
+                        need[a[5]] = a[6]
+        for sem in sorted(need, key=lambda s: -need[s]):
+            wait(q, sem, need[sem])
+
+    def note(q, reads, writes, sem, n):
+        for lst, wr in ((reads, False), (writes, True)):
+            for x in lst:
+                nm, lo, hi, st = bank(x)
+                l = log.setdefault(nm, [])
+                if wr:
+                    l[:] = [a for a in l if not inside(a, lo, hi, st)]
+                else:
+                    l[:] = [a for a in l if not (a[3] == q and not a[4] and a[0] >= lo and a[1] <= hi and a[2] == st and st == 1)]
+                l.append((lo, hi, st, q, wr, sem, n))
+
+    ops = []
+
+    def record(q, reads, writes, cost, lag, issue):
+        rd, wr = [], []
+        for x in reads:
+            if isinstance(x, tuple):
+                rd += [x[1], x[2]] if x[0] == "ind" else [x]
+        for x in writes:
+            if x[0] == "ind":
+                wr.append(x[1])
+                rd.append(x[2])
+            else:
+                wr.append(x)
+        ops.append((q, rd, wr, cost, lag, issue))
+
+    def plan():
+        seen, preds, last = {}, [], {}
+        for i, (q, rd, wr, _, _, _) in enumerate(ops):
+            ps = set()
+            for lst, w in ((rd, False), (wr, True)):
+                for x in lst:
+                    n, lo, hi, st = bank(x)
+                    psum = SCRATCH[n][0] == "psum"
+                    for a in seen.get(n, ()):
+                        if hits((lo, hi, st), a) and (a[4] or w or (psum and ops[a[3]][0] != q)):
+                            ps.add(a[3])
+            if q in ("G", "S"):
+                if q in last:
+                    ps.add(last[q])
+                last[q] = i
+            for lst, w in ((rd, False), (wr, True)):
+                for x in lst:
+                    n, lo, hi, st = bank(x)
+                    l = seen.setdefault(n, [])
+                    if w:
+                        l[:] = [a for a in l if not inside(a, lo, hi, st)]
+                    l.append((lo, hi, st, i, w))
+            ps.discard(i)
+            preds.append(ps)
+        succ = [[] for _ in ops]
+        for i, ps in enumerate(preds):
+            for j in ps:
+                succ[j].append(i)
+
+        def between(i, j):
+            return 0.0 if ops[i][0] == ops[j][0] and ops[i][0] in ("P", "G", "S") else WAKE + ops[i][4]
+
+        prio = [0.0] * len(ops)
+        for i in range(len(ops) - 1, -1, -1):
+            prio[i] = ops[i][3] + max([prio[j] + between(i, j) for j in succ[i]], default=0.0)
+        left = [len(p) for p in preds]
+        at = [0.0] * len(ops)
+        free, ready, res = {}, {}, []
+        for i in range(len(ops)):
+            if not left[i]:
+                ready.setdefault(ops[i][0], []).append(i)
+        while ready:
+            best = None
+            for q, c in ready.items():
+                f = 0.0 if q is None else free.get(q, 0.0)
+                t0 = min(max(f, at[i]) for i in c)
+                if best is None or t0 < best[0]:
+                    best = (t0, q, f)
+            t0, q, f = best
+            c = ready[q]
+            i = max((i for i in c if max(f, at[i]) <= t0), key=lambda i: (prio[i], -i))
+            c.remove(i)
+            if not c:
+                del ready[q]
+            e = max(f, at[i]) + ops[i][3]
+            free[q] = e
+            res.append(i)
+            for j in succ[i]:
+                at[j] = max(at[j], e + between(i, j))
+                left[j] -= 1
+                if not left[j]:
+                    ready.setdefault(ops[j][0], []).append(j)
+        return res
+
+    def many(x):
+        if x[0] == "ind":
+            return 16 * (x[2][2] - x[2][1])
+        return (x[2] - x[1] + x[3] - 1) // x[3]
+
+    def half(x):
+        return SCRATCH[(x[1] if x[0] == "ind" else x)[0]][2] in (BF, U16, F16)
+
+    def cost(q, kind, out, ins):
+        n = many(out)
+        if kind == "mm":
+            return 0.00071 * max(64, many(ins[1])) * (4 if SCRATCH[ins[0][0]][2] == F32 else 1)
+        if kind == "iota":
+            return 0.13 + 2 * n * CY
+        if out[0] == "ind":
+            return 0.05 + 3.5 * n * CY
+        if any(x[0] == "ind" for x in ins):
+            return 0.05 + 1.5 * n * CY
+        if kind == "tt" and not any(SCRATCH[x[0]][0] == "psum" for x in ins):
+            n = 2 * n
+        if kind == "ts" and all(half(x) for x in ins + [out]):
+            n = n / 2
+        return max(n, 64) * CY + (0.05 if q == "A" else 0.03)
+
+    def emit(q, kind, reads, writes, fn):
+        def issue():
+            rd, wr = ops[now[0]][1:3]
+            order(q, rd, wr)
+            s = qsem[q]
+            count[s] = count.get(s, 0) + 1
+            fn(queue[q]).then_inc(T.sem[s], 1)
+            snap[(s, count[s])] = dict(known[q])
+            note(q, rd, wr, s, count[s])
+        record(q, reads, writes, cost(q, kind, writes[0], [x for x in reads if isinstance(x, tuple)]), 0.0, issue)
+
+    def dma(q, out, in_, reads, writes):
+        s = "d%d" % ndma[0]
+        ndma[0] += 1
+
+        def issue():
+            order(q, reads, writes)
+            count[s] = 16
+            queue[q].dma_start(out, in_).then_inc(T.sem[s], 16)
+            snap[(s, 16)] = dict(known[q])
+            note(q + "dma", reads, writes, s, 16)
+        record(q, reads, writes, 0.1, 3.5, issue)
+
+    def tt(out, a, b, op):
+        emit("V", "tt", [a, b], [out], lambda e: e.tensor_tensor(opnd(out), opnd(a), opnd(b), op))
+
+    def ts(out, a, s1, op0, s2=None, op1=None):
+        def f(e):
+            if op1 is None:
+                return e.tensor_scalar(ap(out), opnd(a), arg(s1), None, op0)
+            return e.tensor_scalar(ap(out), opnd(a), arg(s1), arg(s2), op0, op1)
+        emit("V", "ts", [a, s1, s2], [out], f)
+
+    def cp(q, out, a):
+        if q == "V":
+            emit("V", "ts", [a], [out], lambda e: e.tensor_copy(opnd(out), opnd(a)))
+        else:
+            emit("A", "", [a], [out], lambda e: e.activation(ap(out), opnd(a), AF.Copy))
+
+    def act(out, a, func, bias=0.0, scale=1.0):
+        emit("A", "", [a, bias, scale], [out], lambda e: e.activation(ap(out), opnd(a), func, bias=arg(bias), scale=arg(scale)))
+
+    def fill(out, c):
+        emit("V", "ts", [], [out], lambda e: e.memset(ap(out), c))
+
+    def scan(out, a, b, op0, op1, init=0.0):
+        emit("V", "", [a, b, init], [out], lambda e: e.tensor_tensor_scan(ap(out), ap(a), ap(b), arg(init), op0, op1))
+
+    def mm(out, l, r, start=True, stop=True):
+        emit("P", "mm", [l, r], [out], lambda e: e.matmul(ap(out), ap(l), ap(r), start, stop))
+
+    def iota(out, pattern, base, cm):
+        if SCRATCH[out[0]][2] == I32:
+            emit("G", "iota", [], [out], lambda e: e.iota(ap(out), pattern, base, cm))
+        else:
+            emit("G", "iota", [], [out], lambda e: e.iota(ap(out), pattern, base, cm, allow_small_or_imprecise_dtypes=True))
+
+    def ez(n, a):
+        return v(n, 15 - a, 143 - a)
+
+    def sel(a):
+        return v("SEL", 128 * a, 128 * a + 128)
+
+    AND, SHR = OP.bitwise_and, OP.logical_shift_right
+    wtq = v("WT", 0, 1)
+    dma("S", ap(wtq), T.wt[:], [], [wtq])
+    dma("A", ap(v("TH", 0, 2)), T.th[:], [], [v("TH", 0, 2)])
+    for n in ("XA", "Y0"):
+        for c in range(4):
+            x = v(n, 1024 * c, 1024 * c + 1024)
+            dma("SA"[c % 2], ap(x), T.x0[:, 1024 * c:1024 * c + 1024], [], [x])
+    iota(v("IC", 0, 1), [[1, 1]], 0, 1)
+    iota(v("JI"), [[1, 512]], 0, 0)
+    iota(v("QI"), [[16, 256]], 0, 1)
+    iota(v("PB8"), [[64, 8], [1, 4], [4, 16]], 0, 0)
+    ts(v("IC", 1, 2), v("IC", 0, 1), 15, AND)
+    ts(v("IC", 2, 3), v("IC", 0, 1), 112, AND)
+    fill(v("EZ"), 0.0)
+    fill(v("PAR", 2, 4), 0.0)
+    cp("V", v("FC", 0, 3), v("IC", 0, 3))
+    pf, p15, pg, t1 = v("FC", 0, 1), v("FC", 1, 2), v("FC", 2, 3), v("FC", 3, 4)
+    J = v("JI", 0, 128)
+    cp("V", v("PAR", 0, 1), wtq)
+    ts(v("PAR", 1, 2), v("TH", 1, 2), 16.0, OP.mult)
+    cp("V", t1, v("TH", 0, 1))
+    ts(v("EZ", 15, 143), J, pg, OP.is_equal)
+    ts(v("IDN"), J, pf, OP.is_equal)
+    ts(v("EW"), v("EZ"), wtq, OP.mult)
+    ts(v("NID"), J, pf, OP.is_equal, -1.0, OP.mult)
+    ts(v("QF"), v("QI"), pg, OP.subtract)
+    ts(v("J15"), J, 15, AND)
+    ts(v("JG"), J, 112, AND)
+    ts(v("J7"), J, 7, AND)
+    ts(v("MASK"), v("J15"), p15, OP.is_equal)
+    ts(v("BB"), v("JG"), pg, OP.is_equal)
+    ts(v("KEEP"), v("J15"), 0.0, OP.not_equal)
+    ts(v("KP8"), v("J7"), 0.0, OP.not_equal)
+    for a in range(16):
+        ts(sel(a), v("BB"), v("MASK", a, a + 1), OP.mult)
+    ts(v("DEF"), v("QF"), 32769.0, OP.add)
+    for k in range(3):
+        cp("A", v("MASK3", 128 * k, 128 * k + 128), v("MASK"))
+        cp("A", v("KEEP3", 128 * k, 128 * k + 128), v("KEEP"))
+    ts(v("K2", 0, 128), v("J7"), 0.0, OP.is_gt, 2.0, OP.mult)
+    ts(v("K2", 128, 256), v("J7"), 0.0, OP.is_gt, 2.0, OP.mult)
+    ts(v("BB4"), v("JG"), pg, OP.is_equal, 4.0, OP.mult)
+    ts(v("TT0"), J, pf, OP.is_gt)
+    ts(v("TT1"), J, pf, OP.is_lt)
+    tt(v("LT"), v("TT0"), v("BB"), OP.mult)
+    tt(v("UT"), v("TT1"), v("BB"), OP.mult)
+    ts(v("LT4"), v("LT"), 4.0, OP.mult)
+    ts(v("EX"), v("EZ"), 16.0, OP.mult)
+    ts(v("EZF"), v("EZ"), 0.0625, OP.mult)
+    ts(v("LE", 0, 8), v("QF", 0, 8), 32.0, OP.mult)
+    ts(v("SB", 0, 256, 32), v("QF", 0, 8), 32.0, OP.mult, -2048.0, OP.add)
+    ts(v("WTS"), v("PB8"), 4096.0, OP.mult, float(1 << 21), OP.add)
+    ts(v("IDV"), v("JI"), 8.0, OP.mult)
+    tt(v("IDV"), v("IDV"), v("WTS"), OP.add)
+    ts(v("TRJ"), v("QF", 0, 32), 4096.0, OP.add)
+    ts(v("TR6", 0, 6), v("QF", 0, 6), 4.0, OP.mult, 4800.0, OP.add)
+    ts(v("M2", 0, 16), v("JI", 0, 16), 2.0, OP.mult)
+    cp("V", v("F4", 0, 4), v("JI", 0, 4))
+    ts(v("F41", 0, 4), v("JI", 0, 4), 1.0, OP.add)
+    ts(v("TI"), v("JI", 0, 96), 1, SHR, 15, AND)
+    cp("V", v("MK"), v("TI"))
+    fill(v("EB", 0, 4), 0.0)
+    fill(v("CS", 0, 1), 0.0)
+
+    mine = topo.chip(core)
+    mate = [c for c in cores if topo.mates(topo.chip(c), mine) and topo.die(c) == topo.die(core)][0]
+    near = [c for c in cores if c != core and topo.chip(c) == mine][0]
+    diag = [c for c in cores if c not in (core, mate, near)][0]
+
+    def slot(receiver, owner):
+        return (T.rank_of(owner) - T.rank_of(receiver) - 1) % N
+
+    off = topo.engines(core, mate)
+    on = [e for e in topo.engines(core, near) if e not in off]
+
+    def dst(c):
+        a = topo.addr(c)
+        return DstId(rid=a[0], pnc=a[1])
+
+    def remote(transfers, local, reads):
+        n = sum(len(es) for _, _, _, es, _ in transfers)
+
+        def issue():
+            order("G", reads, [])
+            count[local] = count.get(local, 0) + n
+            g.remote_dma_fused([RemoteDMATransfer(dst_ids=[dst(c)], dma_engine_mask=sum(1 << e for e in es), remote_sem=T.sem[rs], src=s, dst=d)
+                                for c, s, d, es, rs in transfers], local_sem=T.sem[local])
+            snap[(local, count[local])] = dict(known["G"])
+            note("Gremote", reads, [], local, count[local])
+        record("G", reads, [], 1.0, 8.0, issue)
+
+    def arrives(name, lo, hi, sem, n, like=()):
+        def issue():
+            count[sem] = n
+            note("remote", [], [v(name, lo, hi)], sem, n)
+        record(None, list(like), [v(name, lo, hi)], 0.0, 12.0, issue)
+
+    for d in range(3):
+        arrives("PR%d" % d, 0, 4, "par", 3)
+
+    def send_params():
+        remote([(c, ap(v("PAR")), T["PR%d" % slot(c, core)][:], [es], "par")
+                for c, es in ((near, on[0]), (mate, off[0]), (diag, off[1]))], "lpar", [v("PAR")])
+
+    def halves():
+        return [(h, 2048 * h, 2048 * h + 2048) for h in range(2)]
+
+    def broadcast(rd, x):
+        for h, lo, hi in halves():
+            src = v(x, lo, hi)
+            remote([(mate, ap(src), T["XR%d%d" % (rd, slot(mate, core))][:, lo:hi], off, "am%d%d" % (rd, h)),
+                    (near, ap(src), T["XR%d%d" % (rd, slot(near, core))][:, lo:hi], on, "ap%d%d" % (rd, h))], "lx%d%d" % (rd, h), [src])
+        for h, lo, hi in halves():
+            src = v(x, lo, hi)
+            a, b, c = ("XR%d%d" % (rd, slot(core, o)) for o in (mate, near, diag))
+            arrives(a, lo, hi, "am%d%d" % (rd, h), len(off), [src])
+            arrives(b, lo, hi, "ap%d%d" % (rd, h), len(on), [src])
+            arrives(c, lo, hi, "aq%d%d" % (rd, h), len(on), [src])
+
+    def hand_on(rd):
+        for h, lo, hi in halves():
+            src = v("XR%d%d" % (rd, slot(core, mate)), lo, hi)
+            remote([(near, ap(src), T["XR%d%d" % (rd, slot(near, mate))][:, lo:hi], on, "aq%d%d" % (rd, h))], "lf%d%d" % (rd, h), [src])
+
+    for rd in range(RO):
+        X, Xn = ("XA", "XB") if rd % 2 == 0 else ("XB", "XA")
+        if rd > 0:
+            for c in range(4):
+                x, y = v(X, 1024 * c, 1024 * c + 1024), v("Y0", 1024 * c, 1024 * c + 1024)
+                dma("S", ap(y), ap(x), [x], [y])
+        broadcast(rd, X)
+        if rd == 0:
+            send_params()
+        iota(v("SW", 0, 96), [[0, 96]], 0, 0)
+        iota(v("WA", 0, 1024), [[0, 1024]], 0, 0)
+        iota(v("WB", 4, 1032), [[0, 1028]], 0, 0)
+        hand_on(rd)
+        hb = ["P0", "P7"]
+        for s, (lo, hi) in enumerate(SEGS):
+            for a in range(16):
+                mm(v(hb[s], 0, hi - lo), ez("EW", a), v(X, 16 * lo + a, 16 * hi, 16), a == 0, a == 15)
+
+        def cl(m, lo, hi):
+            if m == 3:
+                return v("CL3", lo, hi)
+            s0, s1 = SEGS[0] if hi <= SEGS[0][1] else SEGS[1]
+            o = 3 * s0 + m * (s1 - s0) - s0
+            return v("CLX", o + lo, o + hi)
+
+        def looks(s):
+            lo, hi = SEGS[s]
+            w = hi - lo
+            u, hm, u2 = v("UI", 0, w), v(hb[s], w, 2 * w), v(hb[s], 0, w)
+            t = [v("TM", m * w, m * w + w) for m in range(3)]
+            cp("V", u, v(hb[s], 0, w))
+            ts(u, u, W - 1, AND)
+            ts(v("HI", 0, w), u, 5, SHR)
+            ts(hm, v("HI", 0, w), 7.0, OP.add)
+            tt(t[0], hm, u, OP.mult)
+            ts(v("CC3", lo, hi), t[0], W - 1, AND)
+            cp("V", v("CL3", lo, hi), v("CC3", lo, hi))
+            ts(hm, v("HI", 0, w), 1.0, OP.add)
+            tt(t[0], hm, u, OP.mult)
+            ts(u2, u, 2.0, OP.mult)
+            tt(t[1], u2, t[0], OP.add)
+            tt(t[2], u2, t[1], OP.add)
+            c = (3 * lo, 3 * hi)
+            ts(v("CCX", *c), v("TM", 0, 3 * w), W - 1, AND)
+            cp("V", v("CLX", *c), v("CCX", *c))
+
+        def keys(s):
+            lo, hi = SEGS[s]
+            w = hi - lo
+            for m in range(3):
+                ts(v("CN%d" % m, lo, hi), v("CCX", 3 * lo + m * w, 3 * lo + m * w + w), float(1 + 8192 * m), OP.add)
+            ts(v("CN3", lo, hi), v("CC3", lo, hi), float(1 + 8192 * 3), OP.add)
+
+        dn, an, kn = [0], [0], [0]
+
+        def dist(m, s):
+            lo, hi = SEGS[s]
+            w = hi - lo
+            if s == 0:
+                o = 512 * (m // 2) + w * (m % 2)
+                return v("P12", o, o + w)
+            return v("P34", 0, w) if m == 2 else v("P0", 64 * (m % 3) + 128 * (m // 3), 64 * (m % 3) + 128 * (m // 3) + w)
+
+        def reduce_abs(m, q, buf):
+            s = 0 if 64 * q + 64 <= SEGS[0][1] else 1
+            n, o, _, _ = dist(m, s)
+            o += 64 * q - SEGS[s][0]
+            for a in range(16):
+                mm((n, o, o + 64, 1), ez("EZ", a), v(buf, a, 1024, 16), a == 0, a == 15)
+
+        def unit(m, q):
+            win, x = ind(v(X, 0, W), cl(m, 64 * q, 64 * q + 64)), (1024 * q, 1024 * q + 1024)
+            if m == 3 or (m, q) in ON_SCALAR:
+                b, c = "GA%d" % (an[0] % 2), "AB%d" % (an[0] % 2)
+                an[0] += 1
+                for k in range(2):
+                    mm(v("P34", 512 * k, 512 * k + 512), v("NID"), v(X, x[0] + 512 * k, x[0] + 512 * k + 512), True, False)
+                cp("A", v(b), win)
+                for k in range(2):
+                    mm(v("P34", 512 * k, 512 * k + 512), v("IDN"), v(b, 512 * k, 512 * k + 512), False, True)
+                act(v(c), v("P34"), AF.Abs)
+            else:
+                c = "DD%d" % (dn[0] % 4)
+                dn[0] += 1
+                tt(v(c), win, v("Y0", *x), OP.subtract)
+                act(v(c), v(c), AF.Abs)
+            reduce_abs(m, q, c)
+
+        def nearest(s, ms):
+            lo, hi = SEGS[s]
+            w = hi - lo
+            o = (lo, hi)
+            pen, run = v("P56", 0, w), v("P56", 512, 512 + w)
+            for m in ms:
+                key = v("KEY%d" % (kn[0] % 2), 0, w)
+                kn[0] += 1
+                ts(pen, dist(m, s), t1, OP.is_ge, 65536.0, OP.mult)
+                tt(key, pen, v("CN%d" % m, *o), OP.add)
+                tt(v("KI", *o) if m == ms[-1] else run, v("DEF", *o) if m == ms[0] else run, key, OP.min)
+            ts(v("NXI", *o), v("KI", *o), W - 1, AND)
+            ts(v("NXH", *o), v("NXI", *o), -2048.0, OP.add)
+            cp("V", v("NXL", *o), v("NXI", *o))
+            banks = [("P56", 0), ("P56", 512), ("P7", 0)]
+            per = 512 // w
+            for i in range(0, 16, per):
+                bn, b0 = banks[i // per % 3]
+                for j in range(per):
+                    mm(v(bn, b0 + w * j, b0 + w * j + w), sel(i + j), v("NXH", *o))
+                for j in range(per):
+                    cp("VA"[i // per % 2], v("NX1", 16 * lo + i + j, 16 * hi, 16), v(bn, b0 + w * j, b0 + w * j + w))
+
+        for s in range(2):
+            looks(s)
+            keys(s)
+        for q in range(3):
+            for m in (3, 0, 1, 2):
+                unit(m, q)
+        for m in (3, 0, 1):
+            unit(m, 3)
+        nearest(0, (0, 1, 3, 2))
+        unit(2, 3)
+        nearest(1, (3, 0, 1, 2))
+        cp("V", v("NX2", 0, 2048), ind(v("NX1"), v("NXL", 0, 128)))
+        cp("A", v("NX2", 2048, 4096), ind(v("NX1"), v("NXL", 128, 256)))
+
+        def y0(k):
+            l = v("LE" if k % 2 == 0 else "LO", 8 * (k // 2), 8 * (k // 2) + 8)
+            cp("A", v("Y0", k, W, 32), ind(v(X, 0, W), l))
+
+        def sb_of(k):
+            return v("SB", k, 256, 32)
+
+        def odd_by_tensor(j, n, pb, ro):
+            cp("A", v(ro, 0, 128 * n), ind(v("NX1"), v("LE", 8 * j, 8 * j + 8 * n)))
+            for a in range(16):
+                mm(v(pb, 0, 8 * n), ez("EZF", a), v(ro, a, 128 * n, 16), a == 0, a == 15)
+            ts(v("LO", 8 * j, 8 * j + 8 * n), v(pb, 0, 8 * n), 2048.0, OP.add)
+            for k in range(n):
+                cp("A", sb_of(2 * (j + k) + 1), v(pb, 8 * k, 8 * k + 8))
+
+        def odd_by_vector(j, n, ro, zo):
+            w = 128 * n
+            tt(v(ro, 0, w), ind(v("NX1"), v("LE", 8 * j, 8 * j + 8 * n)), v("MASK3", 0, w), OP.mult)
+            scan(v(zo, 0, w), v("KEEP3", 0, w), v(ro, 0, w), OP.mult, OP.add)
+            ts(v("LO", 8 * j, 8 * j + 8 * n), v(zo, 15, w, 16), 2048.0, OP.add)
+            for k in range(n):
+                cp("V", sb_of(2 * (j + k) + 1), v(zo, 128 * k + 15, 128 * k + 128, 16))
+
+        for i in range(16):
+            le = v("LE", 8 * i, 8 * i + 8)
+            if i < 15:
+                r, z = v("R%d" % (i % 2)), "Z%d" % (i % 4)
+                tt(r, ind(v("NX2"), le), v("MASK"), OP.mult)
+                scan(v(z), v("KEEP"), r, OP.mult, OP.add)
+                ts(v("LE", 8 * i + 8, 8 * i + 16), v(z, 15, 128, 16), 2048.0, OP.add)
+                cp("A", sb_of(2 * i + 2), v(z, 15, 128, 16))
+            y0(2 * i)
+            for e in range(2):
+                for lst, fn in ((TEN, odd_by_tensor), (VEC, odd_by_vector)):
+                    j, n = lst[e]
+                    if i == j + n - 1:
+                        if fn is odd_by_tensor:
+                            fn(j, n, ("P0", "P7")[e], "RO%d" % e)
+                        else:
+                            fn(j, n, "ROV%d" % e, "ZOV%d" % e)
+                        for k in range(j, j + n):
+                            y0(2 * k + 1)
+        tt(v("DI", 0, 255), v("SB", 1, 256), v("SB", 0, 255), OP.subtract)
+        ts(v("DI", 0, 255), v("DI", 0, 255), W - 1, AND)
+        ts(v("FF", 0, 255), v("DI", 0, 255), 1.0, OP.not_equal)
+        fill(v("FF", 31, 256, 32), 0.0)
+        scan(v("CU"), v("FF"), v("FF"), OP.add, OP.max)
+        scan(v("WD"), v("K2"), v("FF"), OP.mult, OP.add)
+        for k in range(4):
+            cp("V", v("EB", 4 + k, 36, 4), v("CU", 31, 256, 32))
+        tt(v("CX", 0, 32), v("CU", 0, 256, 8), v("FF", 0, 256, 8), OP.subtract)
+        first = v("P12", 0, 32)
+        mm(first, v("LT"), v("EB", 4, 36), True, False)
+        mm(first, v("UT"), v("EB", 0, 32), False, False)
+        mm(first, v("IDN"), v("CX", 0, 32), False, True)
+        cp("V", v("W16"), v("WD", 7, 256, 8))
+        for a in range(16):
+            mm(v("P12", 512 + a, 1024, 16), sel(a), v("W16"))
+        cp("A", v("WTS"), v("P12", 512, 1024))
+        mm(v("P0", 0, 1), v("BB"), v("EB", 35, 36))
+        ts(v("ZE"), v("WD", 7, 256, 8), 0.0, OP.is_equal)
+        tt(v("ZE"), v("ZE"), v("TRJ"), OP.mult)
+        tt(v("OF"), first, v("ZE"), OP.max)
+        cp("V", v("OL"), v("OF"))
+        cp("V", ind(v("SW"), v("OL")), v("IDV"))
+        ts(v("KN"), v("SW", 0, 96), 0.0, OP.is_equal)
+        scan(v("CD"), v("KN"), v("SW", 0, 96), OP.mult, OP.add)
+        scan(v("RR"), v("KN"), v("KN"), OP.mult, OP.add)
+        tt(v("VM"), v("CD"), v("RR"), OP.add)
+        tt(v("VM"), v("VM"), v("MASK", 0, 96), OP.mult)
+        scan(v("ZV"), v("KEEP", 0, 96), v("VM"), OP.mult, OP.add)
+        cp("V", v("VI", 0, 6), v("ZV", 15, 96, 16))
+        ts(v("JX", 0, 6), v("VI", 0, 6), 3, SHR, 511, AND)
+        ts(v("RX", 0, 6), v("VI", 0, 6), 7, AND)
+        cp("V", v("JL", 0, 6), v("JX", 0, 6))
+        ts(v("PX", 0, 6), v("VI", 0, 6), 12, SHR, 511, AND)
+        tt(v("VM"), ind(v("WTS"), v("JL", 0, 6)), v("MASK", 0, 96), OP.mult)
+        ts(v("Q6", 0, 6), v("PX", 0, 6), 8.0, OP.mult)
+        scan(v("ZV"), v("KEEP", 0, 96), v("VM"), OP.mult, OP.add)
+        ts(v("LV", 0, 6), v("QF", 0, 6), v("P0", 0, 1), OP.is_lt)
+        cp("V", v("WI", 0, 6), v("ZV", 15, 96, 16))
+        for k in range(8):
+            ts(v("BI", k, 48, 8), v("WI", 0, 6), 7 - k, SHR, 1, AND)
+        cp("V", v("BF8"), v("BI"))
+        tt(v("BF8", 0, 48, 8), v("BI", 0, 48, 8), v("RX", 0, 6), OP.subtract)
+        scan(v("CM8"), v("KP8", 0, 48), v("BF8"), OP.mult, OP.add)
+        ts(v("IN8"), v("CM8"), 0.0, OP.is_le)
+        scan(v("CM8"), v("KP8", 0, 48), v("IN8"), OP.mult, OP.add)
+        tt(v("I6", 0, 6), v("Q6", 0, 6), v("CM8", 7, 48, 8), OP.add)
+        ts(v("PL", 0, 6), v("I6", 0, 6), 4095.0, OP.min)
+        cp("V", v("AQ"), ind(v("Y0"), v("PL", 0, 6)))
+        if rd == 0:
+            for d in range(3):
+                ts(v("WB%d" % d), v("BB"), v("PR%d" % d, 0, 1), OP.mult)
+        for d in range(3):
+            mm(v("P7", 32 * d, 32 * d + 32), v("WB%d" % d), v("AQ", 32 * d, 32 * d + 32))
+        for d in range(3):
+            o = 512 * d
+            cp("A", v("AR", o, o + 32), v("AQ", 32 * d, 32 * d + 32))
+            for w in (32, 64, 128, 256):
+                cp("A", v("AR", o + w, o + 2 * w), v("AR", o, o + w))
+        ts(v("IT6", 0, 6), v("I6", 0, 6), 1.0, OP.add)
+        tt(v("IT6", 0, 6), v("IT6", 0, 6), v("TR6", 0, 6), OP.subtract)
+        tt(v("VM"), v("P7", 0, 96), v("MASK", 0, 96), OP.mult)
+        scan(v("ZV"), v("KEEP", 0, 96), v("VM"), OP.mult, OP.add)
+        cp("V", v("U6", 0, 6), v("ZV", 15, 96, 16))
+        ts(v("U6", 0, 6), v("U6", 0, 6), W - 1, AND)
+        ts(v("H6", 0, 6), v("U6", 0, 6), 5, SHR)
+        cp("V", v("UF", 0, 6), v("U6", 0, 6))
+        ts(v("H6", 0, 6), v("H6", 0, 6), 1.0, OP.add)
+        ts(v("UF2", 0, 6), v("U6", 0, 6), 2.0, OP.mult)
+        tt(v("T0F", 0, 6), v("U6", 0, 6), v("H6", 0, 6), OP.mult)
+        for c in range(6):
+            ts(v("TI", 32 * (c // 2) + c % 2, 32 * (c // 2) + 32, 2), v("M2", 0, 16), v("UF", c, c + 1), OP.mult, v("T0F", c, c + 1), OP.add)
+        ts(v("TI"), v("TI"), W - 1, AND)
+        cp("V", v("TL"), v("TI"))
+        ky = "P12"
+        mm(v(ky, 0, 96), v("IDN"), v("MK"), True, False)
+        for d in range(3):
+            o = v("AD", 512 * d, 512 * d + 512)
+            tt(o, ind(v("XR%d%d" % (rd, d)), v("TL", 32 * d, 32 * d + 32)), v("AR", 512 * d, 512 * d + 512), OP.subtract)
+            act(o, o, AF.Abs)
+        for a in range(16):
+            mm(v(ky, 0, 96), ez("EX", a), v("AD", a, 1536, 16), False, a == 15)
+        for c in range(6):
+            o, i_ = v("KM", c, c + 1), v(ky, 32 * (c // 2) + c % 2, 32 * (c // 2) + 32, 2)
+            emit("V", "", [i_], [o], lambda e, o=o, i_=i_: e.tensor_reduce(ap(o), ap(i_), AxisListType.X, OP.min))
+        for d in range(3):
+            ts(v("FD", 2 * d, 2 * d + 2), v("KM", 2 * d, 2 * d + 2), v("PR%d" % d, 1, 2), OP.is_lt)
+        cp("V", v("M6", 0, 6), v("KM", 0, 6))
+        tt(v("FD", 0, 6), v("FD", 0, 6), v("LV", 0, 6), OP.mult)
+        ts(v("M6", 0, 6), v("M6", 0, 6), 15, AND)
+        scan(v("FS", 0, 6), v("FD", 0, 6), v("FD", 0, 6), OP.add, OP.max)
+        cp("V", v("FB6", 0, 6), v("FD", 0, 6))
+        cp("V", v("CS", 1, 7), v("FS", 0, 6))
+        tt(v("CBF", 0, 6), v("M6", 0, 6), v("UF2", 0, 6), OP.mult)
+        mm(v("P7", 0, 6), v("LT4"), v("FB6", 0, 6), True, False)
+        mm(v("P7", 0, 6), v("BB4"), v("CS", 0, 6), False, True)
+        tt(v("CB", 0, 6), v("CBF", 0, 6), v("T0F", 0, 6), OP.add)
+        tt(v("P1", 0, 6), v("P7", 0, 6), v("IT6", 0, 6), OP.add)
+        ts(v("CB", 0, 6), v("CB", 0, 6), W - 1, AND)
+        tt(v("P1", 0, 6), v("P1", 0, 6), v("FD", 0, 6), OP.mult)
+        cp("V", v("CBF", 0, 6), v("CB", 0, 6))
+        tt(v("P1", 0, 6), v("P1", 0, 6), v("TR6", 0, 6), OP.add)
+        cp("V", v("PI6", 0, 6), v("P1", 0, 6))
+        ts(v("X6", 0, 6), v("PI6", 0, 6), 15, AND)
+        ts(v("SI6", 0, 6), v("PI6", 0, 6), 2, SHR)
+        cp("V", v("XF", 0, 6), v("X6", 0, 6))
+        cp("V", v("SL", 0, 6), v("SI6", 0, 6))
+        for c in range(6):
+            if c % 2:
+                act(v("EXB", 16 * c, 16 * c + 16), v("MASK", 0, 16), AF.Copy, scale=v("XF", c, c + 1))
+            else:
+                ts(v("EXB", 16 * c, 16 * c + 16), v("MASK", 0, 16), v("XF", c, c + 1), OP.mult)
+        mm(v("P0", 0, 96), v("BB"), v("EXB"))
+        for c in range(6):
+            o = 8 * (c // 2) + c % 2, 8 * (c // 2) + 8, 2
+            act(v("FIF", *o), v("F41", 0, 4), AF.Identity, bias=v("CBF", c, c + 1))
+        cp("V", v("FI", 0, 24), v("FIF", 0, 24))
+        ts(v("FI", 0, 24), v("FI", 0, 24), W - 1, AND)
+        cp("V", v("FL", 0, 24), v("FI", 0, 24))
+        for d in range(3):
+            cp("A", v("FB", 128 * d, 128 * d + 128), ind(v("XR%d%d" % (rd, d)), v("FL", 8 * d, 8 * d + 8)))
+        for c in range(6):
+            o = 8 * (c // 2) + c % 2, 8 * (c // 2) + 8, 2
+            act(v("FPF", *o), v("F4", 0, 4), AF.Identity, bias=v("P1", c, c + 1))
+        ts(v("KN"), v("P0", 0, 96), p15, OP.is_le, -4.0, OP.mult)
+        ts(v("CD"), v("P0", 0, 96), p15, OP.is_gt, -4.0, OP.mult)
+        cp("V", ind(v("WA", 0, 1304), v("SL", 0, 6)), v("KN"))
+        cp("V", ind(v("WB", 8, 1312), v("SL", 0, 6)), v("CD"))
+        for s in range(2):
+            o, h = (128 * s, 128 * s + 128), (512 * s, 512 * s + 512)
+            init = 0.0 if s == 0 else v("P34", 511, 512)
+            scan(v("P34", *h), v("WA", *h), v("WB", 512 * s + 4, 512 * s + 516), OP.add, OP.add, init)
+            tt(v("SR", *o), v("P34", 512 * s + 3, 512 * s + 512, 4), v("QF", *o), OP.add)
+            cp("V", v("SRL", *o), v("SR", *o))
+            cp("AV"[s], v(Xn, 2048 * s, 2048 * s + 2048), ind(v("Y0"), v("SRL", *o)))
+        cp("V", v("FP", 0, 24), v("FPF", 0, 24))
+        cp("V", ind(v(Xn), v("FP", 0, 24)), v("FB"))
+    Xn = "XA" if RO % 2 == 0 else "XB"
+    for c in range(4):
+        x = v(Xn, 1024 * c, 1024 * c + 1024)
+        dma("SA"[c % 2], T.y[:, 1024 * c:1024 * c + 1024], ap(x), [x], [])
+    for i in plan():
+        now[0] = i
+        ops[i][5]()
+    for s in SEMAPHORES:
+        if count.get(s, 0):
+            wait("G", s, count[s])

@@ -4,14 +4,19 @@ from concourse.mybir import dt, AluOpType as OP, AxisListType, ActivationFunctio
 
 W = 4096
 RO = 2
-XW = 5184
+FREE = 1120
+XW = 5632
 F32, BF, I32, U16, F16 = "float32", "bfloat16", "int32", "uint16", "float16"
-SEGS = [(0, 192), (192, 256)]
-ON_SCALAR = ((1, 3),)
-TEN = ((0, 5), (5, 5))
-VEC = ((10, 3), (13, 3))
-WAKE = 0.06
+SEGS = [(0, 64), (64, 192), (192, 256)]
+ON_SCALAR = ((0, 0), (0, 1), (0, 2), (0, 3))
+ODD = ((0, 4), (4, 4), (8, 4), (12, 3))
+SEARCH_V = (4, 5)
+CUT = 128
+RANK = float(1 << 20)
+FAR = float(1 << 23)
+WAKE = 0.1
 CY = 0.00083
+PE = 0.0006
 
 SCRATCH = {}
 PLACE = {}
@@ -30,47 +35,47 @@ def _pack(cols, dtype, host, *names):
 
 
 _buf("sbuf", XW, BF, "XA", "XB")
-_buf("sbuf", W, BF, "Y0", "XR00", "XR01", "XR02", "XR10", "XR11", "XR12")
+_buf("sbuf", W, BF, "Y0", "XC")
+_buf("sbuf", W + 16, BF, "XR00", "XR01", "XR02", "XR10", "XR11", "XR12")
 _buf("sbuf", W, F32, "NX1", "NX2")
-_buf("sbuf", 1024, BF, "DD0", "DD1", "DD2", "DD3", "GA0", "GA1", "AB0", "AB1")
-_pack(256, I32, "hI", "CC3", "QI", "DI", "KI", "NXI", "UI", "HI")
-_pack(256, U16, "hU", "CL3", "NXL", "SRL")
-_pack(256, F32, "hF", "CN0", "CN1", "CN2", "CN3", "QF", "DEF", "K2", "SB", "FF", "CU", "WD", "SR", "KEY0", "KEY1")
-_pack(768, I32, "kI", "CCX", "TM")
-_buf("sbuf", 768, U16, "CLX")
+_buf("sbuf", 1024, BF, "DD0", "DD1", "DD2", "DD3", "GA0", "GA1", "AB0", "AB1", "ZS")
+_buf("sbuf", 1024, I32, "KK", "CC")
+_buf("sbuf", 1024, U16, "CL")
+_pack(256, I32, "hI", "QI", "UI", "UU", "HI", "KI", "NXI")
+_pack(256, U16, "hU", "NXL", "SRL")
+_pack(256, F32, "hF", "DEF", "RUN")
 _buf("sbuf", 256, F16, "NXH")
-_pack(128, I32, "gI", "J15", "JG", "J7")
-_pack(128, F32, "gF", "MASK", "KEEP", "KP8", "R0", "R1", "Z0", "Z1", "Z2", "Z3", "TT0", "TT1")
+_buf("sbuf", 256, BF, "K16")
+_pack(192, I32, "gI", "JI", "J15", "JG")
+_pack(192, F32, "gF", "MASK", "NLIN", "VM", "ZV")
+_pack(192, BF, "gB", "KEEP", "CMP")
 _pack(128, U16, "gU", "LE", "LO")
-_buf("sbuf", 640, F32, "RO0", "RO1")
-_buf("sbuf", 384, F32, "ROV0", "ROV1", "ZOV0", "ZOV1", "MASK3", "KEEP3")
-_buf("sbuf", 512, F32, "IDV", "WTS")
-_buf("sbuf", 512, I32, "JI", "PB8")
-_buf("sbuf", 4608, F32, "SW")
-_buf("sbuf", 1312, F32, "WA", "WB")
-_buf("sbuf", 144, BF, "EZ", "EW", "EX")
-_buf("sbuf", 144, F32, "EZF")
-_buf("sbuf", 128, BF, "BB", "IDN", "NID", "LT", "UT", "LT4", "BB4", "WB0", "WB1", "WB2")
-_buf("sbuf", 2048, F16, "SEL")
+_buf("sbuf", 2048, F16, "RE", "RD")
+_pack(128, F16, "zH", "Z0", "Z1", "Z2", "Z3", "RL")
+_buf("sbuf", 144, BF, "EZ", "EW", "EX", "EF", "EN", "ED", "ER", "EDR")
+_buf("sbuf", 128, BF, "BB", "IDN", "NID", "LT", "UT", "WB0", "WB1", "WB2", "BL", "ONE", "CD", "NE", "F0", "F1")
+_buf("sbuf", 2048, BF, "SEL")
+_buf("sbuf", 512, BF, "DM", "GB")
+_buf("sbuf", 128, F32, "END", "TT0", "TT1")
+_buf("sbuf", 272, F32, "GW")
+_buf("sbuf", 136, F32, "BW")
+_buf("sbuf", 136 * 6, BF, "JK")
+_buf("sbuf", 1408, BF, "WA")
+_buf("sbuf", 1424, BF, "WB")
 _buf("sbuf", 16, I32, "TH", "IC")
-_buf("sbuf", 16, F32, "FC")
-_buf("sbuf", 16, BF, "WT")
+_buf("sbuf", 32, F32, "FC")
+_buf("sbuf", 16, BF, "WT", "FDP")
 _buf("sbuf", 4, F32, "PAR", "PR0", "PR1", "PR2")
-_pack(40, BF, "sB", "EB", "CX", "CS", "FB6")
-_buf("sbuf", 32, F16, "W16")
-_pack(32, F32, "sF", "TRJ", "ZE", "OF", "TR6", "M2", "F4", "F41", "T0F", "UF", "UF2", "I6", "IT6", "LV", "KM", "FD", "FS",
-      "CBF", "P1", "XF", "Q6", "FIF", "FPF")
-_pack(32, U16, "sU", "OL", "JL", "PL", "FL", "FP", "SL")
-_pack(48, I32, "sI", "BI", "VI", "JX", "RX", "PX", "WI", "U6", "H6", "M6", "CB", "FI", "PI6", "SI6", "X6")
-_pack(48, F32, "tF", "BF8", "CM8", "IN8")
-_pack(96, F32, "uF", "KN", "CD", "RR", "VM", "ZV")
-_pack(96, I32, "uI", "TI")
-_pack(96, U16, "uU", "TL")
-_pack(96, BF, "uB", "AQ", "MK", "EXB")
+_pack(32, F32, "sF", "QF", "NW", "NWH", "TN", "M2", "FQ", "ACC", "THR", "H1", "QT", "QQ", "SS", "R4", "PQ", "FPF")
+_pack(32, U16, "sU", "JL", "FL", "FP", "SL")
+_pack(32, I32, "sI", "WI", "U6", "H6", "Q6", "R6", "K6", "S6", "T6", "C6")
+_pack(96, F32, "uF", "RS", "KM")
+_pack(96, I32, "uI", "AI", "AU", "AH", "AT", "AC", "RI", "RJ")
+_pack(96, U16, "uU", "TL", "PL")
+_pack(96, BF, "uB", "BG", "MK", "VA", "VB")
 _buf("sbuf", 1536, BF, "AR", "AD")
 _buf("sbuf", 384, BF, "FB")
-_buf("psum", 512, F32, "P0", "P7")
-_buf("psum", 1024, F32, "P12", "P34", "P56")
+_buf("psum", 1024, F32, "PA", "PB", "PC", "PD")
 
 NDMA = 20
 SEMAPHORES = ["sV", "sA", "sT", "sG", "par", "lpar"] + ["d%d" % i for i in range(NDMA)]
@@ -94,6 +99,9 @@ def rank_program(g, core, T, topo):
     def v(name, lo=0, hi=None, st=1):
         host, base, cols = PLACE[name]
         return (host, base + lo, base + (cols if hi is None else hi), st)
+
+    def pb(b, lo=0, hi=512, st=1):
+        return v(("PA", "PB", "PC", "PD")[b // 2], 512 * (b % 2) + lo, 512 * (b % 2) + hi, st)
 
     def ap(x):
         n, lo, hi, st = x
@@ -146,7 +154,9 @@ def rank_program(g, core, T, topo):
                     if not hits((lo, hi, st), a):
                         continue
                     if aq == q and q in qsem:
-                        if not (aw or wr) or (ps and q == "P"):
+                        if ps and q == "P":
+                            continue
+                        if not (aw or wr) or (ps and not hits(x[1:], a[7])):
                             continue
                     elif not (aw or wr or ps):
                         continue
@@ -160,11 +170,13 @@ def rank_program(g, core, T, topo):
             for x in lst:
                 nm, lo, hi, st = bank(x)
                 l = log.setdefault(nm, [])
-                if wr:
+                if SCRATCH[nm][0] == "psum":
+                    l[:] = [a for a in l if not (inside(a, lo, hi, st) and (a[3] != q or q == "P" or ((wr or not a[4]) and inside(a[7], *x[1:]))))]
+                elif wr:
                     l[:] = [a for a in l if not inside(a, lo, hi, st)]
                 else:
                     l[:] = [a for a in l if not (a[3] == q and not a[4] and a[0] >= lo and a[1] <= hi and a[2] == st and st == 1)]
-                l.append((lo, hi, st, q, wr, sem, n))
+                l.append((lo, hi, st, q, wr, sem, n, x[1:]))
 
     ops = []
 
@@ -190,7 +202,12 @@ def rank_program(g, core, T, topo):
                     n, lo, hi, st = bank(x)
                     psum = SCRATCH[n][0] == "psum"
                     for a in seen.get(n, ()):
-                        if hits((lo, hi, st), a) and (a[4] or w or (psum and ops[a[3]][0] != q)):
+                        if not hits((lo, hi, st), a):
+                            continue
+                        if psum and ops[a[3]][0] == q != "P":
+                            if (a[4] or w) and hits(x[1:], a[5]):
+                                ps.add(a[3])
+                        elif a[4] or w or psum:
                             ps.add(a[3])
             if q in ("G", "S"):
                 if q in last:
@@ -200,9 +217,12 @@ def rank_program(g, core, T, topo):
                 for x in lst:
                     n, lo, hi, st = bank(x)
                     l = seen.setdefault(n, [])
-                    if w:
+                    if SCRATCH[n][0] == "psum":
+                        if q == "P":
+                            l[:] = [a for a in l if not inside(a, lo, hi, st)]
+                    elif w:
                         l[:] = [a for a in l if not inside(a, lo, hi, st)]
-                    l.append((lo, hi, st, i, w))
+                    l.append((lo, hi, st, i, w, x[1:]))
             ps.discard(i)
             preds.append(ps)
         succ = [[] for _ in ops]
@@ -256,16 +276,18 @@ def rank_program(g, core, T, topo):
     def cost(q, kind, out, ins):
         n = many(out)
         if kind == "mm":
-            return 0.00071 * max(64, many(ins[1])) * (4 if SCRATCH[ins[0][0]][2] == F32 else 1)
+            return PE * max(64, many(ins[1])) * (4 if SCRATCH[ins[0][0]][2] == F32 else 1)
         if kind == "iota":
             return 0.13 + 2 * n * CY
         if out[0] == "ind":
             return 0.05 + 3.5 * n * CY
         if any(x[0] == "ind" for x in ins):
             return 0.05 + 1.5 * n * CY
+        if kind == "red":
+            n = many(ins[0])
         if kind == "tt" and not any(SCRATCH[x[0]][0] == "psum" for x in ins):
             n = 2 * n
-        if kind == "ts" and all(half(x) for x in ins + [out]):
+        if kind == "ts" and all(half(x) for x in ins + [out] if many(x) > 1):
             n = n / 2
         return max(n, 64) * CY + (0.05 if q == "A" else 0.03)
 
@@ -280,7 +302,7 @@ def rank_program(g, core, T, topo):
             note(q, rd, wr, s, count[s])
         record(q, reads, writes, cost(q, kind, writes[0], [x for x in reads if isinstance(x, tuple)]), 0.0, issue)
 
-    def dma(q, out, in_, reads, writes):
+    def dma(q, out, in_, reads, writes, lag=2.2):
         s = "d%d" % ndma[0]
         ndma[0] += 1
 
@@ -290,7 +312,7 @@ def rank_program(g, core, T, topo):
             queue[q].dma_start(out, in_).then_inc(T.sem[s], 16)
             snap[(s, 16)] = dict(known[q])
             note(q + "dma", reads, writes, s, 16)
-        record(q, reads, writes, 0.1, 3.5, issue)
+        record(q, reads, writes, 0.1, lag, issue)
 
     def tt(out, a, b, op):
         emit("V", "tt", [a, b], [out], lambda e: e.tensor_tensor(opnd(out), opnd(a), opnd(b), op))
@@ -308,17 +330,28 @@ def rank_program(g, core, T, topo):
         else:
             emit("A", "", [a], [out], lambda e: e.activation(ap(out), opnd(a), AF.Copy))
 
-    def act(out, a, func, bias=0.0, scale=1.0):
-        emit("A", "", [a, bias, scale], [out], lambda e: e.activation(ap(out), opnd(a), func, bias=arg(bias), scale=arg(scale)))
+    def act(out, a, func, bias=0.0, scale=1.0, total=None):
+        if total is None:
+            emit("A", "", [a, bias, scale], [out], lambda e: e.activation(ap(out), opnd(a), func, bias=arg(bias), scale=arg(scale)))
+        else:
+            emit("A", "", [a, bias, scale], [out, total],
+                 lambda e: e.activation(ap(out), opnd(a), func, bias=arg(bias), scale=arg(scale), accum_out=ap(total)))
+
+    def times(out, a, s):
+        act(out, a, AF.Copy, scale=s)
 
     def fill(out, c):
         emit("V", "ts", [], [out], lambda e: e.memset(ap(out), c))
 
     def scan(out, a, b, op0, op1, init=0.0):
-        emit("V", "", [a, b, init], [out], lambda e: e.tensor_tensor_scan(ap(out), ap(a), ap(b), arg(init), op0, op1))
+        emit("V", "ts", [a, b, init], [out], lambda e: e.tensor_tensor_scan(ap(out), ap(a), ap(b), arg(init), op0, op1))
 
     def mm(out, l, r, start=True, stop=True):
         emit("P", "mm", [l, r], [out], lambda e: e.matmul(ap(out), ap(l), ap(r), start, stop))
+
+    def group(calls):
+        for i, (out, l, r) in enumerate(calls):
+            mm(out, l, r, i == 0, i == len(calls) - 1)
 
     def iota(out, pattern, base, cm):
         if SCRATCH[out[0]][2] == I32:
@@ -334,68 +367,95 @@ def rank_program(g, core, T, topo):
 
     AND, SHR = OP.bitwise_and, OP.logical_shift_right
     wtq = v("WT", 0, 1)
-    dma("S", ap(wtq), T.wt[:], [], [wtq])
-    dma("A", ap(v("TH", 0, 2)), T.th[:], [], [v("TH", 0, 2)])
-    for n in ("XA", "Y0"):
+    for k, n in enumerate(("XA", "XC")):
         for c in range(4):
             x = v(n, 1024 * c, 1024 * c + 1024)
-            dma("SA"[c % 2], ap(x), T.x0[:, 1024 * c:1024 * c + 1024], [], [x])
+            dma("S", ap(x), T.x0[:, 1024 * c:1024 * c + 1024], [], [x], 2.8 + 0.7 * (4 * k + c))
+    dma("A", ap(wtq), T.wt[:], [], [wtq])
+    dma("A", ap(v("TH", 0, 2)), T.th[:], [], [v("TH", 0, 2)])
     iota(v("IC", 0, 1), [[1, 1]], 0, 1)
-    iota(v("JI"), [[1, 512]], 0, 0)
+    iota(v("JI"), [[1, 192]], 0, 0)
     iota(v("QI"), [[16, 256]], 0, 1)
-    iota(v("PB8"), [[64, 8], [1, 4], [4, 16]], 0, 0)
-    ts(v("IC", 1, 2), v("IC", 0, 1), 15, AND)
-    ts(v("IC", 2, 3), v("IC", 0, 1), 112, AND)
-    fill(v("EZ"), 0.0)
-    fill(v("PAR", 2, 4), 0.0)
-    cp("V", v("FC", 0, 3), v("IC", 0, 3))
-    pf, p15, pg, t1 = v("FC", 0, 1), v("FC", 1, 2), v("FC", 2, 3), v("FC", 3, 4)
+    iota(v("ONE"), [[0, 128]], 1, 0)
+    iota(v("FDP"), [[0, 16]], 0, 0)
+    iota(v("K16"), [[16, 256]], 0, 0)
+    iota(v("M2", 0, 16), [[2, 16]], 0, 0)
+    iota(v("FQ", 4, 8), [[1, 4]], 0, 0)
+    iota(v("NW", 8, 14), [[32, 3], [8, 2]], 0, 0)
+    iota(v("TN", 8, 14), [[32, 6]], FREE, 2)
+    iota(v("TT0"), [[32, 128]], -2048, 0)
+    iota(v("TT1"), [[2, 128]], 0, 0)
+    for h in range(2):
+        iota(v("NLIN", 96 * h, 96 * h + 96), [[32, 3], [1, 16], [16, 2]], 0, 0)
+        iota(v("GW", 136 * h + 128, 136 * h + 136), [[0, 8]], 1 << 20, 0)
+    for c in SEARCH_V:
+        iota(v("JK", 136 * c + 128, 136 * c + 136), [[0, 8]], -128, 0)
+
+    def ic(k):
+        return v("IC", k, k + 1)
+
+    def fc(k):
+        return v("FC", k, k + 1)
+
     J = v("JI", 0, 128)
+    for k, (s, m) in enumerate(((0, 15), (0, 112), (0, 3), (2, 3), (1, 7), (0, 1))):
+        ts(ic(1 + k), ic(0), s, SHR, m, AND)
+    cp("V", v("FC", 0, 7), v("IC", 0, 7))
+    pf, p15, pg, p3, pq, ph, p1 = [fc(k) for k in range(7)]
+    first, second, keep, odd, hi_, lo_, pg2 = [fc(k) for k in range(8, 15)]
+    fill(v("EZ"), 0.0)
+    fill(v("ED"), 0.0)
+    fill(v("PAR", 2, 4), 0.0)
     cp("V", v("PAR", 0, 1), wtq)
-    ts(v("PAR", 1, 2), v("TH", 1, 2), 16.0, OP.mult)
-    cp("V", t1, v("TH", 0, 1))
     ts(v("EZ", 15, 143), J, pg, OP.is_equal)
+    times(v("EW"), v("EZ"), v("PAR", 0, 1))
+    ts(v("PAR", 1, 2), v("TH", 1, 2), 256.0, OP.mult)
     ts(v("IDN"), J, pf, OP.is_equal)
-    ts(v("EW"), v("EZ"), wtq, OP.mult)
-    ts(v("NID"), J, pf, OP.is_equal, -1.0, OP.mult)
-    ts(v("QF"), v("QI"), pg, OP.subtract)
-    ts(v("J15"), J, 15, AND)
-    ts(v("JG"), J, 112, AND)
-    ts(v("J7"), J, 7, AND)
+    times(v("NID"), v("IDN"), -1.0)
+    times(v("EF"), v("EZ"), FAR)
+    ts(v("J15"), v("JI"), 15, AND)
+    ts(v("JG", 0, 128), J, 112, AND)
     ts(v("MASK"), v("J15"), p15, OP.is_equal)
-    ts(v("BB"), v("JG"), pg, OP.is_equal)
+    ts(v("BB"), v("JG", 0, 128), pg, OP.is_equal)
     ts(v("KEEP"), v("J15"), 0.0, OP.not_equal)
-    ts(v("KP8"), v("J7"), 0.0, OP.not_equal)
+    ts(first, p15, 0.0, OP.is_equal)
+    ts(second, p15, 1.0, OP.is_equal)
+    ts(keep, p15, 15.0, OP.not_equal)
+    ts(odd, p15, 2.0, OP.mult, 1.0, OP.add)
+    ts(ic(8), v("TH", 0, 1), 8128, AND)
+    ts(ic(9), v("TH", 0, 1), 63, AND)
+    ts(hi_, ic(8), first, OP.mult)
+    ts(lo_, ic(9), -1.0, OP.add, second, OP.mult)
+    ts(hi_, hi_, lo_, OP.add, -FAR, OP.mult)
+    times(v("BL"), v("BB"), hi_)
     for a in range(16):
-        ts(sel(a), v("BB"), v("MASK", a, a + 1), OP.mult)
-    ts(v("DEF"), v("QF"), 32769.0, OP.add)
-    for k in range(3):
-        cp("A", v("MASK3", 128 * k, 128 * k + 128), v("MASK"))
-        cp("A", v("KEEP3", 128 * k, 128 * k + 128), v("KEEP"))
-    ts(v("K2", 0, 128), v("J7"), 0.0, OP.is_gt, 2.0, OP.mult)
-    ts(v("K2", 128, 256), v("J7"), 0.0, OP.is_gt, 2.0, OP.mult)
-    ts(v("BB4"), v("JG"), pg, OP.is_equal, 4.0, OP.mult)
-    ts(v("TT0"), J, pf, OP.is_gt)
-    ts(v("TT1"), J, pf, OP.is_lt)
-    tt(v("LT"), v("TT0"), v("BB"), OP.mult)
-    tt(v("UT"), v("TT1"), v("BB"), OP.mult)
-    ts(v("LT4"), v("LT"), 4.0, OP.mult)
-    ts(v("EX"), v("EZ"), 16.0, OP.mult)
-    ts(v("EZF"), v("EZ"), 0.0625, OP.mult)
+        times(sel(a), v("BB"), v("MASK", a, a + 1))
+    ts(v("DEF"), v("QI"), pg, OP.subtract, 4 * RANK, OP.add)
+    ts(v("QF", 0, 8), v("QI", 0, 8), pg, OP.subtract)
     ts(v("LE", 0, 8), v("QF", 0, 8), 32.0, OP.mult)
-    ts(v("SB", 0, 256, 32), v("QF", 0, 8), 32.0, OP.mult, -2048.0, OP.add)
-    ts(v("WTS"), v("PB8"), 4096.0, OP.mult, float(1 << 21), OP.add)
-    ts(v("IDV"), v("JI"), 8.0, OP.mult)
-    tt(v("IDV"), v("IDV"), v("WTS"), OP.add)
-    ts(v("TRJ"), v("QF", 0, 32), 4096.0, OP.add)
-    ts(v("TR6", 0, 6), v("QF", 0, 6), 4.0, OP.mult, 4800.0, OP.add)
-    ts(v("M2", 0, 16), v("JI", 0, 16), 2.0, OP.mult)
-    cp("V", v("F4", 0, 4), v("JI", 0, 4))
-    ts(v("F41", 0, 4), v("JI", 0, 4), 1.0, OP.add)
-    ts(v("TI"), v("JI", 0, 96), 1, SHR, 15, AND)
-    cp("V", v("MK"), v("TI"))
-    fill(v("EB", 0, 4), 0.0)
-    fill(v("CS", 0, 1), 0.0)
+    tt(v("RE", 0, 128), v("TT0"), v("MASK", 0, 128), OP.mult)
+    times(v("EN"), v("EZ"), -1.0)
+    times(v("ER"), v("EZ"), 0.0625)
+    times(v("EX"), v("EZ"), 256.0)
+    tt(v("ED", 0, 143), v("EZ", 1, 144), v("EZ", 0, 143), OP.subtract)
+    times(v("EDR"), v("ED"), 0.0625)
+    ts(v("CD"), v("ONE"), 256.0, OP.mult, first, OP.subtract)
+    ts(v("BW", 0, 128), v("TT1"), first, OP.add)
+    cp("A", v("BW", 128, 136), v("CD", 0, 8))
+    ts(v("LT"), J, pf, OP.is_gt)
+    ts(v("UT"), J, pf, OP.is_lt)
+    tt(v("LT"), v("LT"), v("BB"), OP.mult)
+    tt(v("UT"), v("UT"), v("BB"), OP.mult)
+    for q in range(4):
+        ts(fc(16 + q), pq, float(q), OP.is_equal, -4.0, OP.mult)
+        times(v("DM", 128 * q, 128 * q + 128), v("IDN"), fc(16 + q))
+    ts(ph, p1, 16.0, OP.mult, ph, OP.add)
+    ts(v("NW", 0, 6), v("NW", 8, 14), ph, OP.add)
+    ts(v("NWH", 0, 6), v("NW", 8, 14), ph, OP.add, 0.5, OP.add)
+    ts(pg2, pg, 2.0, OP.mult)
+    ts(v("TN", 0, 6), v("TN", 8, 14), pg2, OP.subtract)
+    times(v("FQ", 0, 4), v("FQ", 4, 8), 0.25)
+    ts(v("RS"), v("J15", 0, 96), 0.0, OP.is_equal, 4 * RANK, OP.mult)
 
     mine = topo.chip(core)
     mate = [c for c in cores if topo.mates(topo.chip(c), mine) and topo.die(c) == topo.die(core)][0]
@@ -444,7 +504,7 @@ def rank_program(g, core, T, topo):
         for h, lo, hi in halves():
             src = v(x, lo, hi)
             remote([(mate, ap(src), T["XR%d%d" % (rd, slot(mate, core))][:, lo:hi], off, "am%d%d" % (rd, h)),
-                    (near, ap(src), T["XR%d%d" % (rd, slot(near, core))][:, lo:hi], on, "ap%d%d" % (rd, h))], "lx%d%d" % (rd, h), [src])
+                    (near, ap(src), T["XR%d%d" % (rd, slot(near, core))][:, lo:hi], on, "ap%d%d" % (rd, h))], "lx%d%d" % (rd, h), [src, v("XC")])
         for h, lo, hi in halves():
             src = v(x, lo, hi)
             a, b, c = ("XR%d%d" % (rd, slot(core, o)) for o in (mate, near, diag))
@@ -459,126 +519,100 @@ def rank_program(g, core, T, topo):
 
     for rd in range(RO):
         X, Xn = ("XA", "XB") if rd % 2 == 0 else ("XB", "XA")
+        XR = ["XR%d%d" % (rd, d) for d in range(3)]
         if rd > 0:
             for c in range(4):
-                x, y = v(X, 1024 * c, 1024 * c + 1024), v("Y0", 1024 * c, 1024 * c + 1024)
-                dma("S", ap(y), ap(x), [x], [y])
+                x, y = v(X, 1024 * c, 1024 * c + 1024), v("XC", 1024 * c, 1024 * c + 1024)
+                dma("S", ap(y), ap(x), [x], [y], 2.8 + 0.7 * c)
         broadcast(rd, X)
         if rd == 0:
             send_params()
-        iota(v("SW", 0, 96), [[0, 96]], 0, 0)
         iota(v("WA", 0, 1024), [[0, 1024]], 0, 0)
-        iota(v("WB", 4, 1032), [[0, 1028]], 0, 0)
+        iota(v("WB", 0, 1040), [[0, 1040]], 0, 0)
         hand_on(rd)
-        hb = ["P0", "P7"]
-        for s, (lo, hi) in enumerate(SEGS):
-            for a in range(16):
-                mm(v(hb[s], 0, hi - lo), ez("EW", a), v(X, 16 * lo + a, 16 * hi, 16), a == 0, a == 15)
 
-        def cl(m, lo, hi):
-            if m == 3:
-                return v("CL3", lo, hi)
-            s0, s1 = SEGS[0] if hi <= SEGS[0][1] else SEGS[1]
-            o = 3 * s0 + m * (s1 - s0) - s0
-            return v("CLX", o + lo, o + hi)
+        def seg(q):
+            return [s for s, (lo, hi) in enumerate(SEGS) if lo <= 64 * q < hi][0]
+
+        def part(n, s, m0, m1, lo=None, hi=None):
+            a, b = SEGS[s]
+            if lo is None:
+                return v(n, 4 * a + m0 * (b - a), 4 * a + m1 * (b - a))
+            return v(n, 4 * a + m0 * (b - a) + lo - a, 4 * a + m0 * (b - a) + hi - a)
 
         def looks(s):
             lo, hi = SEGS[s]
-            w = hi - lo
-            u, hm, u2 = v("UI", 0, w), v(hb[s], w, 2 * w), v(hb[s], 0, w)
-            t = [v("TM", m * w, m * w + w) for m in range(3)]
-            cp("V", u, v(hb[s], 0, w))
-            ts(u, u, W - 1, AND)
-            ts(v("HI", 0, w), u, 5, SHR)
-            ts(hm, v("HI", 0, w), 7.0, OP.add)
-            tt(t[0], hm, u, OP.mult)
-            ts(v("CC3", lo, hi), t[0], W - 1, AND)
-            cp("V", v("CL3", lo, hi), v("CC3", lo, hi))
-            ts(hm, v("HI", 0, w), 1.0, OP.add)
-            tt(t[0], hm, u, OP.mult)
-            ts(u2, u, 2.0, OP.mult)
-            tt(t[1], u2, t[0], OP.add)
-            tt(t[2], u2, t[1], OP.add)
-            c = (3 * lo, 3 * hi)
-            ts(v("CCX", *c), v("TM", 0, 3 * w), W - 1, AND)
-            cp("V", v("CLX", *c), v("CCX", *c))
+            w, b = hi - lo, s % 2
+            group([(pb(b, 0, w), ez("EW", a), v(X, 16 * lo + a, 16 * hi, 16)) for a in range(16)])
+            u, h, h1, u2 = v("UU", lo, hi), v("HI", lo, hi), pb(b, w, 2 * w), pb(b, 2 * w, 3 * w)
+            cp("V", v("UI", lo, hi), pb(b, 0, w))
+            ts(h, v("UI", lo, hi), 5, SHR, 127, AND)
+            ts(u, v("UI", lo, hi), W - 1, AND)
+            ts(h1, h, 1.0, OP.add)
+            ts(u2, u, 2.0, OP.mult, RANK, OP.add)
+            tt(part("KK", s, 0, 1), h1, u, OP.mult)
+            for m in range(1, 4):
+                tt(part("KK", s, m, m + 1), u2, part("KK", s, m - 1, m), OP.add)
+            for m0, m1 in ((0, 1), (1, 4)) if s == 0 else ((0, 4),):
+                ts(part("CC", s, m0, m1), part("KK", s, m0, m1), W - 1, AND)
+                cp("V", part("CL", s, m0, m1), part("CC", s, m0, m1))
 
-        def keys(s):
-            lo, hi = SEGS[s]
-            w = hi - lo
-            for m in range(3):
-                ts(v("CN%d" % m, lo, hi), v("CCX", 3 * lo + m * w, 3 * lo + m * w + w), float(1 + 8192 * m), OP.add)
-            ts(v("CN3", lo, hi), v("CC3", lo, hi), float(1 + 8192 * 3), OP.add)
+        dn, an = [0], [0]
+        LAST = 3
 
-        dn, an, kn = [0], [0], [0]
-
-        def dist(m, s):
-            lo, hi = SEGS[s]
-            w = hi - lo
-            if s == 0:
-                o = 512 * (m // 2) + w * (m % 2)
-                return v("P12", o, o + w)
-            return v("P34", 0, w) if m == 2 else v("P0", 64 * (m % 3) + 128 * (m // 3), 64 * (m % 3) + 128 * (m // 3) + w)
-
-        def reduce_abs(m, q, buf):
-            s = 0 if 64 * q + 64 <= SEGS[0][1] else 1
-            n, o, _, _ = dist(m, s)
-            o += 64 * q - SEGS[s][0]
-            for a in range(16):
-                mm((n, o, o + 64, 1), ez("EZ", a), v(buf, a, 1024, 16), a == 0, a == 15)
+        def dist(s, m0, m1):
+            w = SEGS[s][1] - SEGS[s][0]
+            if s == len(SEGS) - 1 and m0 == LAST:
+                return pb(1, 0, w)
+            return pb(2 + s % 2, w * m0, w * m1)
 
         def unit(m, q):
-            win, x = ind(v(X, 0, W), cl(m, 64 * q, 64 * q + 64)), (1024 * q, 1024 * q + 1024)
-            if m == 3 or (m, q) in ON_SCALAR:
+            s = seg(q)
+            win, x = ind(v(X, 0, W), part("CL", s, m, m + 1, 64 * q, 64 * q + 64)), (1024 * q, 1024 * q + 1024)
+            n, o, _, _ = dist(s, m, m + 1)
+            o += 64 * q - SEGS[s][0]
+            if (m, q) in ON_SCALAR:
                 b, c = "GA%d" % (an[0] % 2), "AB%d" % (an[0] % 2)
                 an[0] += 1
                 for k in range(2):
-                    mm(v("P34", 512 * k, 512 * k + 512), v("NID"), v(X, x[0] + 512 * k, x[0] + 512 * k + 512), True, False)
+                    mm(pb(4 + k), v("NID"), v(X, x[0] + 512 * k, x[0] + 512 * k + 512), True, False)
                 cp("A", v(b), win)
                 for k in range(2):
-                    mm(v("P34", 512 * k, 512 * k + 512), v("IDN"), v(b, 512 * k, 512 * k + 512), False, True)
-                act(v(c), v("P34"), AF.Abs)
+                    mm(pb(4 + k), v("IDN"), v(b, 512 * k, 512 * k + 512), False, True)
+                act(v(c), v("PC"), AF.Abs)
             else:
                 c = "DD%d" % (dn[0] % 4)
                 dn[0] += 1
-                tt(v(c), win, v("Y0", *x), OP.subtract)
+                tt(v(c), win, v("XC", *x), OP.subtract)
                 act(v(c), v(c), AF.Abs)
-            reduce_abs(m, q, c)
+            out = (n, o, o + 64, 1)
+            group([(out, v("BL"), v("ONE", 0, 64))] + [(out, ez("EF", a), v(c, a, 1024, 16)) for a in range(16)])
 
-        def nearest(s, ms):
+        def nearest(s):
             lo, hi = SEGS[s]
-            w = hi - lo
             o = (lo, hi)
-            pen, run = v("P56", 0, w), v("P56", 512, 512 + w)
-            for m in ms:
-                key = v("KEY%d" % (kn[0] % 2), 0, w)
-                kn[0] += 1
-                ts(pen, dist(m, s), t1, OP.is_ge, 65536.0, OP.mult)
-                tt(key, pen, v("CN%d" % m, *o), OP.add)
-                tt(v("KI", *o) if m == ms[-1] else run, v("DEF", *o) if m == ms[0] else run, key, OP.min)
+            for m0, m1 in ((0, LAST), (LAST, 4)) if s == len(SEGS) - 1 else ((0, 4),):
+                tt(dist(s, m0, m1), dist(s, m0, m1), part("KK", s, m0, m1), OP.max)
+            for m in range(4):
+                tt(v("RUN", *o), dist(s, m, m + 1), v("DEF" if m == 0 else "RUN", *o), OP.min)
+            ts(v("KI", *o), v("RUN", *o), 1.0, OP.add)
             ts(v("NXI", *o), v("KI", *o), W - 1, AND)
             ts(v("NXH", *o), v("NXI", *o), -2048.0, OP.add)
             cp("V", v("NXL", *o), v("NXI", *o))
-            banks = [("P56", 0), ("P56", 512), ("P7", 0)]
-            per = 512 // w
-            for i in range(0, 16, per):
-                bn, b0 = banks[i // per % 3]
-                for j in range(per):
-                    mm(v(bn, b0 + w * j, b0 + w * j + w), sel(i + j), v("NXH", *o))
-                for j in range(per):
-                    cp("VA"[i // per % 2], v("NX1", 16 * lo + i + j, 16 * hi, 16), v(bn, b0 + w * j, b0 + w * j + w))
+            for q in range(lo // 64, hi // 64):
+                banks = (0, 3) if q == 2 else (6, 7)
+                for a in range(16):
+                    mm(pb(banks[a % 2], a // 2, 512, 8), sel(a), v("NXH", 64 * q, 64 * q + 64))
+                for b in range(2):
+                    cp("VA"[b] if q == 3 else "A", v("NX1", 1024 * q + b, 1024 * q + 1024, 2), pb(banks[b]))
 
-        for s in range(2):
+        for s in range(len(SEGS)):
             looks(s)
-            keys(s)
-        for q in range(3):
-            for m in (3, 0, 1, 2):
-                unit(m, q)
-        for m in (3, 0, 1):
-            unit(m, 3)
-        nearest(0, (0, 1, 3, 2))
-        unit(2, 3)
-        nearest(1, (3, 0, 1, 2))
+        for s, (lo, hi) in enumerate(SEGS):
+            for q in range(lo // 64, hi // 64):
+                for m in range(4):
+                    unit(m, q)
+            nearest(s)
         cp("V", v("NX2", 0, 2048), ind(v("NX1"), v("NXL", 0, 128)))
         cp("A", v("NX2", 2048, 4096), ind(v("NX1"), v("NXL", 128, 256)))
 
@@ -586,180 +620,162 @@ def rank_program(g, core, T, topo):
             l = v("LE" if k % 2 == 0 else "LO", 8 * (k // 2), 8 * (k // 2) + 8)
             cp("A", v("Y0", k, W, 32), ind(v(X, 0, W), l))
 
-        def sb_of(k):
-            return v("SB", k, 256, 32)
+        steps = [[], []]
 
-        def odd_by_tensor(j, n, pb, ro):
-            cp("A", v(ro, 0, 128 * n), ind(v("NX1"), v("LE", 8 * j, 8 * j + 8 * n)))
-            for a in range(16):
-                mm(v(pb, 0, 8 * n), ez("EZF", a), v(ro, a, 128 * n, 16), a == 0, a == 15)
-            ts(v("LO", 8 * j, 8 * j + 8 * n), v(pb, 0, 8 * n), 2048.0, OP.add)
-            for k in range(n):
-                cp("A", sb_of(2 * (j + k) + 1), v(pb, 8 * k, 8 * k + 8))
+        def step(k, r, mat):
+            h, a = k // 16, k % 16
+            if a:
+                mm(pb(h, 0, 128), ez(mat, a), r, False, k == steps[h])
+            else:
+                mm(pb(h, 0, 128), ez("EN", 0), r, False, False)
+                if h:
+                    mm(pb(0, 0, 128), ez("EZ", 15), r, False, k == steps[0])
 
-        def odd_by_vector(j, n, ro, zo):
-            w = 128 * n
-            tt(v(ro, 0, w), ind(v("NX1"), v("LE", 8 * j, 8 * j + 8 * n)), v("MASK3", 0, w), OP.mult)
-            scan(v(zo, 0, w), v("KEEP3", 0, w), v(ro, 0, w), OP.mult, OP.add)
-            ts(v("LO", 8 * j, 8 * j + 8 * n), v(zo, 15, w, 16), 2048.0, OP.add)
-            for k in range(n):
-                cp("V", sb_of(2 * (j + k) + 1), v(zo, 128 * k + 15, 128 * k + 128, 16))
+        def flags(h):
+            d = pb(h, 0, 128)
+            if h:
+                ts(v("NE"), d, 4096.0, OP.not_equal, keep, OP.mult)
+            else:
+                ts(v("NE"), d, 4096.0, OP.not_equal)
+            tt(v("F%d" % h), d, v("NE"), OP.min)
 
+        steps[0], steps[1] = 16, 31
+        for h in range(2):
+            mm(pb(h, 0, 128), v("BB"), v("CD"), True, False)
+        step(0, v("RE", 0, 128), "ED")
         for i in range(16):
             le = v("LE", 8 * i, 8 * i + 8)
             if i < 15:
-                r, z = v("R%d" % (i % 2)), "Z%d" % (i % 4)
-                tt(r, ind(v("NX2"), le), v("MASK"), OP.mult)
-                scan(v(z), v("KEEP"), r, OP.mult, OP.add)
+                r, z = v("RE", 128 * i + 128, 128 * i + 256), "Z%d" % (i % 4)
+                tt(r, ind(v("NX2"), le), v("MASK", 0, 128), OP.mult)
+                scan(v(z), v("KEEP", 0, 128), r, OP.mult, OP.add)
                 ts(v("LE", 8 * i + 8, 8 * i + 16), v(z, 15, 128, 16), 2048.0, OP.add)
-                cp("A", sb_of(2 * i + 2), v(z, 15, 128, 16))
+            else:
+                tt(v("RL"), ind(v("NX1"), le), v("MASK", 0, 128), OP.mult)
+                step(31, v("RL"), "ED")
+                scan(v("Z3"), v("KEEP", 0, 128), v("RL"), OP.mult, OP.add)
+                ts(v("LO", 120, 128), v("Z3", 15, 128, 16), 2048.0, OP.add)
+                y0(31)
             y0(2 * i)
+            for e, (j, n) in enumerate(ODD):
+                if i == j + n - 1:
+                    cp("A", v("RD", 128 * j, 128 * (j + n)), ind(v("NX1"), v("LE", 8 * j, 8 * j + 8 * n)))
+                    for k in range(j, j + n):
+                        step(2 * k + 1, v("RD", 128 * k, 128 * k + 128), "EDR")
+                    o = pb(2 + e % 2, 0, 8 * n)
+                    group([(o, ez("ER", a), v("RD", 128 * j + a, 128 * (j + n), 16)) for a in range(16)])
+                    ts(v("LO", 8 * j, 8 * j + 8 * n), o, 2048.0, OP.add)
+                    for k in range(j, j + n):
+                        y0(2 * k + 1)
+            if i < 15:
+                step(2 * i + 2, r, "ED")
+            if i == 7:
+                flags(0)
+                mm(pb(4, 0, 128), v("BB"), v("F0"), True, False)
+                mm(pb(5, 0, 128), v("UT"), v("F0"), True, False)
+        flags(1)
+        mm(pb(4, 0, 128), v("BB"), v("F1"), False, True)
+        mm(pb(5, 0, 128), v("BB"), v("F1"), False, True)
+        mm(pb(5, 128, 256), v("UT"), v("F1"))
+        scan(v("END"), v("ONE"), pb(4, 0, 128), OP.mult, OP.add)
+        for c in range(6):
+            if c in SEARCH_V:
+                ts(v("JK", 136 * c, 136 * c + 128), v("END"), v("NW", c, c + 1), OP.is_le, 2.0, OP.mult)
+                o, i_ = v("ACC", c, c + 1), v("JK", 136 * c, 136 * c + 129)
+                emit("V", "red", [i_], [o], lambda e, o=o, i_=i_: e.tensor_reduce(ap(o), ap(i_), AxisListType.X, OP.add))
+            else:
+                act(v("JK", 136 * c, 136 * c + 128), v("END"), AF.Sign, bias=v("NWH", c, c + 1), scale=-1.0, total=v("ACC", c, c + 1))
+        for h in range(2):
+            tt(v("GW", 136 * h, 136 * h + 128), v("END"), pb(5, 128 * h, 128 * h + 128), OP.subtract)
+        for h in range(2):
+            ts(v("JL", 6 * h, 6 * h + 6), v("ACC", 0, 6), 0.5, OP.mult, 64.0 + 136 * h, OP.add)
+        tt(v("CMP"), ind(v("GW"), v("JL", 0, 12)), v("NLIN"), OP.is_le)
+        cp("A", v("BG"), ind(v("BW"), v("JL", 0, 6)))
+        parts = (v("BG"), v("CMP", 0, 96), v("CMP", 96, 192))
+        group([(pb(6, 0, 96), v("BB"), x) for x in parts])
+        ts(v("PL"), pb(6, 0, 96), -1.0, OP.add)
+        for d in range(3):
             for e in range(2):
-                for lst, fn in ((TEN, odd_by_tensor), (VEC, odd_by_vector)):
-                    j, n = lst[e]
-                    if i == j + n - 1:
-                        if fn is odd_by_tensor:
-                            fn(j, n, ("P0", "P7")[e], "RO%d" % e)
-                        else:
-                            fn(j, n, "ROV%d" % e, "ZOV%d" % e)
-                        for k in range(j, j + n):
-                            y0(2 * k + 1)
-        tt(v("DI", 0, 255), v("SB", 1, 256), v("SB", 0, 255), OP.subtract)
-        ts(v("DI", 0, 255), v("DI", 0, 255), W - 1, AND)
-        ts(v("FF", 0, 255), v("DI", 0, 255), 1.0, OP.not_equal)
-        fill(v("FF", 31, 256, 32), 0.0)
-        scan(v("CU"), v("FF"), v("FF"), OP.add, OP.max)
-        scan(v("WD"), v("K2"), v("FF"), OP.mult, OP.add)
-        for k in range(4):
-            cp("V", v("EB", 4 + k, 36, 4), v("CU", 31, 256, 32))
-        tt(v("CX", 0, 32), v("CU", 0, 256, 8), v("FF", 0, 256, 8), OP.subtract)
-        first = v("P12", 0, 32)
-        mm(first, v("LT"), v("EB", 4, 36), True, False)
-        mm(first, v("UT"), v("EB", 0, 32), False, False)
-        mm(first, v("IDN"), v("CX", 0, 32), False, True)
-        cp("V", v("W16"), v("WD", 7, 256, 8))
-        for a in range(16):
-            mm(v("P12", 512 + a, 1024, 16), sel(a), v("W16"))
-        cp("A", v("WTS"), v("P12", 512, 1024))
-        mm(v("P0", 0, 1), v("BB"), v("EB", 35, 36))
-        ts(v("ZE"), v("WD", 7, 256, 8), 0.0, OP.is_equal)
-        tt(v("ZE"), v("ZE"), v("TRJ"), OP.mult)
-        tt(v("OF"), first, v("ZE"), OP.max)
-        cp("V", v("OL"), v("OF"))
-        cp("V", ind(v("SW"), v("OL")), v("IDV"))
-        ts(v("KN"), v("SW", 0, 96), 0.0, OP.is_equal)
-        scan(v("CD"), v("KN"), v("SW", 0, 96), OP.mult, OP.add)
-        scan(v("RR"), v("KN"), v("KN"), OP.mult, OP.add)
-        tt(v("VM"), v("CD"), v("RR"), OP.add)
-        tt(v("VM"), v("VM"), v("MASK", 0, 96), OP.mult)
-        scan(v("ZV"), v("KEEP", 0, 96), v("VM"), OP.mult, OP.add)
-        cp("V", v("VI", 0, 6), v("ZV", 15, 96, 16))
-        ts(v("JX", 0, 6), v("VI", 0, 6), 3, SHR, 511, AND)
-        ts(v("RX", 0, 6), v("VI", 0, 6), 7, AND)
-        cp("V", v("JL", 0, 6), v("JX", 0, 6))
-        ts(v("PX", 0, 6), v("VI", 0, 6), 12, SHR, 511, AND)
-        tt(v("VM"), ind(v("WTS"), v("JL", 0, 6)), v("MASK", 0, 96), OP.mult)
-        ts(v("Q6", 0, 6), v("PX", 0, 6), 8.0, OP.mult)
-        scan(v("ZV"), v("KEEP", 0, 96), v("VM"), OP.mult, OP.add)
-        ts(v("LV", 0, 6), v("QF", 0, 6), v("P0", 0, 1), OP.is_lt)
-        cp("V", v("WI", 0, 6), v("ZV", 15, 96, 16))
-        for k in range(8):
-            ts(v("BI", k, 48, 8), v("WI", 0, 6), 7 - k, SHR, 1, AND)
-        cp("V", v("BF8"), v("BI"))
-        tt(v("BF8", 0, 48, 8), v("BI", 0, 48, 8), v("RX", 0, 6), OP.subtract)
-        scan(v("CM8"), v("KP8", 0, 48), v("BF8"), OP.mult, OP.add)
-        ts(v("IN8"), v("CM8"), 0.0, OP.is_le)
-        scan(v("CM8"), v("KP8", 0, 48), v("IN8"), OP.mult, OP.add)
-        tt(v("I6", 0, 6), v("Q6", 0, 6), v("CM8", 7, 48, 8), OP.add)
-        ts(v("PL", 0, 6), v("I6", 0, 6), 4095.0, OP.min)
-        cp("V", v("AQ"), ind(v("Y0"), v("PL", 0, 6)))
+                group([(pb(7, 32 * d + 16 * e, 32 * d + 16 * e + 16), v("BB"), (x[0], x[1] + 32 * d + e, x[1] + 32 * d + 32, 2)) for x in parts])
+        for d in range(3):
+            ts(v("THR", 2 * d, 2 * d + 2), v("QF", 2 * d, 2 * d + 2), v("END", 127, 128), OP.is_lt, v("PR%d" % d, 1, 2), OP.mult)
+        cp("V", v("AR", 0, 768), ind(v("Y0"), v("PL", 0, 48)))
+        cp("A", v("AR", 768, 1536), ind(v("Y0"), v("PL", 48, 96)))
         if rd == 0:
             for d in range(3):
-                ts(v("WB%d" % d), v("BB"), v("PR%d" % d, 0, 1), OP.mult)
+                times(v("WB%d" % d), v("BB"), v("PR%d" % d, 0, 1))
         for d in range(3):
-            mm(v("P7", 32 * d, 32 * d + 32), v("WB%d" % d), v("AQ", 32 * d, 32 * d + 32))
+            cp("A", v(XR[d], W, W + 4), v(XR[d], 0, 4))
         for d in range(3):
-            o = 512 * d
-            cp("A", v("AR", o, o + 32), v("AQ", 32 * d, 32 * d + 32))
-            for w in (32, 64, 128, 256):
-                cp("A", v("AR", o + w, o + 2 * w), v("AR", o, o + w))
-        ts(v("IT6", 0, 6), v("I6", 0, 6), 1.0, OP.add)
-        tt(v("IT6", 0, 6), v("IT6", 0, 6), v("TR6", 0, 6), OP.subtract)
-        tt(v("VM"), v("P7", 0, 96), v("MASK", 0, 96), OP.mult)
-        scan(v("ZV"), v("KEEP", 0, 96), v("VM"), OP.mult, OP.add)
-        cp("V", v("U6", 0, 6), v("ZV", 15, 96, 16))
-        ts(v("U6", 0, 6), v("U6", 0, 6), W - 1, AND)
-        ts(v("H6", 0, 6), v("U6", 0, 6), 5, SHR)
-        cp("V", v("UF", 0, 6), v("U6", 0, 6))
-        ts(v("H6", 0, 6), v("H6", 0, 6), 1.0, OP.add)
-        ts(v("UF2", 0, 6), v("U6", 0, 6), 2.0, OP.mult)
-        tt(v("T0F", 0, 6), v("U6", 0, 6), v("H6", 0, 6), OP.mult)
+            mm(pb(0, 32 * d, 32 * d + 32), v("WB%d" % d), v("AR", 512 * d, 512 * d + 512, 16))
+        for d in range(3):
+            for e in range(2):
+                mm(pb(7, 96 + 32 * d + 16 * e, 112 + 32 * d + 16 * e), v("WB%d" % d), v("AR", 512 * d + 16 * e, 512 * d + 512, 32))
+        cp("V", v("AI"), pb(0, 0, 96))
+        ts(v("AH"), v("AI"), 5, SHR, 127, AND)
+        ts(v("AU"), v("AI"), W - 1, AND)
+        ts(pb(0, 96, 192), v("AH"), odd, OP.add)
+        tt(v("AT"), pb(0, 96, 192), v("AU"), OP.mult)
+        ts(v("AC"), v("AT"), W - 1, AND)
+        cp("V", v("TL"), v("AC"))
+        cp("V", v("RI"), pb(7, 0, 96))
+        tt(v("VM"), pb(7, 0, 192), v("MASK"), OP.mult)
+        scan(v("ZV"), v("KEEP"), v("VM"), OP.mult, OP.add)
+        cp("V", v("WI", 0, 12), v("ZV", 15, 192, 16))
+        ts(v("H6", 0, 6), v("WI", 6, 12), 5, SHR, 127, AND)
+        ts(v("H1", 0, 6), v("H6", 0, 6), 1.0, OP.add)
         for c in range(6):
-            ts(v("TI", 32 * (c // 2) + c % 2, 32 * (c // 2) + 32, 2), v("M2", 0, 16), v("UF", c, c + 1), OP.mult, v("T0F", c, c + 1), OP.add)
-        ts(v("TI"), v("TI"), W - 1, AND)
-        cp("V", v("TL"), v("TI"))
-        ky = "P12"
-        mm(v(ky, 0, 96), v("IDN"), v("MK"), True, False)
-        for d in range(3):
-            o = v("AD", 512 * d, 512 * d + 512)
-            tt(o, ind(v("XR%d%d" % (rd, d)), v("TL", 32 * d, 32 * d + 32)), v("AR", 512 * d, 512 * d + 512), OP.subtract)
-            act(o, o, AF.Abs)
-        for a in range(16):
-            mm(v(ky, 0, 96), ez("EX", a), v("AD", a, 1536, 16), False, a == 15)
-        for c in range(6):
-            o, i_ = v("KM", c, c + 1), v(ky, 32 * (c // 2) + c % 2, 32 * (c // 2) + 32, 2)
-            emit("V", "", [i_], [o], lambda e, o=o, i_=i_: e.tensor_reduce(ap(o), ap(i_), AxisListType.X, OP.min))
-        for d in range(3):
-            ts(v("FD", 2 * d, 2 * d + 2), v("KM", 2 * d, 2 * d + 2), v("PR%d" % d, 1, 2), OP.is_lt)
-        cp("V", v("M6", 0, 6), v("KM", 0, 6))
-        tt(v("FD", 0, 6), v("FD", 0, 6), v("LV", 0, 6), OP.mult)
-        ts(v("M6", 0, 6), v("M6", 0, 6), 15, AND)
-        scan(v("FS", 0, 6), v("FD", 0, 6), v("FD", 0, 6), OP.add, OP.max)
-        cp("V", v("FB6", 0, 6), v("FD", 0, 6))
-        cp("V", v("CS", 1, 7), v("FS", 0, 6))
-        tt(v("CBF", 0, 6), v("M6", 0, 6), v("UF2", 0, 6), OP.mult)
-        mm(v("P7", 0, 6), v("LT4"), v("FB6", 0, 6), True, False)
-        mm(v("P7", 0, 6), v("BB4"), v("CS", 0, 6), False, True)
-        tt(v("CB", 0, 6), v("CBF", 0, 6), v("T0F", 0, 6), OP.add)
-        tt(v("P1", 0, 6), v("P7", 0, 6), v("IT6", 0, 6), OP.add)
-        ts(v("CB", 0, 6), v("CB", 0, 6), W - 1, AND)
-        tt(v("P1", 0, 6), v("P1", 0, 6), v("FD", 0, 6), OP.mult)
-        cp("V", v("CBF", 0, 6), v("CB", 0, 6))
-        tt(v("P1", 0, 6), v("P1", 0, 6), v("TR6", 0, 6), OP.add)
-        cp("V", v("PI6", 0, 6), v("P1", 0, 6))
-        ts(v("X6", 0, 6), v("PI6", 0, 6), 15, AND)
-        ts(v("SI6", 0, 6), v("PI6", 0, 6), 2, SHR)
-        cp("V", v("XF", 0, 6), v("X6", 0, 6))
-        cp("V", v("SL", 0, 6), v("SI6", 0, 6))
-        for c in range(6):
-            if c % 2:
-                act(v("EXB", 16 * c, 16 * c + 16), v("MASK", 0, 16), AF.Copy, scale=v("XF", c, c + 1))
+            act(v("MK", 16 * c, 16 * c + 16), v("M2", 0, 16), AF.Identity, bias=v("H1", c, c + 1))
+        ts(v("U6", 0, 6), v("WI", 6, 12), W - 1, AND)
+        ts(v("Q6", 0, 6), v("WI", 0, 6), 2, SHR)
+        ts(v("R6", 0, 6), v("WI", 0, 6), 3, AND)
+        tt(v("QT", 0, 6), v("Q6", 0, 6), v("TN", 0, 6), OP.subtract)
+        ts(v("R4", 0, 6), v("R6", 0, 6), 0.25, OP.mult)
+        ts(v("RJ"), v("RI"), 3, AND)
+        ts(v("VA"), v("RJ"), p3, OP.is_le)
+        ts(v("VB"), v("RJ"), p3, OP.is_gt)
+        mm(pb(1), v("NID"), v("AR", 1024, 1536), True, False)
+        for d in (0, 2, 1):
+            o, win = v("AD", 512 * d, 512 * d + 512), ind(v(XR[d], 0, W), v("TL", 32 * d, 32 * d + 32))
+            if d == 2:
+                cp("A", v("GB"), win)
+                mm(pb(1), v("IDN"), v("GB"), False, True)
+                act(o, pb(1), AF.Abs)
             else:
-                ts(v("EXB", 16 * c, 16 * c + 16), v("MASK", 0, 16), v("XF", c, c + 1), OP.mult)
-        mm(v("P0", 0, 96), v("BB"), v("EXB"))
-        for c in range(6):
-            o = 8 * (c // 2) + c % 2, 8 * (c // 2) + 8, 2
-            act(v("FIF", *o), v("F41", 0, 4), AF.Identity, bias=v("CBF", c, c + 1))
-        cp("V", v("FI", 0, 24), v("FIF", 0, 24))
-        ts(v("FI", 0, 24), v("FI", 0, 24), W - 1, AND)
-        cp("V", v("FL", 0, 24), v("FI", 0, 24))
+                tt(o, win, v("AR", 512 * d, 512 * d + 512), OP.subtract)
+                act(o, o, AF.Abs)
+            ky = pb(2 + d, 0, 32)
+            group([(ky, ez("EX", a), v("AD", 512 * d + 32 * a, 512 * d + 32 * a + 32)) for a in range(16)]
+                  + [(ky, v("IDN"), v("MK", 32 * d, 32 * d + 32))])
+            scan(v("KM", 32 * d, 32 * d + 32), v("RS", 0, 32), ky, OP.add, OP.min)
+        km, fd = v("KM", 15, 96, 16), v("FDP", 5, 11)
+        tt(fd, km, v("THR", 0, 6), OP.is_lt)
+        group([(pb(5, 0, 6), v("LT"), fd)] + [(pb(5, 0, 6), v("BB"), v("FDP", 5 - k, 11 - k)) for k in range(1, 6)])
+        tt(v("QQ", 0, 6), fd, v("QT", 0, 6), OP.mult)
+        tt(v("QQ", 0, 6), v("QQ", 0, 6), v("TN", 0, 6), OP.add)
+        tt(v("SS", 0, 6), pb(5, 0, 6), v("QQ", 0, 6), OP.add)
+        cp("V", v("SL", 0, 6), v("SS", 0, 6))
+        cp("V", v("K6", 0, 6), km)
+        ts(v("S6", 0, 6), v("K6", 0, 6), 255, AND)
+        tt(v("T6", 0, 6), v("S6", 0, 6), v("U6", 0, 6), OP.mult)
+        ts(v("C6", 0, 6), v("T6", 0, 6), W - 1, AND)
+        for f in range(4):
+            ts(v("FL", f, 24, 4), v("C6", 0, 6), 1.0 + f, OP.add)
         for d in range(3):
-            cp("A", v("FB", 128 * d, 128 * d + 128), ind(v("XR%d%d" % (rd, d)), v("FL", 8 * d, 8 * d + 8)))
+            cp("A", v("FB", 128 * d, 128 * d + 128), ind(v(XR[d], 0, W + 4), v("FL", 8 * d, 8 * d + 8)))
+        tt(v("PQ", 0, 6), v("SS", 0, 6), v("R4", 0, 6), OP.add)
         for c in range(6):
-            o = 8 * (c // 2) + c % 2, 8 * (c // 2) + 8, 2
-            act(v("FPF", *o), v("F4", 0, 4), AF.Identity, bias=v("P1", c, c + 1))
-        ts(v("KN"), v("P0", 0, 96), p15, OP.is_le, -4.0, OP.mult)
-        ts(v("CD"), v("P0", 0, 96), p15, OP.is_gt, -4.0, OP.mult)
-        cp("V", ind(v("WA", 0, 1304), v("SL", 0, 6)), v("KN"))
-        cp("V", ind(v("WB", 8, 1312), v("SL", 0, 6)), v("CD"))
-        for s in range(2):
-            o, h = (128 * s, 128 * s + 128), (512 * s, 512 * s + 512)
-            init = 0.0 if s == 0 else v("P34", 511, 512)
-            scan(v("P34", *h), v("WA", *h), v("WB", 512 * s + 4, 512 * s + 516), OP.add, OP.add, init)
-            tt(v("SR", *o), v("P34", 512 * s + 3, 512 * s + 512, 4), v("QF", *o), OP.add)
-            cp("V", v("SRL", *o), v("SR", *o))
-            cp("AV"[s], v(Xn, 2048 * s, 2048 * s + 2048), ind(v("Y0"), v("SRL", *o)))
-        cp("V", v("FP", 0, 24), v("FPF", 0, 24))
+            act(v("FPF", 4 * c, 4 * c + 4), v("FQ", 0, 4), AF.Identity, bias=v("PQ", c, c + 1))
+        ts(v("FP", 0, 24), v("FPF", 0, 24), 4.0, OP.mult)
+        cp("V", ind(v("WA"), v("SL", 0, 6)), v("VA"))
+        cp("V", ind(v("WB", 16, 1424), v("SL", 0, 6)), v("VB"))
+        for s, (lo, hi) in enumerate(((0, CUT), (CUT, 256))):
+            init = 0.0 if s == 0 else v("ZS", 4 * lo - 1, 4 * lo)
+            scan(v("ZS", 4 * lo, 4 * hi), v("WA", 4 * lo, 4 * hi), v("WB", 4 * lo + 15, 4 * hi + 15), OP.add, OP.add, init)
+            o = pb(6 + s, 0, hi - lo)
+            group([(o, v("IDN"), v("K16", lo, hi))] + [(o, v("DM", 128 * q, 128 * q + 128), v("ZS", 4 * lo + q, 4 * hi, 4)) for q in range(4)])
+            ts(v("SRL", lo, hi), o, p15, OP.add)
+            cp("AV"[s], v(Xn, 16 * lo, 16 * hi), ind(v("Y0"), v("SRL", lo, hi)))
         cp("V", ind(v(Xn), v("FP", 0, 24)), v("FB"))
     Xn = "XA" if RO % 2 == 0 else "XB"
     for c in range(4):

@@ -8,17 +8,26 @@ FREE = 1120
 XW = 5632
 F32, BF, I32, U16, F16 = "float32", "bfloat16", "int32", "uint16", "float16"
 SEGS = [(0, 64), (64, 192), (192, 256)]
-ON_SCALAR = ((0, 0), (0, 1), (0, 2), (0, 3))
+FOLDED = ((0, 0), (1, 0), (0, 1), (1, 1), (0, 2), (1, 2), (0, 3))
+NDD = 7
+TRIP = 9.0
+PIECES = ((0, 1024), (1024, W))
+CHAINS = ((0, 8),)
+SPREADS = ((0, 1), (1, 2), (2, 3), (3, 4))
+COPIES = "AAAAVAVA"
+EARLY = (6.0, 4.0, 2.0, 0.0)
 ODD = ((0, 4), (4, 4), (8, 4), (12, 3))
 SEARCH_V = (4, 5)
 CUT = 128
 RANK = float(1 << 20)
 FAR = float(1 << 23)
-WAKE = 0.1
+PASSES = 1500
+WAKE = 0.14
 CY = 0.00083
-PE = 0.0006
+PE = 0.0005
 
 SCRATCH = {}
+PLAN = []
 PLACE = {}
 
 
@@ -38,12 +47,14 @@ _buf("sbuf", XW, BF, "XA", "XB")
 _buf("sbuf", W, BF, "Y0", "XC")
 _buf("sbuf", W + 16, BF, "XR00", "XR01", "XR02", "XR10", "XR11", "XR12")
 _buf("sbuf", W, F32, "NX1", "NX2")
-_buf("sbuf", 1024, BF, "DD0", "DD1", "DD2", "DD3", "GA0", "GA1", "AB0", "AB1", "ZS")
-_buf("sbuf", 1024, I32, "KK", "CC")
+_buf("sbuf", 1024, BF, "ZS", "DP", *["DD%d" % k for k in range(4, NDD)], *["%s%d" % (n, k) for n in ("GA", "MX") for k in range(len(FOLDED))])
+PLACE.update({"DD%d" % k: ("Y0", 1024 * k, 1024) for k in range(4)})
+_buf("sbuf", 1024, I32, "CC")
+_buf("sbuf", 1280, I32, "KK")
+_buf("sbuf", 1280, F32, "RUN")
 _buf("sbuf", 1024, U16, "CL")
 _pack(256, I32, "hI", "QI", "UI", "UU", "HI", "KI", "NXI")
 _pack(256, U16, "hU", "NXL", "SRL")
-_pack(256, F32, "hF", "DEF", "RUN")
 _buf("sbuf", 256, F16, "NXH")
 _buf("sbuf", 256, BF, "K16")
 _pack(192, I32, "gI", "JI", "J15", "JG")
@@ -52,7 +63,7 @@ _pack(192, BF, "gB", "KEEP", "CMP")
 _pack(128, U16, "gU", "LE", "LO")
 _buf("sbuf", 2048, F16, "RE", "RD")
 _pack(128, F16, "zH", "Z0", "Z1", "Z2", "Z3", "RL")
-_buf("sbuf", 144, BF, "EZ", "EW", "EX", "EF", "EN", "ED", "ER", "EDR")
+_buf("sbuf", 144, BF, "EZ", "EW", "EX", "EF", "EN", "ED", "ER", "EDR", "EF2", "EFN", "EX2", "EXN")
 _buf("sbuf", 128, BF, "BB", "IDN", "NID", "LT", "UT", "WB0", "WB1", "WB2", "BL", "ONE", "CD", "NE", "F0", "F1")
 _buf("sbuf", 2048, BF, "SEL")
 _buf("sbuf", 512, BF, "DM", "GB")
@@ -63,10 +74,11 @@ _buf("sbuf", 136 * 6, BF, "JK")
 _buf("sbuf", 1408, BF, "WA")
 _buf("sbuf", 1424, BF, "WB")
 _buf("sbuf", 16, I32, "TH", "IC")
-_buf("sbuf", 32, F32, "FC")
+_buf("sbuf", 128, F32, "FC")
+_buf("sbuf", 320, BF, "PAT")
 _buf("sbuf", 16, BF, "WT", "FDP")
 _buf("sbuf", 4, F32, "PAR", "PR0", "PR1", "PR2")
-_pack(32, F32, "sF", "QF", "NW", "NWH", "TN", "M2", "FQ", "ACC", "THR", "H1", "QT", "QQ", "SS", "R4", "PQ", "FPF")
+_pack(32, F32, "sF", "QF", "NW", "NWH", "TN", "M2", "FQ", "ACC", "THR", "H1", "QT", "QQ", "SS", "R4", "PQ", "FPF", "CQ", "FIF")
 _pack(32, U16, "sU", "JL", "FL", "FP", "SL")
 _pack(32, I32, "sI", "WI", "U6", "H6", "Q6", "R6", "K6", "S6", "T6", "C6")
 _pack(96, F32, "uF", "RS", "KM")
@@ -80,14 +92,33 @@ _buf("psum", 1024, F32, "PA", "PB", "PC", "PD")
 NDMA = 20
 SEMAPHORES = ["sV", "sA", "sT", "sG", "par", "lpar"] + ["d%d" % i for i in range(NDMA)]
 SEMAPHORES += ["%s%d%d" % (k, r, h) for k in ("am", "ap", "aq", "lx", "lf") for r in range(RO) for h in range(2)]
+SEMAPHORES += ["%s%d%d" % (n, r, k) for n in ("fo", "fb", "fl") for r in range(RO) for k in range(len(FOLDED))] + ["back"]
 
 
 def rank_program(g, core, T, topo):
     rank = T.rank_of(core)
-    if rank is None:
-        return
     cores = list(T.cores)
     N = len(cores)
+    helper = {c: [h for h in topo.cores_of(c) if h not in cores and topo.die(h) == topo.die(c)][0] for c in cores}
+
+    def dst(c):
+        a = topo.addr(c)
+        return DstId(rid=a[0], pnc=a[1])
+
+    def stop_over(rd, k):
+        return T["XR%d%d" % (rd, k // 4)][:, 1024 * (k % 4):1024 * (k % 4) + 1024]
+
+    if rank is None:
+        for c in cores:
+            if helper[c] == core:
+                es = topo.engines(core, c)
+                for rd in range(RO):
+                    for k in range(len(FOLDED)):
+                        g.wait_ge(T.sem["fo%d%d" % (rd, k)], len(es))
+                        g.remote_dma_fused([RemoteDMATransfer(dst_ids=[dst(c)], dma_engine_mask=sum(1 << e for e in es), remote_sem=T.sem["fb%d%d" % (rd, k)],
+                                                              src=stop_over(rd, k), dst=T["MX%d" % k][:])], local_sem=T.sem["back"])
+                g.wait_ge(T.sem["back"], len(es) * RO * len(FOLDED))
+        return
     queue = {"V": g.vector, "A": g.scalar, "P": g.tensor, "G": g, "S": g.sync}
     qsem = {"V": "sV", "A": "sA", "P": "sT", "G": "sG"}
     count = {}
@@ -180,6 +211,9 @@ def rank_program(g, core, T, topo):
 
     ops = []
 
+    loose, open_ = {}, {}
+    ahead = {}
+
     def record(q, reads, writes, cost, lag, issue):
         rd, wr = [], []
         for x in reads:
@@ -202,7 +236,7 @@ def rank_program(g, core, T, topo):
                     n, lo, hi, st = bank(x)
                     psum = SCRATCH[n][0] == "psum"
                     for a in seen.get(n, ()):
-                        if not hits((lo, hi, st), a):
+                        if not hits((lo, hi, st), a) or (psum and i in loose and loose[i] == loose.get(a[3])):
                             continue
                         if psum and ops[a[3]][0] == q != "P":
                             if (a[4] or w) and hits(x[1:], a[5]):
@@ -218,7 +252,7 @@ def rank_program(g, core, T, topo):
                     n, lo, hi, st = bank(x)
                     l = seen.setdefault(n, [])
                     if SCRATCH[n][0] == "psum":
-                        if q == "P":
+                        if q == "P" and i not in loose:
                             l[:] = [a for a in l if not inside(a, lo, hi, st)]
                     elif w:
                         l[:] = [a for a in l if not inside(a, lo, hi, st)]
@@ -233,37 +267,57 @@ def rank_program(g, core, T, topo):
         def between(i, j):
             return 0.0 if ops[i][0] == ops[j][0] and ops[i][0] in ("P", "G", "S") else WAKE + ops[i][4]
 
+        forth = [[(j, between(i, j)) for j in succ[i]] for i in range(len(ops))]
+        back = [[(j, between(j, i)) for j in preds[i]] for i in range(len(ops))]
+
+        def lay(key, before, after):
+            at, left, busy, start = [0.0] * len(ops), [len(p) for p in before], {}, [0.0] * len(ops)
+            ready = [(key[i], i) for i in range(len(ops)) if not left[i]]
+            done = []
+            while ready:
+                first = min(ready)
+                ready.remove(first)
+                i = first[1]
+                q, c, t = ops[i][0], ops[i][3], at[i]
+                if q is not None:
+                    l = busy.setdefault(q, [])
+                    k = len(l)
+                    while k and l[k - 1][1] > t:
+                        k -= 1
+                    while k < len(l) and l[k][0] < t + c:
+                        t = max(t, l[k][1])
+                        k += 1
+                    l.insert(k, (t, t + c))
+                start[i] = t
+                done.append(i)
+                t += c
+                for j, gap in after[i]:
+                    if at[j] < t + gap:
+                        at[j] = t + gap
+                    left[j] -= 1
+                    if not left[j]:
+                        ready.append((key[j], j))
+            return start, done
+
         prio = [0.0] * len(ops)
         for i in range(len(ops) - 1, -1, -1):
-            prio[i] = ops[i][3] + max([prio[j] + between(i, j) for j in succ[i]], default=0.0)
-        left = [len(p) for p in preds]
-        at = [0.0] * len(ops)
-        free, ready, res = {}, {}, []
-        for i in range(len(ops)):
-            if not left[i]:
-                ready.setdefault(ops[i][0], []).append(i)
-        while ready:
-            best = None
-            for q, c in ready.items():
-                f = 0.0 if q is None else free.get(q, 0.0)
-                t0 = min(max(f, at[i]) for i in c)
-                if best is None or t0 < best[0]:
-                    best = (t0, q, f)
-            t0, q, f = best
-            c = ready[q]
-            i = max((i for i in c if max(f, at[i]) <= t0), key=lambda i: (prio[i], -i))
-            c.remove(i)
-            if not c:
-                del ready[q]
-            e = max(f, at[i]) + ops[i][3]
-            free[q] = e
-            res.append(i)
-            for j in succ[i]:
-                at[j] = max(at[j], e + between(i, j))
-                left[j] -= 1
-                if not left[j]:
-                    ready.setdefault(ops[j][0], []).append(j)
-        return res
+            prio[i] = ops[i][3] + ahead.get(i, 0.0) + max([prio[j] + between(i, j) for j in succ[i]], default=0.0)
+        key, best = [-p for p in prio], None
+        rng = np.random.default_rng(1)
+        for k in range(PASSES):
+            start, done = lay(key, back, forth)
+            end = max(start[i] + ops[i][3] + ops[i][4] for i in done)
+            if best is None or end <= best[0]:
+                best = (end, start, done)
+            if k < 3:
+                late, _ = lay([-(start[i] + ops[i][3]) for i in range(len(ops))], forth, back)
+                key = [-(late[i] + ops[i][3]) for i in range(len(ops))]
+            else:
+                t, w, was = rng.random() * best[0], (2.0, 5.0, 10.0)[k % 3], np.array(best[1])
+                some = (was > t) & (was < t + w) & (rng.random(len(ops)) < 0.3)
+                key = [float(x) for x in was + some * rng.normal(0, w / 5, len(ops))]
+        place = {i: k for k, i in enumerate(best[2])}
+        return sorted(best[2], key=lambda i: (best[1][i], place[i]))
 
     def many(x):
         if x[0] == "ind":
@@ -349,9 +403,29 @@ def rank_program(g, core, T, topo):
     def mm(out, l, r, start=True, stop=True):
         emit("P", "mm", [l, r], [out], lambda e: e.matmul(ap(out), ap(l), ap(r), start, stop))
 
+    def mms(calls, flags):
+        def f(e):
+            for k, (out, l, r) in enumerate(calls):
+                last = e.matmul(ap(out), ap(l), ap(r), *flags(k))
+            return last
+        emit("P", "mm", [x for c in calls for x in c[1:]], [calls[0][0]], f)
+        ops[-1] = ops[-1][:3] + (sum(cost("P", "mm", out, [l, r]) for out, l, r in calls),) + ops[-1][4:]
+
     def group(calls):
-        for i, (out, l, r) in enumerate(calls):
-            mm(out, l, r, i == 0, i == len(calls) - 1)
+        mms(calls, lambda k: (k == 0, k == len(calls) - 1))
+
+    def each(calls):
+        mms(calls, lambda k: (True, True))
+
+    def add_to(name, calls):
+        loose[len(ops)] = name
+        open_[name] = open_.get(name, 0) + 1
+
+        def flags(k):
+            if k == len(calls) - 1:
+                open_[name] -= 1
+            return False, open_[name] == 0
+        mms(calls, flags)
 
     def iota(out, pattern, base, cm):
         if SCRATCH[out[0]][2] == I32:
@@ -368,18 +442,19 @@ def rank_program(g, core, T, topo):
     AND, SHR = OP.bitwise_and, OP.logical_shift_right
     wtq = v("WT", 0, 1)
     for k, n in enumerate(("XA", "XC")):
-        for c in range(4):
-            x = v(n, 1024 * c, 1024 * c + 1024)
-            dma("S", ap(x), T.x0[:, 1024 * c:1024 * c + 1024], [], [x], 2.8 + 0.7 * (4 * k + c))
+        for lo, hi in PIECES:
+            dma("S", ap(v(n, lo, hi)), T.x0[:, lo:hi], [], [v(n, lo, hi)], 2.1 + 0.0007 * (W * k + hi))
     dma("A", ap(wtq), T.wt[:], [], [wtq])
     dma("A", ap(v("TH", 0, 2)), T.th[:], [], [v("TH", 0, 2)])
     iota(v("IC", 0, 1), [[1, 1]], 0, 1)
     iota(v("JI"), [[1, 192]], 0, 0)
     iota(v("QI"), [[16, 256]], 0, 1)
     iota(v("ONE"), [[0, 128]], 1, 0)
+    iota(v("PAT"), [[0, 64], [1, 5]], 0, 0)
+    ts(v("PAT"), v("PAT"), 1.0, OP.min)
     iota(v("FDP"), [[0, 16]], 0, 0)
     iota(v("K16"), [[16, 256]], 0, 0)
-    iota(v("M2", 0, 16), [[2, 16]], 0, 0)
+    iota(v("MK", 0, 32), [[0, 2], [2, 16]], 1, 0)
     iota(v("FQ", 4, 8), [[1, 4]], 0, 0)
     iota(v("NW", 8, 14), [[32, 3], [8, 2]], 0, 0)
     iota(v("TN", 8, 14), [[32, 6]], FREE, 2)
@@ -413,6 +488,8 @@ def rank_program(g, core, T, topo):
     ts(v("IDN"), J, pf, OP.is_equal)
     times(v("NID"), v("IDN"), -1.0)
     times(v("EF"), v("EZ"), FAR)
+    times(v("EF2"), v("EZ"), 2 * FAR)
+    times(v("EFN"), v("EZ"), -FAR)
     ts(v("J15"), v("JI"), 15, AND)
     ts(v("JG", 0, 128), J, 112, AND)
     ts(v("MASK"), v("J15"), p15, OP.is_equal)
@@ -430,13 +507,15 @@ def rank_program(g, core, T, topo):
     times(v("BL"), v("BB"), hi_)
     for a in range(16):
         times(sel(a), v("BB"), v("MASK", a, a + 1))
-    ts(v("DEF"), v("QI"), pg, OP.subtract, 4 * RANK, OP.add)
+    ts(v("KK", 0, 1280, 5), v("QI"), pg, OP.subtract, 4 * RANK, OP.add)
     ts(v("QF", 0, 8), v("QI", 0, 8), pg, OP.subtract)
     ts(v("LE", 0, 8), v("QF", 0, 8), 32.0, OP.mult)
     tt(v("RE", 0, 128), v("TT0"), v("MASK", 0, 128), OP.mult)
     times(v("EN"), v("EZ"), -1.0)
     times(v("ER"), v("EZ"), 0.0625)
     times(v("EX"), v("EZ"), 256.0)
+    times(v("EX2"), v("EZ"), 512.0)
+    times(v("EXN"), v("EZ"), -256.0)
     tt(v("ED", 0, 143), v("EZ", 1, 144), v("EZ", 0, 143), OP.subtract)
     times(v("EDR"), v("ED"), 0.0625)
     ts(v("CD"), v("ONE"), 256.0, OP.mult, first, OP.subtract)
@@ -466,11 +545,10 @@ def rank_program(g, core, T, topo):
         return (T.rank_of(owner) - T.rank_of(receiver) - 1) % N
 
     off = topo.engines(core, mate)
-    on = [e for e in topo.engines(core, near) if e not in off]
+    both = topo.engines(core, near)
+    on = [e for e in both if e not in off]
 
-    def dst(c):
-        a = topo.addr(c)
-        return DstId(rid=a[0], pnc=a[1])
+    sent, landed = [0], []
 
     def remote(transfers, local, reads):
         n = sum(len(es) for _, _, _, es, _ in transfers)
@@ -482,20 +560,22 @@ def rank_program(g, core, T, topo):
                                 for c, s, d, es, rs in transfers], local_sem=T.sem[local])
             snap[(local, count[local])] = dict(known["G"])
             note("Gremote", reads, [], local, count[local])
-        record("G", reads, [], 1.0, 8.0, issue)
+        sent[0] += 1
+        record("G", reads, [fc(31 + sent[0])], 1.0, 8.0, issue)
+        return fc(31 + sent[0])
 
-    def arrives(name, lo, hi, sem, n, like=()):
+    def arrives(name, lo, hi, sem, n, like):
         def issue():
             count[sem] = n
             note("remote", [], [v(name, lo, hi)], sem, n)
-        record(None, list(like), [v(name, lo, hi)], 0.0, 12.0, issue)
-
-    for d in range(3):
-        arrives("PR%d" % d, 0, 4, "par", 3)
+        landed.append(fc(64 + len(landed)))
+        record(None, [like], [v(name, lo, hi), landed[-1]], 0.0, 2.0, issue)
 
     def send_params():
-        remote([(c, ap(v("PAR")), T["PR%d" % slot(c, core)][:], [es], "par")
-                for c, es in ((near, on[0]), (mate, off[0]), (diag, off[1]))], "lpar", [v("PAR")])
+        call = remote([(c, ap(v("PAR")), T["PR%d" % slot(c, core)][:], [es], "par")
+                       for c, es in ((near, on[0]), (mate, off[0]), (diag, off[1]))], "lpar", [v("PAR")])
+        for d in range(3):
+            arrives("PR%d" % d, 0, 4, "par", 3, call)
 
     def halves():
         return [(h, 2048 * h, 2048 * h + 2048) for h in range(2)]
@@ -503,33 +583,46 @@ def rank_program(g, core, T, topo):
     def broadcast(rd, x):
         for h, lo, hi in halves():
             src = v(x, lo, hi)
-            remote([(mate, ap(src), T["XR%d%d" % (rd, slot(mate, core))][:, lo:hi], off, "am%d%d" % (rd, h)),
-                    (near, ap(src), T["XR%d%d" % (rd, slot(near, core))][:, lo:hi], on, "ap%d%d" % (rd, h))], "lx%d%d" % (rd, h), [src, v("XC")])
-        for h, lo, hi in halves():
-            src = v(x, lo, hi)
-            a, b, c = ("XR%d%d" % (rd, slot(core, o)) for o in (mate, near, diag))
-            arrives(a, lo, hi, "am%d%d" % (rd, h), len(off), [src])
-            arrives(b, lo, hi, "ap%d%d" % (rd, h), len(on), [src])
-            arrives(c, lo, hi, "aq%d%d" % (rd, h), len(on), [src])
+            call = remote([(mate, ap(src), T["XR%d%d" % (rd, slot(mate, core))][:, lo:hi], off, "am%d%d" % (rd, h)),
+                           (near, ap(src), T["XR%d%d" % (rd, slot(near, core))][:, lo:hi], on, "ap%d%d" % (rd, h))], "lx%d%d" % (rd, h),
+                          [src])
+            arrives("XR%d%d" % (rd, slot(core, mate)), lo, hi, "am%d%d" % (rd, h), len(off), call)
+            arrives("XR%d%d" % (rd, slot(core, near)), lo, hi, "ap%d%d" % (rd, h), len(on), call)
 
     def hand_on(rd):
         for h, lo, hi in halves():
             src = v("XR%d%d" % (rd, slot(core, mate)), lo, hi)
-            remote([(near, ap(src), T["XR%d%d" % (rd, slot(near, mate))][:, lo:hi], on, "aq%d%d" % (rd, h))], "lf%d%d" % (rd, h), [src])
+            call = remote([(near, ap(src), T["XR%d%d" % (rd, slot(near, mate))][:, lo:hi], both, "aq%d%d" % (rd, h))], "lf%d%d" % (rd, h), [src])
+            arrives("XR%d%d" % (rd, slot(core, diag)), lo, hi, "aq%d%d" % (rd, h), len(both), call)
 
+    def fold(rd, k, a, b):
+        local, es = "fl%d%d" % (rd, k), topo.engines(core, helper[core])
+
+        def issue():
+            order("G", [a, b], [])
+            count[local] = len(es)
+            g.remote_dma_fused([RemoteDMATransfer(dst_ids=[dst(helper[core])], dma_engine_mask=sum(1 << e for e in es), remote_sem=T.sem["fo%d%d" % (rd, k)],
+                                                  srcs=[ap(a), ap(b)], dsts=[stop_over(rd, k)], alu_op=2)], local_sem=T.sem[local])
+            snap[(local, len(es))] = dict(known["G"])
+            note("Gremote", [a, b], [], local, len(es))
+        sent[0] += 1
+        record("G", [a, b], [fc(31 + sent[0])], 1.0, TRIP - 3.0, issue)
+        arrives("MX%d" % k, 0, 1024, "fb%d%d" % (rd, k), len(es), fc(31 + sent[0]))
+
+    send_params()
     for rd in range(RO):
         X, Xn = ("XA", "XB") if rd % 2 == 0 else ("XB", "XA")
         XR = ["XR%d%d" % (rd, d) for d in range(3)]
         if rd > 0:
-            for c in range(4):
-                x, y = v(X, 1024 * c, 1024 * c + 1024), v("XC", 1024 * c, 1024 * c + 1024)
-                dma("S", ap(y), ap(x), [x], [y], 2.8 + 0.7 * c)
-        broadcast(rd, X)
-        if rd == 0:
-            send_params()
-        iota(v("WA", 0, 1024), [[0, 1024]], 0, 0)
-        iota(v("WB", 0, 1040), [[0, 1040]], 0, 0)
-        hand_on(rd)
+            for lo, hi in PIECES:
+                x, y = v(X, lo, hi), v("XC", lo, hi)
+                dma("S", ap(y), ap(x), [x], [y], 2.1 + 0.0007 * hi)
+
+        def sends():
+            broadcast(rd, X)
+            hand_on(rd)
+            iota(v("WA", 0, 1024), [[0, 1024]], 0, 0)
+            iota(v("WB", 0, 1040), [[0, 1040]], 0, 0)
 
         def seg(q):
             return [s for s, (lo, hi) in enumerate(SEGS) if lo <= 64 * q < hi][0]
@@ -550,69 +643,61 @@ def rank_program(g, core, T, topo):
             ts(u, v("UI", lo, hi), W - 1, AND)
             ts(h1, h, 1.0, OP.add)
             ts(u2, u, 2.0, OP.mult, RANK, OP.add)
-            tt(part("KK", s, 0, 1), h1, u, OP.mult)
+            keys = [v("KK", 5 * lo + 4 - m, 5 * hi, 5) for m in range(4)]
+            tt(keys[0], h1, u, OP.mult)
             for m in range(1, 4):
-                tt(part("KK", s, m, m + 1), u2, part("KK", s, m - 1, m), OP.add)
-            for m0, m1 in ((0, 1), (1, 4)) if s == 0 else ((0, 4),):
-                ts(part("CC", s, m0, m1), part("KK", s, m0, m1), W - 1, AND)
+                tt(keys[m], u2, keys[m - 1], OP.add)
+            for m in range(4):
+                ts(part("CC", s, m, m + 1), keys[m], W - 1, AND)
+            for m0, m1 in ((0, 1), (1, 2), (2, 4)) if s == 0 else ((0, 4),):
                 cp("V", part("CL", s, m0, m1), part("CC", s, m0, m1))
 
         dn, an = [0], [0]
-        LAST = 3
-
-        def dist(s, m0, m1):
-            w = SEGS[s][1] - SEGS[s][0]
-            if s == len(SEGS) - 1 and m0 == LAST:
-                return pb(1, 0, w)
-            return pb(2 + s % 2, w * m0, w * m1)
 
         def unit(m, q):
             s = seg(q)
             win, x = ind(v(X, 0, W), part("CL", s, m, m + 1, 64 * q, 64 * q + 64)), (1024 * q, 1024 * q + 1024)
-            n, o, _, _ = dist(s, m, m + 1)
-            o += 64 * q - SEGS[s][0]
-            if (m, q) in ON_SCALAR:
-                b, c = "GA%d" % (an[0] % 2), "AB%d" % (an[0] % 2)
-                an[0] += 1
-                for k in range(2):
-                    mm(pb(4 + k), v("NID"), v(X, x[0] + 512 * k, x[0] + 512 * k + 512), True, False)
-                cp("A", v(b), win)
-                for k in range(2):
-                    mm(pb(4 + k), v("IDN"), v(b, 512 * k, 512 * k + 512), False, True)
-                act(v(c), v("PC"), AF.Abs)
+            if (m, q) in FOLDED:
+                k = FOLDED.index((m, q))
+                cp("A", v("GA%d" % k), win)
+                fold(rd, k, v("GA%d" % k), v(X, *x))
+                sums = [("EFN", X, x[0]), ("EFN", "GA%d" % k, 0), ("EF2", "MX%d" % k, 0)]
             else:
-                c = "DD%d" % (dn[0] % 4)
+                c = "DD%d" % (dn[0] % NDD)
                 dn[0] += 1
                 tt(v(c), win, v("XC", *x), OP.subtract)
                 act(v(c), v(c), AF.Abs)
-            out = (n, o, o + 64, 1)
-            group([(out, v("BL"), v("ONE", 0, 64))] + [(out, ez("EF", a), v(c, a, 1024, 16)) for a in range(16)])
+                sums = [("EF", c, 0)]
+            out = pb(2 + q, 4 - m, 320, 5)
+            for e, n, o in sums:
+                add_to((rd, q), [(out, ez(e, a), v(n, o + a, o + 1024, 16)) for a in range(16)])
 
-        def nearest(s):
-            lo, hi = SEGS[s]
-            o = (lo, hi)
-            for m0, m1 in ((0, LAST), (LAST, 4)) if s == len(SEGS) - 1 else ((0, 4),):
-                tt(dist(s, m0, m1), dist(s, m0, m1), part("KK", s, m0, m1), OP.max)
+        def nearest(q):
+            mm(pb(2 + q, 0, 320), v("BL"), v("PAT"), True, False)
             for m in range(4):
-                tt(v("RUN", *o), dist(s, m, m + 1), v("DEF" if m == 0 else "RUN", *o), OP.min)
-            ts(v("KI", *o), v("RUN", *o), 1.0, OP.add)
+                unit(m, q)
+            scan(v("RUN", 320 * q, 320 * q + 320), pb(2 + q, 0, 320), v("KK", 320 * q, 320 * q + 320), OP.min, OP.max)
+
+        def spread(q0, q1):
+            o = (64 * q0, 64 * q1)
+            ts(v("KI", *o), v("RUN", 320 * q0 + 4, 320 * q1, 5), 1.0, OP.add)
             ts(v("NXI", *o), v("KI", *o), W - 1, AND)
             ts(v("NXH", *o), v("NXI", *o), -2048.0, OP.add)
             cp("V", v("NXL", *o), v("NXI", *o))
-            for q in range(lo // 64, hi // 64):
-                banks = (0, 3) if q == 2 else (6, 7)
-                for a in range(16):
-                    mm(pb(banks[a % 2], a // 2, 512, 8), sel(a), v("NXH", 64 * q, 64 * q + 64))
+            for q in range(q0, q1):
+                banks = (0, 1) if q % 2 else (6, 7)
                 for b in range(2):
-                    cp("VA"[b] if q == 3 else "A", v("NX1", 1024 * q + b, 1024 * q + 1024, 2), pb(banks[b]))
+                    each([(pb(banks[b], a // 2, 512, 8), sel(a), v("NXH", 64 * q, 64 * q + 64)) for a in range(b, 16, 2)])
+                    cp(COPIES[2 * q + b], v("NX1", 1024 * q + b, 1024 * q + 1024, 2), pb(banks[b]))
+                    ahead[len(ops) - 1] = EARLY[q]
 
         for s in range(len(SEGS)):
             looks(s)
-        for s, (lo, hi) in enumerate(SEGS):
-            for q in range(lo // 64, hi // 64):
-                for m in range(4):
-                    unit(m, q)
-            nearest(s)
+        for q0, q1 in SPREADS:
+            for q in range(q0, q1):
+                nearest(q)
+            spread(q0, q1)
+        sends()
         cp("V", v("NX2", 0, 2048), ind(v("NX1"), v("NXL", 0, 128)))
         cp("A", v("NX2", 2048, 4096), ind(v("NX1"), v("NXL", 128, 256)))
 
@@ -632,12 +717,13 @@ def rank_program(g, core, T, topo):
                     mm(pb(0, 0, 128), ez("EZ", 15), r, False, k == steps[0])
 
         def flags(h):
-            d = pb(h, 0, 128)
-            if h:
-                ts(v("NE"), d, 4096.0, OP.not_equal, keep, OP.mult)
-            else:
-                ts(v("NE"), d, 4096.0, OP.not_equal)
-            tt(v("F%d" % h), d, v("NE"), OP.min)
+            for lo, hi in ((0, 128),) if h else ((0, 64), (64, 128)):
+                d, ne = pb(h, lo, hi), v("NE", lo, hi)
+                if h:
+                    ts(ne, d, 4096.0, OP.not_equal, keep, OP.mult)
+                else:
+                    ts(ne, d, 4096.0, OP.not_equal)
+                tt(v("F%d" % h, lo, hi), d, ne, OP.min)
 
         steps[0], steps[1] = 16, 31
         for h in range(2):
@@ -647,9 +733,11 @@ def rank_program(g, core, T, topo):
             le = v("LE", 8 * i, 8 * i + 8)
             if i < 15:
                 r, z = v("RE", 128 * i + 128, 128 * i + 256), "Z%d" % (i % 4)
-                tt(r, ind(v("NX2"), le), v("MASK", 0, 128), OP.mult)
-                scan(v(z), v("KEEP", 0, 128), r, OP.mult, OP.add)
-                ts(v("LE", 8 * i + 8, 8 * i + 16), v(z, 15, 128, 16), 2048.0, OP.add)
+                for lo, hi in CHAINS:
+                    some = v("RE", 128 * i + 128 + 16 * lo, 128 * i + 128 + 16 * hi)
+                    tt(some, ind(v("NX2"), v("LE", 8 * i + lo, 8 * i + hi)), v("MASK", 0, 16 * (hi - lo)), OP.mult)
+                    scan(v(z, 16 * lo, 16 * hi), v("KEEP", 0, 16 * (hi - lo)), some, OP.mult, OP.add)
+                    ts(v("LE", 8 * i + 8 + lo, 8 * i + 8 + hi), v(z, 16 * lo + 15, 16 * hi, 16), 2048.0, OP.add)
             else:
                 tt(v("RL"), ind(v("NX1"), le), v("MASK", 0, 128), OP.mult)
                 step(31, v("RL"), "ED")
@@ -694,6 +782,7 @@ def rank_program(g, core, T, topo):
         parts = (v("BG"), v("CMP", 0, 96), v("CMP", 96, 192))
         group([(pb(6, 0, 96), v("BB"), x) for x in parts])
         ts(v("PL"), pb(6, 0, 96), -1.0, OP.add)
+        ops[-1][1].extend(landed)
         for d in range(3):
             for e in range(2):
                 group([(pb(7, 32 * d + 16 * e, 32 * d + 16 * e + 16), v("BB"), (x[0], x[1] + 32 * d + e, x[1] + 32 * d + 32, 2)) for x in parts])
@@ -705,12 +794,13 @@ def rank_program(g, core, T, topo):
             for d in range(3):
                 times(v("WB%d" % d), v("BB"), v("PR%d" % d, 0, 1))
         for d in range(3):
-            cp("A", v(XR[d], W, W + 4), v(XR[d], 0, 4))
+            o, i_ = v(XR[d], W, W + 4), v(XR[d], 0, 4)
+            emit("A", "", [i_, v("PL")], [o], lambda e, o=o, i_=i_: e.activation(ap(o), ap(i_), AF.Copy))
         for d in range(3):
             mm(pb(0, 32 * d, 32 * d + 32), v("WB%d" % d), v("AR", 512 * d, 512 * d + 512, 16))
         for d in range(3):
             for e in range(2):
-                mm(pb(7, 96 + 32 * d + 16 * e, 112 + 32 * d + 16 * e), v("WB%d" % d), v("AR", 512 * d + 16 * e, 512 * d + 512, 32))
+                mm(pb(5, 32 * d + 16 * e, 16 + 32 * d + 16 * e), v("WB%d" % d), v("AR", 512 * d + 16 * e, 512 * d + 512, 32))
         cp("V", v("AI"), pb(0, 0, 96))
         ts(v("AH"), v("AI"), 5, SHR, 127, AND)
         ts(v("AU"), v("AI"), W - 1, AND)
@@ -719,13 +809,12 @@ def rank_program(g, core, T, topo):
         ts(v("AC"), v("AT"), W - 1, AND)
         cp("V", v("TL"), v("AC"))
         cp("V", v("RI"), pb(7, 0, 96))
-        tt(v("VM"), pb(7, 0, 192), v("MASK"), OP.mult)
-        scan(v("ZV"), v("KEEP"), v("VM"), OP.mult, OP.add)
-        cp("V", v("WI", 0, 12), v("ZV", 15, 192, 16))
+        for k, b in enumerate((7, 5)):
+            o = (96 * k, 96 * k + 96)
+            tt(v("VM", *o), pb(b, 0, 96), v("MASK", 0, 96), OP.mult)
+            scan(v("ZV", *o), v("KEEP", 0, 96), v("VM", *o), OP.mult, OP.add)
+            cp("V", v("WI", 6 * k, 6 * k + 6), v("ZV", o[0] + 15, o[1], 16))
         ts(v("H6", 0, 6), v("WI", 6, 12), 5, SHR, 127, AND)
-        ts(v("H1", 0, 6), v("H6", 0, 6), 1.0, OP.add)
-        for c in range(6):
-            act(v("MK", 16 * c, 16 * c + 16), v("M2", 0, 16), AF.Identity, bias=v("H1", c, c + 1))
         ts(v("U6", 0, 6), v("WI", 6, 12), W - 1, AND)
         ts(v("Q6", 0, 6), v("WI", 0, 6), 2, SHR)
         ts(v("R6", 0, 6), v("WI", 0, 6), 3, AND)
@@ -743,10 +832,13 @@ def rank_program(g, core, T, topo):
                 act(o, pb(1), AF.Abs)
             else:
                 tt(o, win, v("AR", 512 * d, 512 * d + 512), OP.subtract)
-                act(o, o, AF.Abs)
+                if d == 0:
+                    act(o, o, AF.Abs)
+                else:
+                    ts(v("DP", 0, 512), o, 0.0, OP.max)
             ky = pb(2 + d, 0, 32)
-            group([(ky, ez("EX", a), v("AD", 512 * d + 32 * a, 512 * d + 32 * a + 32)) for a in range(16)]
-                  + [(ky, v("IDN"), v("MK", 32 * d, 32 * d + 32))])
+            sums = [("EXN", "AD", 512), ("EX2", "DP", 0)] if d == 1 else [("EX", "AD", 512 * d)]
+            group([(ky, v("IDN"), v("MK", 0, 32))] + [(ky, ez(e, a), v(x, o + 32 * a, o + 32 * a + 32)) for e, x, o in sums for a in range(16)])
             scan(v("KM", 32 * d, 32 * d + 32), v("RS", 0, 32), ky, OP.add, OP.min)
         km, fd = v("KM", 15, 96, 16), v("FDP", 5, 11)
         tt(fd, km, v("THR", 0, 6), OP.is_lt)
@@ -757,10 +849,13 @@ def rank_program(g, core, T, topo):
         cp("V", v("SL", 0, 6), v("SS", 0, 6))
         cp("V", v("K6", 0, 6), km)
         ts(v("S6", 0, 6), v("K6", 0, 6), 255, AND)
+        tt(v("S6", 0, 6), v("S6", 0, 6), v("H6", 0, 6), OP.add)
         tt(v("T6", 0, 6), v("S6", 0, 6), v("U6", 0, 6), OP.mult)
         ts(v("C6", 0, 6), v("T6", 0, 6), W - 1, AND)
-        for f in range(4):
-            ts(v("FL", f, 24, 4), v("C6", 0, 6), 1.0 + f, OP.add)
+        ts(v("CQ", 0, 6), v("C6", 0, 6), 1.0, OP.add)
+        for c in range(6):
+            act(v("FIF", 4 * c, 4 * c + 4), v("FQ", 4, 8), AF.Identity, bias=v("CQ", c, c + 1))
+        cp("V", v("FL", 0, 24), v("FIF", 0, 24))
         for d in range(3):
             cp("A", v("FB", 128 * d, 128 * d + 128), ind(v(XR[d], 0, W + 4), v("FL", 8 * d, 8 * d + 8)))
         tt(v("PQ", 0, 6), v("SS", 0, 6), v("R4", 0, 6), OP.add)
@@ -778,10 +873,10 @@ def rank_program(g, core, T, topo):
             cp("AV"[s], v(Xn, 16 * lo, 16 * hi), ind(v("Y0"), v("SRL", lo, hi)))
         cp("V", ind(v(Xn), v("FP", 0, 24)), v("FB"))
     Xn = "XA" if RO % 2 == 0 else "XB"
-    for c in range(4):
-        x = v(Xn, 1024 * c, 1024 * c + 1024)
-        dma("SA"[c % 2], T.y[:, 1024 * c:1024 * c + 1024], ap(x), [x], [])
-    for i in plan():
+    dma("S", T.y[:], ap(v(Xn, 0, W)), [v(Xn, 0, W)], [], 5.0)
+    if not PLAN:
+        PLAN.extend(plan())
+    for i in PLAN:
         now[0] = i
         ops[i][5]()
     for s in SEMAPHORES:

@@ -4,25 +4,40 @@ from concourse.mybir import dt, AluOpType as OP, AxisListType, ActivationFunctio
 
 W = 4096
 RO = 2
+RW = W + 8
+ASKED = ((0, 5), (5, 11), (11, 16))
 FREE = 1120
 XW = 5632
 F32, BF, I32, U16, F16 = "float32", "bfloat16", "int32", "uint16", "float16"
-SEGS = [(0, 64), (64, 192), (192, 256)]
-FOLDED = ((0, 0), (1, 0), (0, 1), (1, 1), (0, 2), (1, 2), (0, 3))
-NDD = 7
+HASH = (0, 1, 7)
+SEGS = [(0, 64), (64, 128), (128, 256)]
+BY_VECTOR = ((3, 0),)
+FOLDED = ((0, 0), (1, 0), (3, 0), (2, 0), (0, 2), (0, 3), (1, 3))
+ORDER = "a9 g00 a3 g10 a5 b14 c9 g30 g20 c6 g02 g11 g03 g21 g13 g31 g01 g12 r11 r00 r10 g22 r01 r30 r21 r20 g32 r31 r02 n1 r12 n0 g23 r22 r03 g33 r32 r13 r23 n2 r33 n3 s1 s0 s2 s3"
+NSEL = 6
+CALLS = ((0,), (1,), (2, 3), (4,), (5,), (6,))
+SPREAD = ((0, 1), (6, 7), (2, 3), (4, 5))
+ON_SCALAR = ((0, 1),)
+BY_SCALAR = ()
+OWN = ((0, 64), (128, 256))
+HALVED = ()
+ON_VECTOR = ()
+LISTS = (((0, 1), (1, 2), (2, 3), (3, 4)), ((0, 4),), ((0, 1), (1, 4)))
+NDD = 9
 TRIP = 9.0
-PIECES = ((0, 1024), (1024, W))
-CHAINS = ((0, 8),)
-SPREADS = ((0, 1), (1, 2), (2, 3), (3, 4))
-COPIES = "AAAAVAVA"
-EARLY = (6.0, 4.0, 2.0, 0.0)
+PIECES = ((0, 1024), (1024, 2048), (2048, W))
+AGAIN = ((2048, 3072),)
+CHAINS = ((0, 4), (4, 8))
+COPIES = "VAAAVAVA"
 ODD = ((0, 4), (4, 4), (8, 4), (12, 3))
+SOON = (9.0, 6.0, 3.0, 0.0)
 SEARCH_V = (4, 5)
 CUT = 128
+LAST = ((("A", 0, 68), ("V", 68, 128)), (("A", 128, 222), ("V", 222, 256)))
 RANK = float(1 << 20)
 FAR = float(1 << 23)
-PASSES = 1500
-WAKE = 0.14
+PASSES = 5000
+WAKE = 0.16
 CY = 0.00083
 PE = 0.0005
 
@@ -45,17 +60,20 @@ def _pack(cols, dtype, host, *names):
 
 _buf("sbuf", XW, BF, "XA", "XB")
 _buf("sbuf", W, BF, "Y0", "XC")
-_buf("sbuf", W + 16, BF, "XR00", "XR01", "XR02", "XR10", "XR11", "XR12")
+for _r in range(RO):
+    _pack(RW, BF, "XR%d" % _r, *["XR%d%d" % (_r, d) for d in range(3)])
+    PLACE["XR%d" % _r] = ("XR%d" % _r, 0, 3 * RW)
 _buf("sbuf", W, F32, "NX1", "NX2")
-_buf("sbuf", 1024, BF, "ZS", "DP", *["DD%d" % k for k in range(4, NDD)], *["%s%d" % (n, k) for n in ("GA", "MX") for k in range(len(FOLDED))])
-PLACE.update({"DD%d" % k: ("Y0", 1024 * k, 1024) for k in range(4)})
+_buf("sbuf", 1024, BF, "ZS", *["GS%d" % k for k in range(len(ON_SCALAR))], *["%s%d" % (n, k) for n in ("GA", "MX") for k in range(len(FOLDED))])
+for _k, _p in enumerate([("Y0", 1024 * k) for k in range(4)] + [("AR", 0), ("AD", 0), ("ZS", 0), ("WA", 0), ("WB", 0)]):
+    PLACE["DD%d" % _k] = _p + (1024,)
 _buf("sbuf", 1024, I32, "CC")
 _buf("sbuf", 1280, I32, "KK")
 _buf("sbuf", 1280, F32, "RUN")
 _buf("sbuf", 1024, U16, "CL")
 _pack(256, I32, "hI", "QI", "UI", "UU", "HI", "KI", "NXI")
 _pack(256, U16, "hU", "NXL", "SRL")
-_buf("sbuf", 256, F16, "NXH")
+_buf("sbuf", 256, F16, "NXH", "SBH")
 _buf("sbuf", 256, BF, "K16")
 _pack(192, I32, "gI", "JI", "J15", "JG")
 _pack(192, F32, "gF", "MASK", "NLIN", "VM", "ZV")
@@ -64,9 +82,10 @@ _pack(128, U16, "gU", "LE", "LO")
 _buf("sbuf", 2048, F16, "RE", "RD")
 _pack(128, F16, "zH", "Z0", "Z1", "Z2", "Z3", "RL")
 _buf("sbuf", 144, BF, "EZ", "EW", "EX", "EF", "EN", "ED", "ER", "EDR", "EF2", "EFN", "EX2", "EXN")
-_buf("sbuf", 128, BF, "BB", "IDN", "NID", "LT", "UT", "WB0", "WB1", "WB2", "BL", "ONE", "CD", "NE", "F0", "F1")
+_buf("sbuf", 128, BF, "BB", "IDN", "NID", "LT", "UT", "WB0", "WB1", "WB2", "BL", "ONE", "CD", "NE", "F0", "F1", "NF", "NF2")
 _buf("sbuf", 2048, BF, "SEL")
 _buf("sbuf", 512, BF, "DM", "GB")
+_buf("sbuf", 768, BF, "DP")
 _buf("sbuf", 128, F32, "END", "TT0", "TT1")
 _buf("sbuf", 272, F32, "GW")
 _buf("sbuf", 136, F32, "BW")
@@ -76,9 +95,9 @@ _buf("sbuf", 1424, BF, "WB")
 _buf("sbuf", 16, I32, "TH", "IC")
 _buf("sbuf", 128, F32, "FC")
 _buf("sbuf", 320, BF, "PAT")
-_buf("sbuf", 16, BF, "WT", "FDP")
+_buf("sbuf", 16, BF, "WT", "FD")
 _buf("sbuf", 4, F32, "PAR", "PR0", "PR1", "PR2")
-_pack(32, F32, "sF", "QF", "NW", "NWH", "TN", "M2", "FQ", "ACC", "THR", "H1", "QT", "QQ", "SS", "R4", "PQ", "FPF", "CQ", "FIF")
+_pack(32, F32, "sF", "QF", "NW", "NWH", "TN", "NQ", "FQ", "ACC", "THR", "OF", "QT", "QQ", "SS", "R4", "PQ", "FPF", "CQ", "FIF")
 _pack(32, U16, "sU", "JL", "FL", "FP", "SL")
 _pack(32, I32, "sI", "WI", "U6", "H6", "Q6", "R6", "K6", "S6", "T6", "C6")
 _pack(96, F32, "uF", "RS", "KM")
@@ -93,31 +112,58 @@ NDMA = 20
 SEMAPHORES = ["sV", "sA", "sT", "sG", "par", "lpar"] + ["d%d" % i for i in range(NDMA)]
 SEMAPHORES += ["%s%d%d" % (k, r, h) for k in ("am", "ap", "aq", "lx", "lf") for r in range(RO) for h in range(2)]
 SEMAPHORES += ["%s%d%d" % (n, r, k) for n in ("fo", "fb", "fl") for r in range(RO) for k in range(len(FOLDED))] + ["back"]
+SEMAPHORES += ["ah%d" % r for r in range(RO)]
 
 
 def rank_program(g, core, T, topo):
     rank = T.rank_of(core)
     cores = list(T.cores)
     N = len(cores)
-    helper = {c: [h for h in topo.cores_of(c) if h not in cores and topo.die(h) == topo.die(c)][0] for c in cores}
+    helper = {c: [h for h in topo.cores_of(c) if h not in cores and topo.die(h) == topo.die(c) and not all(topo.may_write(h, o) for o in cores)][0]
+              for c in cores}
 
     def dst(c):
         a = topo.addr(c)
         return DstId(rid=a[0], pnc=a[1])
 
     def stop_over(rd, k):
-        return T["XR%d%d" % (rd, k // 4)][:, 1024 * (k % 4):1024 * (k % 4) + 1024]
+        return T["XR%d" % rd][:, 1024 * k:1024 * k + 1024]
 
+    def share(es, ks, k):
+        n = len(es) // len(ks)
+        return sum(1 << e for e in es[n * ks.index(k):n * ks.index(k) + n])
+
+    def others(c):
+        mate = [o for o in cores if topo.mates(topo.chip(o), topo.chip(c)) and topo.die(o) == topo.die(c)][0]
+        near = [o for o in cores if o != c and topo.chip(o) == topo.chip(c)][0]
+        return mate, near, [o for o in cores if o not in (c, mate, near)][0]
+
+    def slot(receiver, owner):
+        return (T.rank_of(owner) - T.rank_of(receiver) - 1) % N
+
+    porter = {c: [h for h in topo.cores_of(c) if h not in cores and h != helper[c] and topo.die(h) == topo.die(c) and topo.may_write(h, others(c)[0])][0]
+              for c in cores}
     if rank is None:
         for c in cores:
+            if porter[c] == core:
+                mate, near, _ = others(c)
+                off = topo.engines(core, mate)
+                on = [e for e in topo.engines(core, near) if e not in off]
+                for rd in range(RO):
+                    g.wait_ge(T.sem["ah%d" % rd], len(on))
+                    g.remote_dma_fused([RemoteDMATransfer(dst_ids=[dst(o)], dma_engine_mask=sum(1 << e for e in es), remote_sem=T.sem["%s%d1" % (s, rd)],
+                                                          src=T[("XA", "XB")[rd % 2]][:, 2048:W],
+                                                          dst=T["XR%d" % rd][:, RW * slot(o, c) + 2048:RW * slot(o, c) + W])
+                                        for o, es, s in ((mate, off, "am"), (near, on, "ap"))], local_sem=T.sem["back"])
+                g.wait_ge(T.sem["back"], (len(off) + len(on)) * RO)
             if helper[c] == core:
                 es = topo.engines(core, c)
                 for rd in range(RO):
-                    for k in range(len(FOLDED)):
-                        g.wait_ge(T.sem["fo%d%d" % (rd, k)], len(es))
-                        g.remote_dma_fused([RemoteDMATransfer(dst_ids=[dst(c)], dma_engine_mask=sum(1 << e for e in es), remote_sem=T.sem["fb%d%d" % (rd, k)],
-                                                              src=stop_over(rd, k), dst=T["MX%d" % k][:])], local_sem=T.sem["back"])
-                g.wait_ge(T.sem["back"], len(es) * RO * len(FOLDED))
+                    for ks in CALLS:
+                        g.wait_ge(T.sem["fo%d%d" % (rd, ks[0])], len(es))
+                        g.remote_dma_fused([RemoteDMATransfer(dst_ids=[dst(c)], dma_engine_mask=share(es, ks, k), remote_sem=T.sem["fb%d%d" % (rd, ks[0])],
+                                                              src=stop_over(rd, k), dst=T["MX%d" % k][:]) for k in ks], local_sem=T.sem["back"])
+                g.wait_ge(T.sem["back"], len(es) * RO * len(CALLS))
         return
     queue = {"V": g.vector, "A": g.scalar, "P": g.tensor, "G": g, "S": g.sync}
     qsem = {"V": "sV", "A": "sA", "P": "sT", "G": "sG"}
@@ -212,6 +258,7 @@ def rank_program(g, core, T, topo):
     ops = []
 
     loose, open_ = {}, {}
+    listed = []
     ahead = {}
 
     def record(q, reads, writes, cost, lag, issue):
@@ -299,10 +346,30 @@ def rank_program(g, core, T, topo):
                         ready.append((key[j], j))
             return start, done
 
+        found = [None, None]
+
+        def waits(start, done):
+            if found[0] is not start:
+                ends = {(ops[i][0], round(start[i] + ops[i][3], 6)): i for i in done}
+                j, pairs = max(done, key=lambda i: start[i] + ops[i][3] + ops[i][4]), []
+                while start[j] > 0:
+                    near_ = [i for i, gap in back[j] if start[i] + ops[i][3] + gap > start[j] - 1e-6]
+                    if not near_:
+                        near_ = [ends[(ops[j][0], round(start[j], 6))]]
+                        pairs.append((near_[0], j))
+                    j = near_[0]
+                found[:] = [start, pairs]
+            return found[1]
+
         prio = [0.0] * len(ops)
         for i in range(len(ops) - 1, -1, -1):
             prio[i] = ops[i][3] + ahead.get(i, 0.0) + max([prio[j] + between(i, j) for j in succ[i]], default=0.0)
         key, best = [-p for p in prio], None
+        for i0, i1 in listed:
+            base = min(key[i0:i1])
+            key[i0:i1] = [base + 1e-4 * (i - i0) for i in range(i0, i1)]
+        for i in range(len(ops) - 1, -1, -1):
+            key[i] = min([key[i]] + [key[j] - 1e-6 for j in succ[i]])
         rng = np.random.default_rng(1)
         for k in range(PASSES):
             start, done = lay(key, back, forth)
@@ -312,8 +379,15 @@ def rank_program(g, core, T, topo):
             if k < 3:
                 late, _ = lay([-(start[i] + ops[i][3]) for i in range(len(ops))], forth, back)
                 key = [-(late[i] + ops[i][3]) for i in range(len(ops))]
+            elif k % 4:
+                i, j = waits(*best[1:])[int(rng.integers(1 << 30)) % len(waits(*best[1:]))]
+                key = list(best[1])
+                if k % 2:
+                    key[i] = key[j] + 0.001
+                else:
+                    key[j] = key[i] - 0.001
             else:
-                t, w, was = rng.random() * best[0], (2.0, 5.0, 10.0)[k % 3], np.array(best[1])
+                t, w, was = rng.random() * best[0], (0.7, 2.0, 6.0)[k % 3], np.array(best[1])
                 some = (was > t) & (was < t + w) & (rng.random(len(ops)) < 0.3)
                 key = [float(x) for x in was + some * rng.normal(0, w / 5, len(ops))]
         place = {i: k for k, i in enumerate(best[2])}
@@ -334,9 +408,9 @@ def rank_program(g, core, T, topo):
         if kind == "iota":
             return 0.13 + 2 * n * CY
         if out[0] == "ind":
-            return 0.05 + 3.5 * n * CY
+            return 0.05 + 3.8 * n * CY
         if any(x[0] == "ind" for x in ins):
-            return 0.05 + 1.5 * n * CY
+            return (0.065 if q == "A" else 0.05) + 1.56 * n * CY
         if kind == "red":
             n = many(ins[0])
         if kind == "tt" and not any(SCRATCH[x[0]][0] == "psum" for x in ins):
@@ -400,6 +474,9 @@ def rank_program(g, core, T, topo):
     def scan(out, a, b, op0, op1, init=0.0):
         emit("V", "ts", [a, b, init], [out], lambda e: e.tensor_tensor_scan(ap(out), ap(a), ap(b), arg(init), op0, op1))
 
+    def reduce(out, a, op):
+        emit("V", "red", [a], [out], lambda e: e.tensor_reduce(ap(out), ap(a), AxisListType.X, op))
+
     def mm(out, l, r, start=True, stop=True):
         emit("P", "mm", [l, r], [out], lambda e: e.matmul(ap(out), ap(l), ap(r), start, stop))
 
@@ -433,6 +510,9 @@ def rank_program(g, core, T, topo):
         else:
             emit("G", "iota", [], [out], lambda e: e.iota(ap(out), pattern, base, cm, allow_small_or_imprecise_dtypes=True))
 
+    def where(out, a, pattern, op, base, cm):
+        emit("G", "iota", [a], [out], lambda e: e.affine_select(ap(out), ap(a), pattern, op, 0.0, base, cm))
+
     def ez(n, a):
         return v(n, 15 - a, 143 - a)
 
@@ -441,9 +521,9 @@ def rank_program(g, core, T, topo):
 
     AND, SHR = OP.bitwise_and, OP.logical_shift_right
     wtq = v("WT", 0, 1)
-    for k, n in enumerate(("XA", "XC")):
-        for lo, hi in PIECES:
-            dma("S", ap(v(n, lo, hi)), T.x0[:, lo:hi], [], [v(n, lo, hi)], 2.1 + 0.0007 * (W * k + hi))
+    for k, (n, pieces) in enumerate((("XA", PIECES), ("XC", AGAIN))):
+        for lo, hi in pieces:
+            dma("S", ap(v(n, lo, hi)), T.x0[:, lo:hi], [], [v(n, lo, hi)], 2.1 + 0.0007 * (W + hi - lo if k else hi))
     dma("A", ap(wtq), T.wt[:], [], [wtq])
     dma("A", ap(v("TH", 0, 2)), T.th[:], [], [v("TH", 0, 2)])
     iota(v("IC", 0, 1), [[1, 1]], 0, 1)
@@ -452,19 +532,7 @@ def rank_program(g, core, T, topo):
     iota(v("ONE"), [[0, 128]], 1, 0)
     iota(v("PAT"), [[0, 64], [1, 5]], 0, 0)
     ts(v("PAT"), v("PAT"), 1.0, OP.min)
-    iota(v("FDP"), [[0, 16]], 0, 0)
-    iota(v("K16"), [[16, 256]], 0, 0)
-    iota(v("MK", 0, 32), [[0, 2], [2, 16]], 1, 0)
-    iota(v("FQ", 4, 8), [[1, 4]], 0, 0)
-    iota(v("NW", 8, 14), [[32, 3], [8, 2]], 0, 0)
-    iota(v("TN", 8, 14), [[32, 6]], FREE, 2)
     iota(v("TT0"), [[32, 128]], -2048, 0)
-    iota(v("TT1"), [[2, 128]], 0, 0)
-    for h in range(2):
-        iota(v("NLIN", 96 * h, 96 * h + 96), [[32, 3], [1, 16], [16, 2]], 0, 0)
-        iota(v("GW", 136 * h + 128, 136 * h + 136), [[0, 8]], 1 << 20, 0)
-    for c in SEARCH_V:
-        iota(v("JK", 136 * c + 128, 136 * c + 136), [[0, 8]], -128, 0)
 
     def ic(k):
         return v("IC", k, k + 1)
@@ -473,20 +541,22 @@ def rank_program(g, core, T, topo):
         return v("FC", k, k + 1)
 
     J = v("JI", 0, 128)
-    for k, (s, m) in enumerate(((0, 15), (0, 112), (0, 3), (2, 3), (1, 7), (0, 1))):
+    for k, (s, m) in enumerate(((0, 15), (0, 112), (0, 3), (2, 3))):
         ts(ic(1 + k), ic(0), s, SHR, m, AND)
-    cp("V", v("FC", 0, 7), v("IC", 0, 7))
-    pf, p15, pg, p3, pq, ph, p1 = [fc(k) for k in range(7)]
-    first, second, keep, odd, hi_, lo_, pg2 = [fc(k) for k in range(8, 15)]
+    cp("V", v("FC", 0, 5), v("IC", 0, 5))
+    pf, p15, pg, p3, pq = [fc(k) for k in range(5)]
+    first, second, keep, odd, hi_, lo_ = [fc(k) for k in range(8, 14)]
     fill(v("EZ"), 0.0)
     fill(v("ED"), 0.0)
     fill(v("PAR", 2, 4), 0.0)
     cp("V", v("PAR", 0, 1), wtq)
     ts(v("EZ", 15, 143), J, pg, OP.is_equal)
-    times(v("EW"), v("EZ"), v("PAR", 0, 1))
+    ts(v("EW"), v("EZ"), wtq, OP.mult)
     ts(v("PAR", 1, 2), v("TH", 1, 2), 256.0, OP.mult)
     ts(v("IDN"), J, pf, OP.is_equal)
     times(v("NID"), v("IDN"), -1.0)
+    times(v("NF"), v("IDN"), -FAR)
+    times(v("NF2"), v("IDN"), -2048 * FAR)
     times(v("EF"), v("EZ"), FAR)
     times(v("EF2"), v("EZ"), 2 * FAR)
     times(v("EFN"), v("EZ"), -FAR)
@@ -505,7 +575,7 @@ def rank_program(g, core, T, topo):
     ts(lo_, ic(9), -1.0, OP.add, second, OP.mult)
     ts(hi_, hi_, lo_, OP.add, -FAR, OP.mult)
     times(v("BL"), v("BB"), hi_)
-    for a in range(16):
+    for a in range(NSEL, 16):
         times(sel(a), v("BB"), v("MASK", a, a + 1))
     ts(v("KK", 0, 1280, 5), v("QI"), pg, OP.subtract, 4 * RANK, OP.add)
     ts(v("QF", 0, 8), v("QI", 0, 8), pg, OP.subtract)
@@ -519,31 +589,36 @@ def rank_program(g, core, T, topo):
     tt(v("ED", 0, 143), v("EZ", 1, 144), v("EZ", 0, 143), OP.subtract)
     times(v("EDR"), v("ED"), 0.0625)
     ts(v("CD"), v("ONE"), 256.0, OP.mult, first, OP.subtract)
-    ts(v("BW", 0, 128), v("TT1"), first, OP.add)
-    cp("A", v("BW", 128, 136), v("CD", 0, 8))
-    ts(v("LT"), J, pf, OP.is_gt)
-    ts(v("UT"), J, pf, OP.is_lt)
-    tt(v("LT"), v("LT"), v("BB"), OP.mult)
-    tt(v("UT"), v("UT"), v("BB"), OP.mult)
     for q in range(4):
         ts(fc(16 + q), pq, float(q), OP.is_equal, -4.0, OP.mult)
         times(v("DM", 128 * q, 128 * q + 128), v("IDN"), fc(16 + q))
-    ts(ph, p1, 16.0, OP.mult, ph, OP.add)
-    ts(v("NW", 0, 6), v("NW", 8, 14), ph, OP.add)
-    ts(v("NWH", 0, 6), v("NW", 8, 14), ph, OP.add, 0.5, OP.add)
-    ts(pg2, pg, 2.0, OP.mult)
-    ts(v("TN", 0, 6), v("TN", 8, 14), pg2, OP.subtract)
-    times(v("FQ", 0, 4), v("FQ", 4, 8), 0.25)
     ts(v("RS"), v("J15", 0, 96), 0.0, OP.is_equal, 4 * RANK, OP.mult)
 
-    mine = topo.chip(core)
-    mate = [c for c in cores if topo.mates(topo.chip(c), mine) and topo.die(c) == topo.die(core)][0]
-    near = [c for c in cores if c != core and topo.chip(c) == mine][0]
-    diag = [c for c in cores if c not in (core, mate, near)][0]
+    def later():
+        where(v("UT"), v("BB"), [[-1, 128]], OP.is_gt, 0, 1)
+        where(v("LT"), v("BB"), [[1, 128]], OP.is_gt, 0, -1)
+        iota(v("TT1"), [[2, 128]], 0, 0)
+        for h in range(2):
+            iota(v("NLIN", 96 * h, 96 * h + 96), [[1, 16], [16, 2], [32, 3]], 0, 0)
+            iota(v("GW", 136 * h + 128, 136 * h + 136), [[0, 8]], 1 << 20, 0)
+        for c in SEARCH_V:
+            iota(v("JK", 136 * c + 128, 136 * c + 136), [[0, 8]], -128, 0)
+        iota(v("NQ", 8, 14), [[16, 2], [32, 3]], 0, 0)
+        iota(v("OF", 0, 6), [[0, 2], [RW, 3]], 1, 0)
+        iota(v("FQ", 4, 8), [[1, 4]], 0, 0)
+        iota(v("MK"), [[0, 6], [2, 16]], 1, 0)
+        iota(v("K16"), [[16, 256]], 0, 0)
+        ts(v("BW", 0, 128), v("TT1"), first, OP.add)
+        cp("A", v("BW", 128, 136), v("CD", 0, 8))
+        tt(v("VM", 0, 96), v("NLIN", 0, 96), v("MASK", 0, 96), OP.mult)
+        scan(v("ZV", 0, 96), v("KEEP", 0, 96), v("VM", 0, 96), OP.mult, OP.add)
+        cp("A", v("NW", 0, 6), v("ZV", 15, 96, 16))
+        ts(v("NWH", 0, 6), v("ZV", 15, 96, 16), 0.5, OP.add)
+        ts(v("NQ", 0, 6), v("NQ", 8, 14), p15, OP.add)
+        ts(v("TN", 0, 6), v("NQ", 0, 6), 2.0, OP.mult, float(FREE), OP.add)
+        times(v("FQ", 0, 4), v("FQ", 4, 8), 0.25)
 
-    def slot(receiver, owner):
-        return (T.rank_of(owner) - T.rank_of(receiver) - 1) % N
-
+    mate, near, diag = others(core)
     off = topo.engines(core, mate)
     both = topo.engines(core, near)
     on = [e for e in both if e not in off]
@@ -572,54 +647,68 @@ def rank_program(g, core, T, topo):
         record(None, [like], [v(name, lo, hi), landed[-1]], 0.0, 2.0, issue)
 
     def send_params():
-        call = remote([(c, ap(v("PAR")), T["PR%d" % slot(c, core)][:], [es], "par")
-                       for c, es in ((near, on[0]), (mate, off[0]), (diag, off[1]))], "lpar", [v("PAR")])
+        n = len(off) // 2
+        call = remote([(c, ap(v("PAR")), T["PR%d" % slot(c, core)][:], es, "par")
+                       for c, es in ((near, on), (mate, off[:n]), (diag, off[n:]))], "lpar", [v("PAR")])
         for d in range(3):
-            arrives("PR%d" % d, 0, 4, "par", 3, call)
+            arrives("PR%d" % d, 0, 4, "par", len(both), call)
 
     def halves():
         return [(h, 2048 * h, 2048 * h + 2048) for h in range(2)]
 
     def broadcast(rd, x):
+        a, b = v(x, 0, 2048), v(x, 2048, W)
+        call = remote([(mate, ap(a), ap(v("XR%d%d" % (rd, slot(mate, core)), 0, 2048)), off, "am%d0" % rd),
+                       (porter[core], ap(b), ap(b), on, "ah%d" % rd)], "lx%d0" % rd, [a, b])
+        remote([(near, ap(a), ap(v("XR%d%d" % (rd, slot(near, core)), 0, 2048)), on, "ap%d0" % rd)], "lx%d1" % rd, [a])
         for h, lo, hi in halves():
-            src = v(x, lo, hi)
-            call = remote([(mate, ap(src), T["XR%d%d" % (rd, slot(mate, core))][:, lo:hi], off, "am%d%d" % (rd, h)),
-                           (near, ap(src), T["XR%d%d" % (rd, slot(near, core))][:, lo:hi], on, "ap%d%d" % (rd, h))], "lx%d%d" % (rd, h),
-                          [src])
             arrives("XR%d%d" % (rd, slot(core, mate)), lo, hi, "am%d%d" % (rd, h), len(off), call)
             arrives("XR%d%d" % (rd, slot(core, near)), lo, hi, "ap%d%d" % (rd, h), len(on), call)
 
     def hand_on(rd):
         for h, lo, hi in halves():
             src = v("XR%d%d" % (rd, slot(core, mate)), lo, hi)
-            call = remote([(near, ap(src), T["XR%d%d" % (rd, slot(near, mate))][:, lo:hi], both, "aq%d%d" % (rd, h))], "lf%d%d" % (rd, h), [src])
+            call = remote([(near, ap(src), ap(v("XR%d%d" % (rd, slot(near, mate)), lo, hi)), both, "aq%d%d" % (rd, h))], "lf%d%d" % (rd, h), [src])
             arrives("XR%d%d" % (rd, slot(core, diag)), lo, hi, "aq%d%d" % (rd, h), len(both), call)
 
-    def fold(rd, k, a, b):
-        local, es = "fl%d%d" % (rd, k), topo.engines(core, helper[core])
+    def fold(rd, ks, x):
+        local, es = "fl%d%d" % (rd, ks[0]), topo.engines(core, helper[core])
+        srcs = {k: [v("GA%d" % k), v(x, 1024 * FOLDED[k][1], 1024 * FOLDED[k][1] + 1024)] for k in ks}
+        reads = [s for k in ks for s in srcs[k]]
 
         def issue():
-            order("G", [a, b], [])
+            order("G", reads, [])
             count[local] = len(es)
-            g.remote_dma_fused([RemoteDMATransfer(dst_ids=[dst(helper[core])], dma_engine_mask=sum(1 << e for e in es), remote_sem=T.sem["fo%d%d" % (rd, k)],
-                                                  srcs=[ap(a), ap(b)], dsts=[stop_over(rd, k)], alu_op=2)], local_sem=T.sem[local])
+            g.remote_dma_fused([RemoteDMATransfer(dst_ids=[dst(helper[core])], dma_engine_mask=share(es, ks, k), remote_sem=T.sem["fo%d%d" % (rd, ks[0])],
+                                                  srcs=[ap(s) for s in srcs[k]], dsts=[stop_over(rd, k)], alu_op=2) for k in ks], local_sem=T.sem[local])
             snap[(local, len(es))] = dict(known["G"])
-            note("Gremote", [a, b], [], local, len(es))
+            note("Gremote", reads, [], local, len(es))
         sent[0] += 1
-        record("G", [a, b], [fc(31 + sent[0])], 1.0, TRIP - 3.0, issue)
-        arrives("MX%d" % k, 0, 1024, "fb%d%d" % (rd, k), len(es), fc(31 + sent[0]))
+        record("G", reads, [fc(31 + sent[0])], 1.0, TRIP - 3.0, issue)
+        for k in ks:
+            arrives("MX%d" % k, 0, 1024, "fb%d%d" % (rd, ks[0]), len(es), fc(31 + sent[0]))
 
+    for a in range(2):
+        where(sel(a), v("ONE"), [[-16, 8], [0, 16]], OP.is_equal, -a, 1)
     send_params()
     for rd in range(RO):
         X, Xn = ("XA", "XB") if rd % 2 == 0 else ("XB", "XA")
         XR = ["XR%d%d" % (rd, d) for d in range(3)]
-        if rd > 0:
-            for lo, hi in PIECES:
-                x, y = v(X, lo, hi), v("XC", lo, hi)
-                dma("S", ap(y), ap(x), [x], [y], 2.1 + 0.0007 * hi)
+
+        def again(q):
+            if rd > 0 or (1024 * q, 1024 * q + 1024) not in AGAIN:
+                where(v("XC", 1024 * q, 1024 * q + 1024), v(X, 1024 * q, 1024 * q + 1024), [[0, 1024]], OP.is_ge, 0, 0)
+            if rd == 0 and q == 3:
+                for a in range(2, NSEL):
+                    where(sel(a), v("ONE"), [[-16, 8], [0, 16]], OP.is_equal, -a, 1)
+
+        again(1)
+        again(2)
 
         def sends():
             broadcast(rd, X)
+            if rd == 0:
+                later()
             hand_on(rd)
             iota(v("WA", 0, 1024), [[0, 1024]], 0, 0)
             iota(v("WB", 0, 1040), [[0, 1040]], 0, 0)
@@ -635,68 +724,107 @@ def rank_program(g, core, T, topo):
 
         def looks(s):
             lo, hi = SEGS[s]
-            w, b = hi - lo, s % 2
-            group([(pb(b, 0, w), ez("EW", a), v(X, 16 * lo + a, 16 * hi, 16)) for a in range(16)])
-            u, h, h1, u2 = v("UU", lo, hi), v("HI", lo, hi), pb(b, w, 2 * w), pb(b, 2 * w, 3 * w)
-            cp("V", v("UI", lo, hi), pb(b, 0, w))
-            ts(h, v("UI", lo, hi), 5, SHR, 127, AND)
-            ts(u, v("UI", lo, hi), W - 1, AND)
-            ts(h1, h, 1.0, OP.add)
-            ts(u2, u, 2.0, OP.mult, RANK, OP.add)
+            w, b = hi - lo, HASH[s]
+            u, h, h1, u2 = v("UU", lo, hi), v("HI", lo, hi), pb(b, w, 2 * w), v("U2", lo, hi) if s in BY_SCALAR else pb(b, 0, w)
             keys = [v("KK", 5 * lo + 4 - m, 5 * hi, 5) for m in range(4)]
-            tt(keys[0], h1, u, OP.mult)
-            for m in range(1, 4):
-                tt(keys[m], u2, keys[m - 1], OP.add)
+            calls = [lambda: cp("V", v("UI", lo, hi), pb(b, 0, w)),
+                     lambda: ts(h, v("UI", lo, hi), 5, SHR, 127, AND),
+                     lambda: ts(u, v("UI", lo, hi), W - 1, AND),
+                     lambda: ts(h1, h, 1.0, OP.add),
+                     lambda: act(u2, u, AF.Copy, bias=RANK, scale=2.0) if s in BY_SCALAR else ts(u2, u, 2.0, OP.mult, RANK, OP.add),
+                     lambda: tt(keys[0], h1, u, OP.mult)]
             for m in range(4):
-                ts(part("CC", s, m, m + 1), keys[m], W - 1, AND)
-            for m0, m1 in ((0, 1), (1, 2), (2, 4)) if s == 0 else ((0, 4),):
-                cp("V", part("CL", s, m0, m1), part("CC", s, m0, m1))
+                calls.append(lambda m=m: ts(part("CC", s, m, m + 1), keys[m], W - 1, AND))
+                if m < 3:
+                    calls.append(lambda m=m: tt(keys[m + 1], u2, keys[m], OP.add))
+                calls += [lambda m0=m0, m1=m1: cp("V", part("CL", s, m0, m1), part("CC", s, m0, m1)) for m0, m1 in LISTS[s] if m1 == m + 1]
+            return calls
 
-        dn, an = [0], [0]
+        dn, rest = [0], {}
 
-        def unit(m, q):
+        def sums(m, q, *parts):
+            out = pb(2 + q, 4 - m, 320, 5)
+            for e, n in parts:
+                add_to((rd, q), [(out, ez(e, a), v(n, a, 1024, 16)) for a in range(16)])
+
+        def gather(m, q):
             s = seg(q)
             win, x = ind(v(X, 0, W), part("CL", s, m, m + 1, 64 * q, 64 * q + 64)), (1024 * q, 1024 * q + 1024)
             if (m, q) in FOLDED:
                 k = FOLDED.index((m, q))
-                cp("A", v("GA%d" % k), win)
-                fold(rd, k, v("GA%d" % k), v(X, *x))
-                sums = [("EFN", X, x[0]), ("EFN", "GA%d" % k, 0), ("EF2", "MX%d" % k, 0)]
+                cp("V" if (m, q) in BY_VECTOR else "A", v("GA%d" % k), win)
+                for ks in CALLS:
+                    if k == ks[-1]:
+                        fold(rd, ks, X)
+                if k == len(FOLDED) - 1:
+                    again(3)
+                out = pb(2 + q, 4 - m, 320, 5)
+                add_to((rd, q), [(out, v("NF"), v("SBH", 64 * q, 64 * q + 64)), (out, v("NF2"), v("ONE", 0, 64))])
+                sums(m, q, ("EFN", "GA%d" % k))
+                rest[m, q] = lambda: sums(m, q, ("EF2", "MX%d" % k))
+            elif (m, q) in ON_SCALAR:
+                b = "GS%d" % ON_SCALAR.index((m, q))
+                for k in range(2):
+                    mm(pb(6 + k), v("NID"), v(X, x[0] + 512 * k, x[0] + 512 * k + 512), True, False)
+                cp("A", v(b), win)
+                for k in range(2):
+                    mm(pb(6 + k), v("IDN"), v(b, 512 * k, 512 * k + 512), False, True)
+                rest[m, q] = lambda: (act(v(b), v("PD"), AF.Abs), sums(m, q, ("EF", b)))
             else:
                 c = "DD%d" % (dn[0] % NDD)
                 dn[0] += 1
+                if (m, q) in HALVED:
+                    for h in range(2):
+                        d, o = v(c, 512 * h, 512 * h + 512), 64 * q + 32 * h
+                        tt(d, ind(v(X, 0, W), part("CL", s, m, m + 1, o, o + 32)), v("XC", 16 * o, 16 * o + 512), OP.subtract)
+                        act(d, d, AF.Abs)
+                        out = pb(2 + q, 4 - m + 160 * h, 160 * h + 160, 5)
+                        add_to((rd, q), [(out, ez("EF", a), v(c, 512 * h + a, 512 * h + 512, 16)) for a in range(16)])
+                    rest[m, q] = lambda: None
+                    return
                 tt(v(c), win, v("XC", *x), OP.subtract)
-                act(v(c), v(c), AF.Abs)
-                sums = [("EF", c, 0)]
-            out = pb(2 + q, 4 - m, 320, 5)
-            for e, n, o in sums:
-                add_to((rd, q), [(out, ez(e, a), v(n, o + a, o + 1024, 16)) for a in range(16)])
+                if (m, q) in ON_VECTOR:
+                    sums(m, q, ("EFN", c))
+                    rest[m, q] = lambda: (ts(v("GA0"), v(c), 0.0, OP.max), sums(m, q, ("EF2", "GA0")))
+                else:
+                    rest[m, q] = lambda: (act(v(c), v(c), AF.Abs), sums(m, q, ("EF", c)))
 
         def nearest(q):
-            mm(pb(2 + q, 0, 320), v("BL"), v("PAT"), True, False)
-            for m in range(4):
-                unit(m, q)
+            o = (64 * q, 64 * q + 64)
             scan(v("RUN", 320 * q, 320 * q + 320), pb(2 + q, 0, 320), v("KK", 320 * q, 320 * q + 320), OP.min, OP.max)
-
-        def spread(q0, q1):
-            o = (64 * q0, 64 * q1)
-            ts(v("KI", *o), v("RUN", 320 * q0 + 4, 320 * q1, 5), 1.0, OP.add)
+            ts(v("KI", *o), v("RUN", 320 * q + 4, 320 * q + 320, 5), 1.0, OP.add)
             ts(v("NXI", *o), v("KI", *o), W - 1, AND)
             ts(v("NXH", *o), v("NXI", *o), -2048.0, OP.add)
             cp("V", v("NXL", *o), v("NXI", *o))
-            for q in range(q0, q1):
-                banks = (0, 1) if q % 2 else (6, 7)
-                for b in range(2):
-                    each([(pb(banks[b], a // 2, 512, 8), sel(a), v("NXH", 64 * q, 64 * q + 64)) for a in range(b, 16, 2)])
-                    cp(COPIES[2 * q + b], v("NX1", 1024 * q + b, 1024 * q + 1024, 2), pb(banks[b]))
-                    ahead[len(ops) - 1] = EARLY[q]
+            for b in range(2):
+                each([(pb(SPREAD[q][b], a // 2, 512, 8), sel(a), v("NXH", *o)) for a in range(b, 16, 2)])
 
-        for s in range(len(SEGS)):
-            looks(s)
-        for q0, q1 in SPREADS:
-            for q in range(q0, q1):
-                nearest(q)
-            spread(q0, q1)
+        def spread(q):
+            for b in range(2):
+                cp(COPIES[2 * q + b], v("NX1", 1024 * q + b, 1024 * q + 1024, 2), pb(SPREAD[q][b]))
+
+        def own(lo, hi):
+            group([(pb(6, lo, hi), ez("EZ", a), v(X, 16 * lo + a, 16 * hi, 16)) for a in range(16)])
+            act(v("SBH", lo, hi), pb(6, lo, hi), AF.Copy, bias=-2048.0)
+
+        i0 = len(ops)
+        for s, (lo, hi) in enumerate(SEGS):
+            group([(pb(HASH[s], 0, hi - lo), ez("EW", a), v(X, 16 * lo + a, 16 * hi, 16)) for a in range(16)])
+        for q in range(4):
+            mm(pb(2 + q, 0, 320), v("BL"), v("PAT"), True, False)
+        for lo, hi in OWN:
+            own(lo, hi)
+        calls = [looks(s) for s in range(len(SEGS))]
+        for word in ORDER.split():
+            what, n = word[0], [int(x) for x in word[1:]]
+            if what in "abc":
+                for _ in range(int(word[1:])):
+                    calls["abc".index(what)].pop(0)()
+            elif what == "r":
+                rest[tuple(n)]()
+            else:
+                {"g": gather, "n": nearest, "s": spread}[what](*n)
+        listed.append((i0, len(ops)))
         sends()
         cp("V", v("NX2", 0, 2048), ind(v("NX1"), v("NXL", 0, 128)))
         cp("A", v("NX2", 2048, 4096), ind(v("NX1"), v("NXL", 128, 256)))
@@ -724,6 +852,7 @@ def rank_program(g, core, T, topo):
                 else:
                     ts(ne, d, 4096.0, OP.not_equal)
                 tt(v("F%d" % h, lo, hi), d, ne, OP.min)
+                ahead[len(ops) - 1] = 0.0 if h else SOON[2]
 
         steps[0], steps[1] = 16, 31
         for h in range(2):
@@ -739,7 +868,8 @@ def rank_program(g, core, T, topo):
                     scan(v(z, 16 * lo, 16 * hi), v("KEEP", 0, 16 * (hi - lo)), some, OP.mult, OP.add)
                     ts(v("LE", 8 * i + 8 + lo, 8 * i + 8 + hi), v(z, 16 * lo + 15, 16 * hi, 16), 2048.0, OP.add)
             else:
-                tt(v("RL"), ind(v("NX1"), le), v("MASK", 0, 128), OP.mult)
+                for lo, hi in CHAINS:
+                    tt(v("RL", 16 * lo, 16 * hi), ind(v("NX1"), v("LE", 8 * i + lo, 8 * i + hi)), v("MASK", 0, 16 * (hi - lo)), OP.mult)
                 step(31, v("RL"), "ED")
                 scan(v("Z3"), v("KEEP", 0, 128), v("RL"), OP.mult, OP.add)
                 ts(v("LO", 120, 128), v("Z3", 15, 128, 16), 2048.0, OP.add)
@@ -753,6 +883,7 @@ def rank_program(g, core, T, topo):
                     o = pb(2 + e % 2, 0, 8 * n)
                     group([(o, ez("ER", a), v("RD", 128 * j + a, 128 * (j + n), 16)) for a in range(16)])
                     ts(v("LO", 8 * j, 8 * j + 8 * n), o, 2048.0, OP.add)
+                    ahead[len(ops) - 1] = SOON[e]
                     for k in range(j, j + n):
                         y0(2 * k + 1)
             if i < 15:
@@ -769,8 +900,7 @@ def rank_program(g, core, T, topo):
         for c in range(6):
             if c in SEARCH_V:
                 ts(v("JK", 136 * c, 136 * c + 128), v("END"), v("NW", c, c + 1), OP.is_le, 2.0, OP.mult)
-                o, i_ = v("ACC", c, c + 1), v("JK", 136 * c, 136 * c + 129)
-                emit("V", "red", [i_], [o], lambda e, o=o, i_=i_: e.tensor_reduce(ap(o), ap(i_), AxisListType.X, OP.add))
+                reduce(v("ACC", c, c + 1), v("JK", 136 * c, 136 * c + 129), OP.add)
             else:
                 act(v("JK", 136 * c, 136 * c + 128), v("END"), AF.Sign, bias=v("NWH", c, c + 1), scale=-1.0, total=v("ACC", c, c + 1))
         for h in range(2):
@@ -783,31 +913,28 @@ def rank_program(g, core, T, topo):
         group([(pb(6, 0, 96), v("BB"), x) for x in parts])
         ts(v("PL"), pb(6, 0, 96), -1.0, OP.add)
         ops[-1][1].extend(landed)
+        for c in range(6):
+            group([(pb(7, 16 * c, 16 * c + 16), v("BB"), (x[0], x[1] + c, x[2], 6)) for x in parts])
         for d in range(3):
-            for e in range(2):
-                group([(pb(7, 32 * d + 16 * e, 32 * d + 16 * e + 16), v("BB"), (x[0], x[1] + 32 * d + e, x[1] + 32 * d + 32, 2)) for x in parts])
-        for d in range(3):
-            ts(v("THR", 2 * d, 2 * d + 2), v("QF", 2 * d, 2 * d + 2), v("END", 127, 128), OP.is_lt, v("PR%d" % d, 1, 2), OP.mult)
+            ts(v("THR", d, 6, 3), v("NQ", d, 6, 3), v("END", 127, 128), OP.is_lt, v("PR%d" % d, 1, 2), OP.mult)
         cp("V", v("AR", 0, 768), ind(v("Y0"), v("PL", 0, 48)))
         cp("A", v("AR", 768, 1536), ind(v("Y0"), v("PL", 48, 96)))
         if rd == 0:
             for d in range(3):
                 times(v("WB%d" % d), v("BB"), v("PR%d" % d, 0, 1))
         for d in range(3):
-            o, i_ = v(XR[d], W, W + 4), v(XR[d], 0, 4)
+            o, i_ = v(XR[d], W, RW), v(XR[d], 0, RW - W)
             emit("A", "", [i_, v("PL")], [o], lambda e, o=o, i_=i_: e.activation(ap(o), ap(i_), AF.Copy))
-        for d in range(3):
-            mm(pb(0, 32 * d, 32 * d + 32), v("WB%d" % d), v("AR", 512 * d, 512 * d + 512, 16))
-        for d in range(3):
-            for e in range(2):
-                mm(pb(5, 32 * d + 16 * e, 16 + 32 * d + 16 * e), v("WB%d" % d), v("AR", 512 * d + 16 * e, 512 * d + 512, 32))
+        each([(pb(0, d, 96, 3), v("WB%d" % d), v("AR", 16 * d, 1536, 48)) for d in range(3)])
+        each([(pb(5, 16 * c, 16 * c + 16), v("WB%d" % (c % 3)), v("AR", 16 * c, 1536, 96)) for c in range(6)])
         cp("V", v("AI"), pb(0, 0, 96))
         ts(v("AH"), v("AI"), 5, SHR, 127, AND)
         ts(v("AU"), v("AI"), W - 1, AND)
         ts(pb(0, 96, 192), v("AH"), odd, OP.add)
         tt(v("AT"), pb(0, 96, 192), v("AU"), OP.mult)
         ts(v("AC"), v("AT"), W - 1, AND)
-        cp("V", v("TL"), v("AC"))
+        for d in range(3):
+            ts(v("TL", d, 96, 3), v("AC", d, 96, 3), float(RW * d), OP.add)
         cp("V", v("RI"), pb(7, 0, 96))
         for k, b in enumerate((7, 5)):
             o = (96 * k, 96 * k + 96)
@@ -823,26 +950,31 @@ def rank_program(g, core, T, topo):
         ts(v("RJ"), v("RI"), 3, AND)
         ts(v("VA"), v("RJ"), p3, OP.is_le)
         ts(v("VB"), v("RJ"), p3, OP.is_gt)
-        mm(pb(1), v("NID"), v("AR", 1024, 1536), True, False)
-        for d in (0, 2, 1):
-            o, win = v("AD", 512 * d, 512 * d + 512), ind(v(XR[d], 0, W), v("TL", 32 * d, 32 * d + 32))
-            if d == 2:
-                cp("A", v("GB"), win)
-                mm(pb(1), v("IDN"), v("GB"), False, True)
-                act(o, pb(1), AF.Abs)
+        ky = pb(2, 0, 96)
+        mm(ky, v("IDN"), v("MK"), True, False)
+        for k, (a0, a1) in enumerate(ASKED):
+            lo, hi = 96 * a0, 96 * a1
+            o, win = v("AD", lo, hi), ind(v("XR%d" % rd), v("TL", 6 * a0, 6 * a1))
+            sums = [("EX", "AD", 0)]
+            if k == 2:
+                mm(pb(1, 0, hi - lo), v("NID"), v("AR", lo, hi), True, False)
+                cp("A", v("GB", 0, hi - lo), win)
+                mm(pb(1, 0, hi - lo), v("IDN"), v("GB", 0, hi - lo), False, True)
+                act(o, pb(1, 0, hi - lo), AF.Abs)
             else:
-                tt(o, win, v("AR", 512 * d, 512 * d + 512), OP.subtract)
-                if d == 0:
+                tt(o, win, v("AR", lo, hi), OP.subtract)
+                if k == 0:
                     act(o, o, AF.Abs)
                 else:
-                    ts(v("DP", 0, 512), o, 0.0, OP.max)
-            ky = pb(2 + d, 0, 32)
-            sums = [("EXN", "AD", 512), ("EX2", "DP", 0)] if d == 1 else [("EX", "AD", 512 * d)]
-            group([(ky, v("IDN"), v("MK", 0, 32))] + [(ky, ez(e, a), v(x, o + 32 * a, o + 32 * a + 32)) for e, x, o in sums for a in range(16)])
-            scan(v("KM", 32 * d, 32 * d + 32), v("RS", 0, 32), ky, OP.add, OP.min)
-        km, fd = v("KM", 15, 96, 16), v("FDP", 5, 11)
+                    ts(v("DP", 0, hi - lo), o, 0.0, OP.max)
+                    sums = [("EXN", "AD", 0), ("EX2", "DP", -lo)]
+            for e, x, o in sums:
+                add_to((rd, "key"), [(ky, ez(e, a), v(x, o + 96 * a, o + 96 * a + 96)) for a in range(a0, a1)])
+        scan(v("KM"), v("RS"), ky, OP.add, OP.min)
+        km, fd = v("KM", 15, 96, 16), v("FD", 0, 6)
         tt(fd, km, v("THR", 0, 6), OP.is_lt)
-        group([(pb(5, 0, 6), v("LT"), fd)] + [(pb(5, 0, 6), v("BB"), v("FDP", 5 - k, 11 - k)) for k in range(1, 6)])
+        group([(pb(5, 0, 6), v("LT"), fd)] + [(pb(5, 3 * e + k, 3 * e + 3), v("BB"), v("FD", 3 * f, 3 * f + 3 - k))
+                                              for e in range(2) for f in range(2) for k in range(0 if e > f else 1, 3)])
         tt(v("QQ", 0, 6), fd, v("QT", 0, 6), OP.mult)
         tt(v("QQ", 0, 6), v("QQ", 0, 6), v("TN", 0, 6), OP.add)
         tt(v("SS", 0, 6), pb(5, 0, 6), v("QQ", 0, 6), OP.add)
@@ -852,12 +984,11 @@ def rank_program(g, core, T, topo):
         tt(v("S6", 0, 6), v("S6", 0, 6), v("H6", 0, 6), OP.add)
         tt(v("T6", 0, 6), v("S6", 0, 6), v("U6", 0, 6), OP.mult)
         ts(v("C6", 0, 6), v("T6", 0, 6), W - 1, AND)
-        ts(v("CQ", 0, 6), v("C6", 0, 6), 1.0, OP.add)
+        tt(v("CQ", 0, 6), v("C6", 0, 6), v("OF", 0, 6), OP.add)
         for c in range(6):
             act(v("FIF", 4 * c, 4 * c + 4), v("FQ", 4, 8), AF.Identity, bias=v("CQ", c, c + 1))
         cp("V", v("FL", 0, 24), v("FIF", 0, 24))
-        for d in range(3):
-            cp("A", v("FB", 128 * d, 128 * d + 128), ind(v(XR[d], 0, W + 4), v("FL", 8 * d, 8 * d + 8)))
+        cp("A", v("FB"), ind(v("XR%d" % rd), v("FL", 0, 24)))
         tt(v("PQ", 0, 6), v("SS", 0, 6), v("R4", 0, 6), OP.add)
         for c in range(6):
             act(v("FPF", 4 * c, 4 * c + 4), v("FQ", 0, 4), AF.Identity, bias=v("PQ", c, c + 1))
@@ -870,10 +1001,17 @@ def rank_program(g, core, T, topo):
             o = pb(6 + s, 0, hi - lo)
             group([(o, v("IDN"), v("K16", lo, hi))] + [(o, v("DM", 128 * q, 128 * q + 128), v("ZS", 4 * lo + q, 4 * hi, 4)) for q in range(4)])
             ts(v("SRL", lo, hi), o, p15, OP.add)
-            cp("AV"[s], v(Xn, 16 * lo, 16 * hi), ind(v("Y0"), v("SRL", lo, hi)))
-        cp("V", ind(v(Xn), v("FP", 0, 24)), v("FB"))
-    Xn = "XA" if RO % 2 == 0 else "XB"
-    dma("S", T.y[:], ap(v(Xn, 0, W)), [v(Xn, 0, W)], [], 5.0)
+            if rd < RO - 1:
+                cp("AV"[s], v(Xn, 16 * lo, 16 * hi), ind(v("Y0"), v("SRL", lo, hi)))
+        if rd < RO - 1:
+            cp("V", ind(v(Xn), v("FP", 0, 24)), v("FB"))
+            continue
+        for x, pieces in zip((Xn, X), LAST):
+            for q, lo, hi in pieces:
+                cp(q, v(x, 16 * lo, 16 * hi), ind(v("Y0"), v("SRL", lo, hi)))
+            cp("V", ind(v(x), v("FP", 0, 24)), v("FB"))
+            lo, hi = 16 * pieces[0][1], 16 * pieces[-1][2]
+            dma("S", T.y[:, lo:hi], ap(v(x, lo, hi)), [v(x, lo, hi)], [], 2.1 + 0.0008 * (hi - lo))
     if not PLAN:
         PLAN.extend(plan())
     for i in PLAN:

import numpy as np
from concourse.bass import DstId, RemoteDMATransfer
from concourse.mybir import dt, AluOpType as OP, AxisListType, ActivationFunctionType as AF

W = 4096
RO = 2
RW = W + 8
ASKED = ((0, 5), (5, 11), (11, 16))
FREE = 1120
XW = 5632
F32, BF, I32, U16, F16 = "float32", "bfloat16", "int32", "uint16", "float16"
HASH = (0, 1, 7)
SEGS = [(0, 64), (64, 128), (128, 256)]
BY_VECTOR = ((3, 0),)
FOLDED = ((0, 0), (1, 0), (3, 0), (2, 0), (0, 2), (0, 3), (1, 3))
ORDER = "a9 g00 a3 g10 a5 b14 c9 g30 g20 c6 g02 g11 g03 g21 g13 g31 g01 g12 r11 r00 r10 g22 r01 r30 r21 r20 g32 r31 r02 n1 r12 n0 g23 r22 r03 g33 r32 r13 r23 n2 r33 n3 s1 s0 s2 s3"
NSEL = 6
CALLS = ((0,), (1,), (2, 3), (4,), (5,), (6,))
SPREAD = ((0, 1), (6, 7), (2, 3), (4, 5))
ON_SCALAR = ((0, 1),)
BY_SCALAR = ()
OWN = ((0, 64), (128, 256))
HALVED = ()
ON_VECTOR = ()
LISTS = (((0, 1), (1, 2), (2, 3), (3, 4)), ((0, 4),), ((0, 1), (1, 4)))
NDD = 9
TRIP = 9.0
PIECES = ((0, 1024), (1024, 2048), (2048, W))
AGAIN = ((2048, 3072),)
CHAINS = ((0, 4), (4, 8))
COPIES = "VAAAVAVA"
ODD = ((0, 4), (4, 4), (8, 4), (12, 3))
SOON = (9.0, 6.0, 3.0, 0.0)
SEARCH_V = (4, 5)
CUT = 128
LAST = ((("A", 0, 68), ("V", 68, 128)), (("A", 128, 222), ("V", 222, 256)))
RANK = float(1 << 20)
FAR = float(1 << 23)
PASSES = 5000
WAKE = 0.16
CY = 0.00083
PE = 0.0005

SCRATCH = {}
PLAN = []
PLACE = {}


def _buf(where, cols, dtype, *names):
    for n in names:
        SCRATCH[n] = (where, [128, cols], dtype)
        PLACE[n] = (n, 0, cols)


def _pack(cols, dtype, host, *names):
    SCRATCH[host] = ("sbuf", [128, cols * len(names)], dtype)
    for i, n in enumerate(names):
        PLACE[n] = (host, cols * i, cols)


_buf("sbuf", XW, BF, "XA", "XB")
_buf("sbuf", W, BF, "Y0", "XC")
for _r in range(RO):
    _pack(RW, BF, "XR%d" % _r, *["XR%d%d" % (_r, d) for d in range(3)])
    PLACE["XR%d" % _r] = ("XR%d" % _r, 0, 3 * RW)
_buf("sbuf", W, F32, "NX1", "NX2")
_buf("sbuf", 1024, BF, "ZS", *["GS%d" % k for k in range(len(ON_SCALAR))], *["%s%d" % (n, k) for n in ("GA", "MX") for k in range(len(FOLDED))])
for _k, _p in enumerate([("Y0", 1024 * k) for k in range(4)] + [("AR", 0), ("AD", 0), ("ZS", 0), ("WA", 0), ("WB", 0)]):
    PLACE["DD%d" % _k] = _p + (1024,)
_buf("sbuf", 1024, I32, "CC")
_buf("sbuf", 1280, I32, "KK")
_buf("sbuf", 1280, F32, "RUN")
_buf("sbuf", 1024, U16, "CL")
_pack(256, I32, "hI", "QI", "UI", "UU", "HI", "KI", "NXI")
_pack(256, U16, "hU", "NXL", "SRL")
_buf("sbuf", 256, F16, "NXH", "SBH")
_buf("sbuf", 256, BF, "K16")
_pack(192, I32, "gI", "JI", "J15", "JG")
_pack(192, F32, "gF", "MASK", "NLIN", "VM", "ZV")
_pack(192, BF, "gB", "KEEP", "CMP")
_pack(128, U16, "gU", "LE", "LO")
_buf("sbuf", 2048, F16, "RE", "RD")
_pack(128, F16, "zH", "Z0", "Z1", "Z2", "Z3", "RL")
_buf("sbuf", 144, BF, "EZ", "EW", "EX", "EF", "EN", "ED", "ER", "EDR", "EF2", "EFN", "EX2", "EXN")
_buf("sbuf", 128, BF, "BB", "IDN", "NID", "LT", "UT", "WB0", "WB1", "WB2", "BL", "ONE", "CD", "NE", "F0", "F1", "NF", "NF2")
_buf("sbuf", 2048, BF, "SEL")
_buf("sbuf", 512, BF, "DM", "GB")
_buf("sbuf", 768, BF, "DP")
_buf("sbuf", 128, F32, "END", "TT0", "TT1")
_buf("sbuf", 272, F32, "GW")
_buf("sbuf", 136, F32, "BW")
_buf("sbuf", 136 * 6, BF, "JK")
_buf("sbuf", 1408, BF, "WA")
_buf("sbuf", 1424, BF, "WB")
_buf("sbuf", 16, I32, "TH", "IC")
_buf("sbuf", 128, F32, "FC")
_buf("sbuf", 320, BF, "PAT")
_buf("sbuf", 16, BF, "WT", "FD")
_buf("sbuf", 4, F32, "PAR", "PR0", "PR1", "PR2")
_pack(32, F32, "sF", "QF", "NW", "NWH", "TN", "NQ", "FQ", "ACC", "THR", "OF", "QT", "QQ", "SS", "R4", "PQ", "FPF", "CQ", "FIF")
_pack(32, U16, "sU", "JL", "FL", "FP", "SL")
_pack(32, I32, "sI", "WI", "U6", "H6", "Q6", "R6", "K6", "S6", "T6", "C6")
_pack(96, F32, "uF", "RS", "KM")
_pack(96, I32, "uI", "AI", "AU", "AH", "AT", "AC", "RI", "RJ")
_pack(96, U16, "uU", "TL", "PL")
_pack(96, BF, "uB", "BG", "MK", "VA", "VB")
_buf("sbuf", 1536, BF, "AR", "AD")
_buf("sbuf", 384, BF, "FB")
_buf("psum", 1024, F32, "PA", "PB", "PC", "PD")

NDMA = 20
SEMAPHORES = ["sV", "sA", "sT", "sG", "par", "lpar"] + ["d%d" % i for i in range(NDMA)]
SEMAPHORES += ["%s%d%d" % (k, r, h) for k in ("am", "ap", "aq", "lx", "lf") for r in range(RO) for h in range(2)]
SEMAPHORES += ["%s%d%d" % (n, r, k) for n in ("fo", "fb", "fl") for r in range(RO) for k in range(len(FOLDED))] + ["back"]
SEMAPHORES += ["ah%d" % r for r in range(RO)]


def rank_program(g, core, T, topo):
    rank = T.rank_of(core)
    cores = list(T.cores)
    N = len(cores)
    helper = {c: [h for h in topo.cores_of(c) if h not in cores and topo.die(h) == topo.die(c) and not all(topo.may_write(h, o) for o in cores)][0]
              for c in cores}

    def dst(c):
        a = topo.addr(c)
        return DstId(rid=a[0], pnc=a[1])

    def stop_over(rd, k):
        return T["XR%d" % rd][:, 1024 * k:1024 * k + 1024]

    def share(es, ks, k):
        n = len(es) // len(ks)
        return sum(1 << e for e in es[n * ks.index(k):n * ks.index(k) + n])

    def others(c):
        mate = [o for o in cores if topo.mates(topo.chip(o), topo.chip(c)) and topo.die(o) == topo.die(c)][0]
        near = [o for o in cores if o != c and topo.chip(o) == topo.chip(c)][0]
        return mate, near, [o for o in cores if o not in (c, mate, near)][0]

    def slot(receiver, owner):
        return (T.rank_of(owner) - T.rank_of(receiver) - 1) % N

    porter = {c: [h for h in topo.cores_of(c) if h not in cores and h != helper[c] and topo.die(h) == topo.die(c) and topo.may_write(h, others(c)[0])][0]
              for c in cores}
    if rank is None:
        for c in cores:
            if porter[c] == core:
                mate, near, _ = others(c)
                off = topo.engines(core, mate)
                on = [e for e in topo.engines(core, near) if e not in off]
                for rd in range(RO):
                    g.wait_ge(T.sem["ah%d" % rd], len(on))
                    g.remote_dma_fused([RemoteDMATransfer(dst_ids=[dst(o)], dma_engine_mask=sum(1 << e for e in es), remote_sem=T.sem["%s%d1" % (s, rd)],
                                                          src=T[("XA", "XB")[rd % 2]][:, 2048:W],
                                                          dst=T["XR%d" % rd][:, RW * slot(o, c) + 2048:RW * slot(o, c) + W])
                                        for o, es, s in ((mate, off, "am"), (near, on, "ap"))], local_sem=T.sem["back"])
                g.wait_ge(T.sem["back"], (len(off) + len(on)) * RO)
            if helper[c] == core:
                es = topo.engines(core, c)
                for rd in range(RO):
                    for ks in CALLS:
                        g.wait_ge(T.sem["fo%d%d" % (rd, ks[0])], len(es))
                        g.remote_dma_fused([RemoteDMATransfer(dst_ids=[dst(c)], dma_engine_mask=share(es, ks, k), remote_sem=T.sem["fb%d%d" % (rd, ks[0])],
                                                              src=stop_over(rd, k), dst=T["MX%d" % k][:]) for k in ks], local_sem=T.sem["back"])
                g.wait_ge(T.sem["back"], len(es) * RO * len(CALLS))
        return
    queue = {"V": g.vector, "A": g.scalar, "P": g.tensor, "G": g, "S": g.sync}
    qsem = {"V": "sV", "A": "sA", "P": "sT", "G": "sG"}
    count = {}
    known = {q: {} for q in queue}
    snap = {}
    log = {}
    ndma, now = [0], [0]

    def v(name, lo=0, hi=None, st=1):
        host, base, cols = PLACE[name]
        return (host, base + lo, base + (cols if hi is None else hi), st)

    def pb(b, lo=0, hi=512, st=1):
        return v(("PA", "PB", "PC", "PD")[b // 2], 512 * (b % 2) + lo, 512 * (b % 2) + hi, st)

    def ap(x):
        n, lo, hi, st = x
        return T[n][:, lo:hi] if st == 1 else T[n][:, lo:hi:st]

    def arg(x):
        return ap(x) if isinstance(x, tuple) else x

    def ind(win, off):
        return ("ind", win, off)

    def opnd(x):
        if x[0] == "ind":
            return ap(x[1]).indirect(ap(x[2]))
        return ap(x)

    def hits(a, b):
        if a[1] <= b[0] or b[1] <= a[0]:
            return False
        if a[2] == b[2] and a[2] > 1 and (a[0] - b[0]) % a[2]:
            return False
        return True

    def inside(a, lo, hi, st):
        return a[0] >= lo and a[1] <= hi and (st == 1 or (a[2] == st and (a[0] - lo) % st == 0))

    def bank(x):
        n, lo, hi, st = x
        if SCRATCH[n][0] == "psum":
            return n, lo // 512 * 512, (hi + 511) // 512 * 512, 1
        return x

    def wait(q, sem, n):
        if known[q].get(sem, 0) >= n:
            return
        queue[q].wait_ge(T.sem[sem], n)
        known[q][sem] = n
        for k, c in snap.get((sem, n), {}).items():
            if known[q].get(k, 0) < c:
                known[q][k] = c

    def order(q, reads, writes):
        need = {}
        for lst, wr in ((reads, False), (writes, True)):
            for x in lst:
                n, lo, hi, st = bank(x)
                ps = SCRATCH[n][0] == "psum"
                for a in log.get(n, ()):
                    aq, aw = a[3], a[4]
                    if not hits((lo, hi, st), a):
                        continue
                    if aq == q and q in qsem:
                        if ps and q == "P":
                            continue
                        if not (aw or wr) or (ps and not hits(x[1:], a[7])):
                            continue
                    elif not (aw or wr or ps):
                        continue
                    if need.get(a[5], 0) < a[6]:
                        need[a[5]] = a[6]
        for sem in sorted(need, key=lambda s: -need[s]):
            wait(q, sem, need[sem])

    def note(q, reads, writes, sem, n):
        for lst, wr in ((reads, False), (writes, True)):
            for x in lst:
                nm, lo, hi, st = bank(x)
                l = log.setdefault(nm, [])
                if SCRATCH[nm][0] == "psum":
                    l[:] = [a for a in l if not (inside(a, lo, hi, st) and (a[3] != q or q == "P" or ((wr or not a[4]) and inside(a[7], *x[1:]))))]
                elif wr:
                    l[:] = [a for a in l if not inside(a, lo, hi, st)]
                else:
                    l[:] = [a for a in l if not (a[3] == q and not a[4] and a[0] >= lo and a[1] <= hi and a[2] == st and st == 1)]
                l.append((lo, hi, st, q, wr, sem, n, x[1:]))

    ops = []

    loose, open_ = {}, {}
    listed = []
    ahead = {}

    def record(q, reads, writes, cost, lag, issue):
        rd, wr = [], []
        for x in reads:
            if isinstance(x, tuple):
                rd += [x[1], x[2]] if x[0] == "ind" else [x]
        for x in writes:
            if x[0] == "ind":
                wr.append(x[1])
                rd.append(x[2])
            else:
                wr.append(x)
        ops.append((q, rd, wr, cost, lag, issue))

    def plan():
        seen, preds, last = {}, [], {}
        for i, (q, rd, wr, _, _, _) in enumerate(ops):
            ps = set()
            for lst, w in ((rd, False), (wr, True)):
                for x in lst:
                    n, lo, hi, st = bank(x)
                    psum = SCRATCH[n][0] == "psum"
                    for a in seen.get(n, ()):
                        if not hits((lo, hi, st), a) or (psum and i in loose and loose[i] == loose.get(a[3])):
                            continue
                        if psum and ops[a[3]][0] == q != "P":
                            if (a[4] or w) and hits(x[1:], a[5]):
                                ps.add(a[3])
                        elif a[4] or w or psum:
                            ps.add(a[3])
            if q in ("G", "S"):
                if q in last:
                    ps.add(last[q])
                last[q] = i
            for lst, w in ((rd, False), (wr, True)):
                for x in lst:
                    n, lo, hi, st = bank(x)
                    l = seen.setdefault(n, [])
                    if SCRATCH[n][0] == "psum":
                        if q == "P" and i not in loose:
                            l[:] = [a for a in l if not inside(a, lo, hi, st)]
                    elif w:
                        l[:] = [a for a in l if not inside(a, lo, hi, st)]
                    l.append((lo, hi, st, i, w, x[1:]))
            ps.discard(i)
            preds.append(ps)
        succ = [[] for _ in ops]
        for i, ps in enumerate(preds):
            for j in ps:
                succ[j].append(i)

        def between(i, j):
            return 0.0 if ops[i][0] == ops[j][0] and ops[i][0] in ("P", "G", "S") else WAKE + ops[i][4]

        forth = [[(j, between(i, j)) for j in succ[i]] for i in range(len(ops))]
        back = [[(j, between(j, i)) for j in preds[i]] for i in range(len(ops))]

        def lay(key, before, after):
            at, left, busy, start = [0.0] * len(ops), [len(p) for p in before], {}, [0.0] * len(ops)
            ready = [(key[i], i) for i in range(len(ops)) if not left[i]]
            done = []
            while ready:
                first = min(ready)
                ready.remove(first)
                i = first[1]
                q, c, t = ops[i][0], ops[i][3], at[i]
                if q is not None:
                    l = busy.setdefault(q, [])
                    k = len(l)
                    while k and l[k - 1][1] > t:
                        k -= 1
                    while k < len(l) and l[k][0] < t + c:
                        t = max(t, l[k][1])
                        k += 1
                    l.insert(k, (t, t + c))
                start[i] = t
                done.append(i)
                t += c
                for j, gap in after[i]:
                    if at[j] < t + gap:
                        at[j] = t + gap
                    left[j] -= 1
                    if not left[j]:
                        ready.append((key[j], j))
            return start, done

        found = [None, None]

        def waits(start, done):
            if found[0] is not start:
                ends = {(ops[i][0], round(start[i] + ops[i][3], 6)): i for i in done}
                j, pairs = max(done, key=lambda i: start[i] + ops[i][3] + ops[i][4]), []
                while start[j] > 0:
                    near_ = [i for i, gap in back[j] if start[i] + ops[i][3] + gap > start[j] - 1e-6]
                    if not near_:
                        near_ = [ends[(ops[j][0], round(start[j], 6))]]
                        pairs.append((near_[0], j))
                    j = near_[0]
                found[:] = [start, pairs]
            return found[1]

        prio = [0.0] * len(ops)
        for i in range(len(ops) - 1, -1, -1):
            prio[i] = ops[i][3] + ahead.get(i, 0.0) + max([prio[j] + between(i, j) for j in succ[i]], default=0.0)
        key, best = [-p for p in prio], None
        for i0, i1 in listed:
            base = min(key[i0:i1])
            key[i0:i1] = [base + 1e-4 * (i - i0) for i in range(i0, i1)]
        for i in range(len(ops) - 1, -1, -1):
            key[i] = min([key[i]] + [key[j] - 1e-6 for j in succ[i]])
        rng = np.random.default_rng(1)
        for k in range(PASSES):
            start, done = lay(key, back, forth)
            end = max(start[i] + ops[i][3] + ops[i][4] for i in done)
            if best is None or end <= best[0]:
                best = (end, start, done)
            if k < 3:
                late, _ = lay([-(start[i] + ops[i][3]) for i in range(len(ops))], forth, back)
                key = [-(late[i] + ops[i][3]) for i in range(len(ops))]
            elif k % 4:
                i, j = waits(*best[1:])[int(rng.integers(1 << 30)) % len(waits(*best[1:]))]
                key = list(best[1])
                if k % 2:
                    key[i] = key[j] + 0.001
                else:
                    key[j] = key[i] - 0.001
            else:
                t, w, was = rng.random() * best[0], (0.7, 2.0, 6.0)[k % 3], np.array(best[1])
                some = (was > t) & (was < t + w) & (rng.random(len(ops)) < 0.3)
                key = [float(x) for x in was + some * rng.normal(0, w / 5, len(ops))]
        place = {i: k for k, i in enumerate(best[2])}
        return sorted(best[2], key=lambda i: (best[1][i], place[i]))

    def many(x):
        if x[0] == "ind":
            return 16 * (x[2][2] - x[2][1])
        return (x[2] - x[1] + x[3] - 1) // x[3]

    def half(x):
        return SCRATCH[(x[1] if x[0] == "ind" else x)[0]][2] in (BF, U16, F16)

    def cost(q, kind, out, ins):
        n = many(out)
        if kind == "mm":
            return PE * max(64, many(ins[1])) * (4 if SCRATCH[ins[0][0]][2] == F32 else 1)
        if kind == "iota":
            return 0.13 + 2 * n * CY
        if out[0] == "ind":
            return 0.05 + 3.8 * n * CY
        if any(x[0] == "ind" for x in ins):
            return (0.065 if q == "A" else 0.05) + 1.56 * n * CY
        if kind == "red":
            n = many(ins[0])
        if kind == "tt" and not any(SCRATCH[x[0]][0] == "psum" for x in ins):
            n = 2 * n
        if kind == "ts" and all(half(x) for x in ins + [out] if many(x) > 1):
            n = n / 2
        return max(n, 64) * CY + (0.05 if q == "A" else 0.03)

    def emit(q, kind, reads, writes, fn):
        def issue():
            rd, wr = ops[now[0]][1:3]
            order(q, rd, wr)
            s = qsem[q]
            count[s] = count.get(s, 0) + 1
            fn(queue[q]).then_inc(T.sem[s], 1)
            snap[(s, count[s])] = dict(known[q])
            note(q, rd, wr, s, count[s])
        record(q, reads, writes, cost(q, kind, writes[0], [x for x in reads if isinstance(x, tuple)]), 0.0, issue)

    def dma(q, out, in_, reads, writes, lag=2.2):
        s = "d%d" % ndma[0]
        ndma[0] += 1

        def issue():
            order(q, reads, writes)
            count[s] = 16
            queue[q].dma_start(out, in_).then_inc(T.sem[s], 16)
            snap[(s, 16)] = dict(known[q])
            note(q + "dma", reads, writes, s, 16)
        record(q, reads, writes, 0.1, lag, issue)

    def tt(out, a, b, op):
        emit("V", "tt", [a, b], [out], lambda e: e.tensor_tensor(opnd(out), opnd(a), opnd(b), op))

    def ts(out, a, s1, op0, s2=None, op1=None):
        def f(e):
            if op1 is None:
                return e.tensor_scalar(ap(out), opnd(a), arg(s1), None, op0)
            return e.tensor_scalar(ap(out), opnd(a), arg(s1), arg(s2), op0, op1)
        emit("V", "ts", [a, s1, s2], [out], f)

    def cp(q, out, a):
        if q == "V":
            emit("V", "ts", [a], [out], lambda e: e.tensor_copy(opnd(out), opnd(a)))
        else:
            emit("A", "", [a], [out], lambda e: e.activation(ap(out), opnd(a), AF.Copy))

    def act(out, a, func, bias=0.0, scale=1.0, total=None):
        if total is None:
            emit("A", "", [a, bias, scale], [out], lambda e: e.activation(ap(out), opnd(a), func, bias=arg(bias), scale=arg(scale)))
        else:
            emit("A", "", [a, bias, scale], [out, total],
                 lambda e: e.activation(ap(out), opnd(a), func, bias=arg(bias), scale=arg(scale), accum_out=ap(total)))

    def times(out, a, s):
        act(out, a, AF.Copy, scale=s)

    def fill(out, c):
        emit("V", "ts", [], [out], lambda e: e.memset(ap(out), c))

    def scan(out, a, b, op0, op1, init=0.0):
        emit("V", "ts", [a, b, init], [out], lambda e: e.tensor_tensor_scan(ap(out), ap(a), ap(b), arg(init), op0, op1))

    def reduce(out, a, op):
        emit("V", "red", [a], [out], lambda e: e.tensor_reduce(ap(out), ap(a), AxisListType.X, op))

    def mm(out, l, r, start=True, stop=True):
        emit("P", "mm", [l, r], [out], lambda e: e.matmul(ap(out), ap(l), ap(r), start, stop))

    def mms(calls, flags):
        def f(e):
            for k, (out, l, r) in enumerate(calls):
                last = e.matmul(ap(out), ap(l), ap(r), *flags(k))
            return last
        emit("P", "mm", [x for c in calls for x in c[1:]], [calls[0][0]], f)
        ops[-1] = ops[-1][:3] + (sum(cost("P", "mm", out, [l, r]) for out, l, r in calls),) + ops[-1][4:]

    def group(calls):
        mms(calls, lambda k: (k == 0, k == len(calls) - 1))

    def each(calls):
        mms(calls, lambda k: (True, True))

    def add_to(name, calls):
        loose[len(ops)] = name
        open_[name] = open_.get(name, 0) + 1

        def flags(k):
            if k == len(calls) - 1:
                open_[name] -= 1
            return False, open_[name] == 0
        mms(calls, flags)

    def iota(out, pattern, base, cm):
        if SCRATCH[out[0]][2] == I32:
            emit("G", "iota", [], [out], lambda e: e.iota(ap(out), pattern, base, cm))
        else:
            emit("G", "iota", [], [out], lambda e: e.iota(ap(out), pattern, base, cm, allow_small_or_imprecise_dtypes=True))

    def where(out, a, pattern, op, base, cm):
        emit("G", "iota", [a], [out], lambda e: e.affine_select(ap(out), ap(a), pattern, op, 0.0, base, cm))

    def ez(n, a):
        return v(n, 15 - a, 143 - a)

    def sel(a):
        return v("SEL", 128 * a, 128 * a + 128)

    AND, SHR = OP.bitwise_and, OP.logical_shift_right
    wtq = v("WT", 0, 1)
    for k, (n, pieces) in enumerate((("XA", PIECES), ("XC", AGAIN))):
        for lo, hi in pieces:
            dma("S", ap(v(n, lo, hi)), T.x0[:, lo:hi], [], [v(n, lo, hi)], 2.1 + 0.0007 * (W + hi - lo if k else hi))
    dma("A", ap(wtq), T.wt[:], [], [wtq])
    dma("A", ap(v("TH", 0, 2)), T.th[:], [], [v("TH", 0, 2)])
    iota(v("IC", 0, 1), [[1, 1]], 0, 1)
    iota(v("JI"), [[1, 192]], 0, 0)
    iota(v("QI"), [[16, 256]], 0, 1)
    iota(v("ONE"), [[0, 128]], 1, 0)
    iota(v("PAT"), [[0, 64], [1, 5]], 0, 0)
    ts(v("PAT"), v("PAT"), 1.0, OP.min)
    iota(v("TT0"), [[32, 128]], -2048, 0)

    def ic(k):
        return v("IC", k, k + 1)

    def fc(k):
        return v("FC", k, k + 1)

    J = v("JI", 0, 128)
    for k, (s, m) in enumerate(((0, 15), (0, 112), (0, 3), (2, 3))):
        ts(ic(1 + k), ic(0), s, SHR, m, AND)
    cp("V", v("FC", 0, 5), v("IC", 0, 5))
    pf, p15, pg, p3, pq = [fc(k) for k in range(5)]
    first, second, keep, odd, hi_, lo_ = [fc(k) for k in range(8, 14)]
    fill(v("EZ"), 0.0)
    fill(v("ED"), 0.0)
    fill(v("PAR", 2, 4), 0.0)
    cp("V", v("PAR", 0, 1), wtq)
    ts(v("EZ", 15, 143), J, pg, OP.is_equal)
    ts(v("EW"), v("EZ"), wtq, OP.mult)
    ts(v("PAR", 1, 2), v("TH", 1, 2), 256.0, OP.mult)
    ts(v("IDN"), J, pf, OP.is_equal)
    times(v("NID"), v("IDN"), -1.0)
    times(v("NF"), v("IDN"), -FAR)
    times(v("NF2"), v("IDN"), -2048 * FAR)
    times(v("EF"), v("EZ"), FAR)
    times(v("EF2"), v("EZ"), 2 * FAR)
    times(v("EFN"), v("EZ"), -FAR)
    ts(v("J15"), v("JI"), 15, AND)
    ts(v("JG", 0, 128), J, 112, AND)
    ts(v("MASK"), v("J15"), p15, OP.is_equal)
    ts(v("BB"), v("JG", 0, 128), pg, OP.is_equal)
    ts(v("KEEP"), v("J15"), 0.0, OP.not_equal)
    ts(first, p15, 0.0, OP.is_equal)
    ts(second, p15, 1.0, OP.is_equal)
    ts(keep, p15, 15.0, OP.not_equal)
    ts(odd, p15, 2.0, OP.mult, 1.0, OP.add)
    ts(ic(8), v("TH", 0, 1), 8128, AND)
    ts(ic(9), v("TH", 0, 1), 63, AND)
    ts(hi_, ic(8), first, OP.mult)
    ts(lo_, ic(9), -1.0, OP.add, second, OP.mult)
    ts(hi_, hi_, lo_, OP.add, -FAR, OP.mult)
    times(v("BL"), v("BB"), hi_)
    for a in range(NSEL, 16):
        times(sel(a), v("BB"), v("MASK", a, a + 1))
    ts(v("KK", 0, 1280, 5), v("QI"), pg, OP.subtract, 4 * RANK, OP.add)
    ts(v("QF", 0, 8), v("QI", 0, 8), pg, OP.subtract)
    ts(v("LE", 0, 8), v("QF", 0, 8), 32.0, OP.mult)
    tt(v("RE", 0, 128), v("TT0"), v("MASK", 0, 128), OP.mult)
    times(v("EN"), v("EZ"), -1.0)
    times(v("ER"), v("EZ"), 0.0625)
    times(v("EX"), v("EZ"), 256.0)
    times(v("EX2"), v("EZ"), 512.0)
    times(v("EXN"), v("EZ"), -256.0)
    tt(v("ED", 0, 143), v("EZ", 1, 144), v("EZ", 0, 143), OP.subtract)
    times(v("EDR"), v("ED"), 0.0625)
    ts(v("CD"), v("ONE"), 256.0, OP.mult, first, OP.subtract)
    for q in range(4):
        ts(fc(16 + q), pq, float(q), OP.is_equal, -4.0, OP.mult)
        times(v("DM", 128 * q, 128 * q + 128), v("IDN"), fc(16 + q))
    ts(v("RS"), v("J15", 0, 96), 0.0, OP.is_equal, 4 * RANK, OP.mult)

    def later():
        where(v("UT"), v("BB"), [[-1, 128]], OP.is_gt, 0, 1)
        where(v("LT"), v("BB"), [[1, 128]], OP.is_gt, 0, -1)
        iota(v("TT1"), [[2, 128]], 0, 0)
        for h in range(2):
            iota(v("NLIN", 96 * h, 96 * h + 96), [[1, 16], [16, 2], [32, 3]], 0, 0)
            iota(v("GW", 136 * h + 128, 136 * h + 136), [[0, 8]], 1 << 20, 0)
        for c in SEARCH_V:
            iota(v("JK", 136 * c + 128, 136 * c + 136), [[0, 8]], -128, 0)
        iota(v("NQ", 8, 14), [[16, 2], [32, 3]], 0, 0)
        iota(v("OF", 0, 6), [[0, 2], [RW, 3]], 1, 0)
        iota(v("FQ", 4, 8), [[1, 4]], 0, 0)
        iota(v("MK"), [[0, 6], [2, 16]], 1, 0)
        iota(v("K16"), [[16, 256]], 0, 0)
        ts(v("BW", 0, 128), v("TT1"), first, OP.add)
        cp("A", v("BW", 128, 136), v("CD", 0, 8))
        tt(v("VM", 0, 96), v("NLIN", 0, 96), v("MASK", 0, 96), OP.mult)
        scan(v("ZV", 0, 96), v("KEEP", 0, 96), v("VM", 0, 96), OP.mult, OP.add)
        cp("A", v("NW", 0, 6), v("ZV", 15, 96, 16))
        ts(v("NWH", 0, 6), v("ZV", 15, 96, 16), 0.5, OP.add)
        ts(v("NQ", 0, 6), v("NQ", 8, 14), p15, OP.add)
        ts(v("TN", 0, 6), v("NQ", 0, 6), 2.0, OP.mult, float(FREE), OP.add)
        times(v("FQ", 0, 4), v("FQ", 4, 8), 0.25)

    mate, near, diag = others(core)
    off = topo.engines(core, mate)
    both = topo.engines(core, near)
    on = [e for e in both if e not in off]

    sent, landed = [0], []

    def remote(transfers, local, reads):
        n = sum(len(es) for _, _, _, es, _ in transfers)

        def issue():
            order("G", reads, [])
            count[local] = count.get(local, 0) + n
            g.remote_dma_fused([RemoteDMATransfer(dst_ids=[dst(c)], dma_engine_mask=sum(1 << e for e in es), remote_sem=T.sem[rs], src=s, dst=d)
                                for c, s, d, es, rs in transfers], local_sem=T.sem[local])
            snap[(local, count[local])] = dict(known["G"])
            note("Gremote", reads, [], local, count[local])
        sent[0] += 1
        record("G", reads, [fc(31 + sent[0])], 1.0, 8.0, issue)
        return fc(31 + sent[0])

    def arrives(name, lo, hi, sem, n, like):
        def issue():
            count[sem] = n
            note("remote", [], [v(name, lo, hi)], sem, n)
        landed.append(fc(64 + len(landed)))
        record(None, [like], [v(name, lo, hi), landed[-1]], 0.0, 2.0, issue)

    def send_params():
        n = len(off) // 2
        call = remote([(c, ap(v("PAR")), T["PR%d" % slot(c, core)][:], es, "par")
                       for c, es in ((near, on), (mate, off[:n]), (diag, off[n:]))], "lpar", [v("PAR")])
        for d in range(3):
            arrives("PR%d" % d, 0, 4, "par", len(both), call)

    def halves():
        return [(h, 2048 * h, 2048 * h + 2048) for h in range(2)]

    def broadcast(rd, x):
        a, b = v(x, 0, 2048), v(x, 2048, W)
        call = remote([(mate, ap(a), ap(v("XR%d%d" % (rd, slot(mate, core)), 0, 2048)), off, "am%d0" % rd),
                       (porter[core], ap(b), ap(b), on, "ah%d" % rd)], "lx%d0" % rd, [a, b])
        remote([(near, ap(a), ap(v("XR%d%d" % (rd, slot(near, core)), 0, 2048)), on, "ap%d0" % rd)], "lx%d1" % rd, [a])
        for h, lo, hi in halves():
            arrives("XR%d%d" % (rd, slot(core, mate)), lo, hi, "am%d%d" % (rd, h), len(off), call)
            arrives("XR%d%d" % (rd, slot(core, near)), lo, hi, "ap%d%d" % (rd, h), len(on), call)

    def hand_on(rd):
        for h, lo, hi in halves():
            src = v("XR%d%d" % (rd, slot(core, mate)), lo, hi)
            call = remote([(near, ap(src), ap(v("XR%d%d" % (rd, slot(near, mate)), lo, hi)), both, "aq%d%d" % (rd, h))], "lf%d%d" % (rd, h), [src])
            arrives("XR%d%d" % (rd, slot(core, diag)), lo, hi, "aq%d%d" % (rd, h), len(both), call)

    def fold(rd, ks, x):
        local, es = "fl%d%d" % (rd, ks[0]), topo.engines(core, helper[core])
        srcs = {k: [v("GA%d" % k), v(x, 1024 * FOLDED[k][1], 1024 * FOLDED[k][1] + 1024)] for k in ks}
        reads = [s for k in ks for s in srcs[k]]

        def issue():
            order("G", reads, [])
            count[local] = len(es)
            g.remote_dma_fused([RemoteDMATransfer(dst_ids=[dst(helper[core])], dma_engine_mask=share(es, ks, k), remote_sem=T.sem["fo%d%d" % (rd, ks[0])],
                                                  srcs=[ap(s) for s in srcs[k]], dsts=[stop_over(rd, k)], alu_op=2) for k in ks], local_sem=T.sem[local])
            snap[(local, len(es))] = dict(known["G"])
            note("Gremote", reads, [], local, len(es))
        sent[0] += 1
        record("G", reads, [fc(31 + sent[0])], 1.0, TRIP - 3.0, issue)
        for k in ks:
            arrives("MX%d" % k, 0, 1024, "fb%d%d" % (rd, ks[0]), len(es), fc(31 + sent[0]))

    for a in range(2):
        where(sel(a), v("ONE"), [[-16, 8], [0, 16]], OP.is_equal, -a, 1)
    send_params()
    for rd in range(RO):
        X, Xn = ("XA", "XB") if rd % 2 == 0 else ("XB", "XA")
        XR = ["XR%d%d" % (rd, d) for d in range(3)]

        def again(q):
            if rd > 0 or (1024 * q, 1024 * q + 1024) not in AGAIN:
                where(v("XC", 1024 * q, 1024 * q + 1024), v(X, 1024 * q, 1024 * q + 1024), [[0, 1024]], OP.is_ge, 0, 0)
            if rd == 0 and q == 3:
                for a in range(2, NSEL):
                    where(sel(a), v("ONE"), [[-16, 8], [0, 16]], OP.is_equal, -a, 1)

        again(1)
        again(2)

        def sends():
            broadcast(rd, X)
            if rd == 0:
                later()
            hand_on(rd)
            iota(v("WA", 0, 1024), [[0, 1024]], 0, 0)
            iota(v("WB", 0, 1040), [[0, 1040]], 0, 0)

        def seg(q):
            return [s for s, (lo, hi) in enumerate(SEGS) if lo <= 64 * q < hi][0]

        def part(n, s, m0, m1, lo=None, hi=None):
            a, b = SEGS[s]
            if lo is None:
                return v(n, 4 * a + m0 * (b - a), 4 * a + m1 * (b - a))
            return v(n, 4 * a + m0 * (b - a) + lo - a, 4 * a + m0 * (b - a) + hi - a)

        def looks(s):
            lo, hi = SEGS[s]
            w, b = hi - lo, HASH[s]
            u, h, h1, u2 = v("UU", lo, hi), v("HI", lo, hi), pb(b, w, 2 * w), v("U2", lo, hi) if s in BY_SCALAR else pb(b, 0, w)
            keys = [v("KK", 5 * lo + 4 - m, 5 * hi, 5) for m in range(4)]
            calls = [lambda: cp("V", v("UI", lo, hi), pb(b, 0, w)),
                     lambda: ts(h, v("UI", lo, hi), 5, SHR, 127, AND),
                     lambda: ts(u, v("UI", lo, hi), W - 1, AND),
                     lambda: ts(h1, h, 1.0, OP.add),
                     lambda: act(u2, u, AF.Copy, bias=RANK, scale=2.0) if s in BY_SCALAR else ts(u2, u, 2.0, OP.mult, RANK, OP.add),
                     lambda: tt(keys[0], h1, u, OP.mult)]
            for m in range(4):
                calls.append(lambda m=m: ts(part("CC", s, m, m + 1), keys[m], W - 1, AND))
                if m < 3:
                    calls.append(lambda m=m: tt(keys[m + 1], u2, keys[m], OP.add))
                calls += [lambda m0=m0, m1=m1: cp("V", part("CL", s, m0, m1), part("CC", s, m0, m1)) for m0, m1 in LISTS[s] if m1 == m + 1]
            return calls

        dn, rest = [0], {}

        def sums(m, q, *parts):
            out = pb(2 + q, 4 - m, 320, 5)
            for e, n in parts:
                add_to((rd, q), [(out, ez(e, a), v(n, a, 1024, 16)) for a in range(16)])

        def gather(m, q):
            s = seg(q)
            win, x = ind(v(X, 0, W), part("CL", s, m, m + 1, 64 * q, 64 * q + 64)), (1024 * q, 1024 * q + 1024)
            if (m, q) in FOLDED:
                k = FOLDED.index((m, q))
                cp("V" if (m, q) in BY_VECTOR else "A", v("GA%d" % k), win)
                for ks in CALLS:
                    if k == ks[-1]:
                        fold(rd, ks, X)
                if k == len(FOLDED) - 1:
                    again(3)
                out = pb(2 + q, 4 - m, 320, 5)
                add_to((rd, q), [(out, v("NF"), v("SBH", 64 * q, 64 * q + 64)), (out, v("NF2"), v("ONE", 0, 64))])
                sums(m, q, ("EFN", "GA%d" % k))
                rest[m, q] = lambda: sums(m, q, ("EF2", "MX%d" % k))
            elif (m, q) in ON_SCALAR:
                b = "GS%d" % ON_SCALAR.index((m, q))
                for k in range(2):
                    mm(pb(6 + k), v("NID"), v(X, x[0] + 512 * k, x[0] + 512 * k + 512), True, False)
                cp("A", v(b), win)
                for k in range(2):
                    mm(pb(6 + k), v("IDN"), v(b, 512 * k, 512 * k + 512), False, True)
                rest[m, q] = lambda: (act(v(b), v("PD"), AF.Abs), sums(m, q, ("EF", b)))
            else:
                c = "DD%d" % (dn[0] % NDD)
                dn[0] += 1
                if (m, q) in HALVED:
                    for h in range(2):
                        d, o = v(c, 512 * h, 512 * h + 512), 64 * q + 32 * h
                        tt(d, ind(v(X, 0, W), part("CL", s, m, m + 1, o, o + 32)), v("XC", 16 * o, 16 * o + 512), OP.subtract)
                        act(d, d, AF.Abs)
                        out = pb(2 + q, 4 - m + 160 * h, 160 * h + 160, 5)
                        add_to((rd, q), [(out, ez("EF", a), v(c, 512 * h + a, 512 * h + 512, 16)) for a in range(16)])
                    rest[m, q] = lambda: None
                    return
                tt(v(c), win, v("XC", *x), OP.subtract)
                if (m, q) in ON_VECTOR:
                    sums(m, q, ("EFN", c))
                    rest[m, q] = lambda: (ts(v("GA0"), v(c), 0.0, OP.max), sums(m, q, ("EF2", "GA0")))
                else:
                    rest[m, q] = lambda: (act(v(c), v(c), AF.Abs), sums(m, q, ("EF", c)))

        def nearest(q):
            o = (64 * q, 64 * q + 64)
            scan(v("RUN", 320 * q, 320 * q + 320), pb(2 + q, 0, 320), v("KK", 320 * q, 320 * q + 320), OP.min, OP.max)
            ts(v("KI", *o), v("RUN", 320 * q + 4, 320 * q + 320, 5), 1.0, OP.add)
            ts(v("NXI", *o), v("KI", *o), W - 1, AND)
            ts(v("NXH", *o), v("NXI", *o), -2048.0, OP.add)
            cp("V", v("NXL", *o), v("NXI", *o))
            for b in range(2):
                each([(pb(SPREAD[q][b], a // 2, 512, 8), sel(a), v("NXH", *o)) for a in range(b, 16, 2)])

        def spread(q):
            for b in range(2):
                cp(COPIES[2 * q + b], v("NX1", 1024 * q + b, 1024 * q + 1024, 2), pb(SPREAD[q][b]))

        def own(lo, hi):
            group([(pb(6, lo, hi), ez("EZ", a), v(X, 16 * lo + a, 16 * hi, 16)) for a in range(16)])
            act(v("SBH", lo, hi), pb(6, lo, hi), AF.Copy, bias=-2048.0)

        i0 = len(ops)
        for s, (lo, hi) in enumerate(SEGS):
            group([(pb(HASH[s], 0, hi - lo), ez("EW", a), v(X, 16 * lo + a, 16 * hi, 16)) for a in range(16)])
        for q in range(4):
            mm(pb(2 + q, 0, 320), v("BL"), v("PAT"), True, False)
        for lo, hi in OWN:
            own(lo, hi)
        calls = [looks(s) for s in range(len(SEGS))]
        for word in ORDER.split():
            what, n = word[0], [int(x) for x in word[1:]]
            if what in "abc":
                for _ in range(int(word[1:])):
                    calls["abc".index(what)].pop(0)()
            elif what == "r":
                rest[tuple(n)]()
            else:
                {"g": gather, "n": nearest, "s": spread}[what](*n)
        listed.append((i0, len(ops)))
        sends()
        cp("V", v("NX2", 0, 2048), ind(v("NX1"), v("NXL", 0, 128)))
        cp("A", v("NX2", 2048, 4096), ind(v("NX1"), v("NXL", 128, 256)))

        def y0(k):
            l = v("LE" if k % 2 == 0 else "LO", 8 * (k // 2), 8 * (k // 2) + 8)
            cp("A", v("Y0", k, W, 32), ind(v(X, 0, W), l))

        steps = [[], []]

        def step(k, r, mat):
            h, a = k // 16, k % 16
            if a:
                mm(pb(h, 0, 128), ez(mat, a), r, False, k == steps[h])
            else:
                mm(pb(h, 0, 128), ez("EN", 0), r, False, False)
                if h:
                    mm(pb(0, 0, 128), ez("EZ", 15), r, False, k == steps[0])

        def flags(h):
            for lo, hi in ((0, 128),) if h else ((0, 64), (64, 128)):
                d, ne = pb(h, lo, hi), v("NE", lo, hi)
                if h:
                    ts(ne, d, 4096.0, OP.not_equal, keep, OP.mult)
                else:
                    ts(ne, d, 4096.0, OP.not_equal)
                tt(v("F%d" % h, lo, hi), d, ne, OP.min)
                ahead[len(ops) - 1] = 0.0 if h else SOON[2]

        steps[0], steps[1] = 16, 31
        for h in range(2):
            mm(pb(h, 0, 128), v("BB"), v("CD"), True, False)
        step(0, v("RE", 0, 128), "ED")
        for i in range(16):
            le = v("LE", 8 * i, 8 * i + 8)
            if i < 15:
                r, z = v("RE", 128 * i + 128, 128 * i + 256), "Z%d" % (i % 4)
                for lo, hi in CHAINS:
                    some = v("RE", 128 * i + 128 + 16 * lo, 128 * i + 128 + 16 * hi)
                    tt(some, ind(v("NX2"), v("LE", 8 * i + lo, 8 * i + hi)), v("MASK", 0, 16 * (hi - lo)), OP.mult)
                    scan(v(z, 16 * lo, 16 * hi), v("KEEP", 0, 16 * (hi - lo)), some, OP.mult, OP.add)
                    ts(v("LE", 8 * i + 8 + lo, 8 * i + 8 + hi), v(z, 16 * lo + 15, 16 * hi, 16), 2048.0, OP.add)
            else:
                for lo, hi in CHAINS:
                    tt(v("RL", 16 * lo, 16 * hi), ind(v("NX1"), v("LE", 8 * i + lo, 8 * i + hi)), v("MASK", 0, 16 * (hi - lo)), OP.mult)
                step(31, v("RL"), "ED")
                scan(v("Z3"), v("KEEP", 0, 128), v("RL"), OP.mult, OP.add)
                ts(v("LO", 120, 128), v("Z3", 15, 128, 16), 2048.0, OP.add)
                y0(31)
            y0(2 * i)
            for e, (j, n) in enumerate(ODD):
                if i == j + n - 1:
                    cp("A", v("RD", 128 * j, 128 * (j + n)), ind(v("NX1"), v("LE", 8 * j, 8 * j + 8 * n)))
                    for k in range(j, j + n):
                        step(2 * k + 1, v("RD", 128 * k, 128 * k + 128), "EDR")
                    o = pb(2 + e % 2, 0, 8 * n)
                    group([(o, ez("ER", a), v("RD", 128 * j + a, 128 * (j + n), 16)) for a in range(16)])
                    ts(v("LO", 8 * j, 8 * j + 8 * n), o, 2048.0, OP.add)
                    ahead[len(ops) - 1] = SOON[e]
                    for k in range(j, j + n):
                        y0(2 * k + 1)
            if i < 15:
                step(2 * i + 2, r, "ED")
            if i == 7:
                flags(0)
                mm(pb(4, 0, 128), v("BB"), v("F0"), True, False)
                mm(pb(5, 0, 128), v("UT"), v("F0"), True, False)
        flags(1)
        mm(pb(4, 0, 128), v("BB"), v("F1"), False, True)
        mm(pb(5, 0, 128), v("BB"), v("F1"), False, True)
        mm(pb(5, 128, 256), v("UT"), v("F1"))
        scan(v("END"), v("ONE"), pb(4, 0, 128), OP.mult, OP.add)
        for c in range(6):
            if c in SEARCH_V:
                ts(v("JK", 136 * c, 136 * c + 128), v("END"), v("NW", c, c + 1), OP.is_le, 2.0, OP.mult)
                reduce(v("ACC", c, c + 1), v("JK", 136 * c, 136 * c + 129), OP.add)
            else:
                act(v("JK", 136 * c, 136 * c + 128), v("END"), AF.Sign, bias=v("NWH", c, c + 1), scale=-1.0, total=v("ACC", c, c + 1))
        for h in range(2):
            tt(v("GW", 136 * h, 136 * h + 128), v("END"), pb(5, 128 * h, 128 * h + 128), OP.subtract)
        for h in range(2):
            ts(v("JL", 6 * h, 6 * h + 6), v("ACC", 0, 6), 0.5, OP.mult, 64.0 + 136 * h, OP.add)
        tt(v("CMP"), ind(v("GW"), v("JL", 0, 12)), v("NLIN"), OP.is_le)
        cp("A", v("BG"), ind(v("BW"), v("JL", 0, 6)))
        parts = (v("BG"), v("CMP", 0, 96), v("CMP", 96, 192))
        group([(pb(6, 0, 96), v("BB"), x) for x in parts])
        ts(v("PL"), pb(6, 0, 96), -1.0, OP.add)
        ops[-1][1].extend(landed)
        for c in range(6):
            group([(pb(7, 16 * c, 16 * c + 16), v("BB"), (x[0], x[1] + c, x[2], 6)) for x in parts])
        for d in range(3):
            ts(v("THR", d, 6, 3), v("NQ", d, 6, 3), v("END", 127, 128), OP.is_lt, v("PR%d" % d, 1, 2), OP.mult)
        cp("V", v("AR", 0, 768), ind(v("Y0"), v("PL", 0, 48)))
        cp("A", v("AR", 768, 1536), ind(v("Y0"), v("PL", 48, 96)))
        if rd == 0:
            for d in range(3):
                times(v("WB%d" % d), v("BB"), v("PR%d" % d, 0, 1))
        for d in range(3):
            o, i_ = v(XR[d], W, RW), v(XR[d], 0, RW - W)
            emit("A", "", [i_, v("PL")], [o], lambda e, o=o, i_=i_: e.activation(ap(o), ap(i_), AF.Copy))
        each([(pb(0, d, 96, 3), v("WB%d" % d), v("AR", 16 * d, 1536, 48)) for d in range(3)])
        each([(pb(5, 16 * c, 16 * c + 16), v("WB%d" % (c % 3)), v("AR", 16 * c, 1536, 96)) for c in range(6)])
        cp("V", v("AI"), pb(0, 0, 96))
        ts(v("AH"), v("AI"), 5, SHR, 127, AND)
        ts(v("AU"), v("AI"), W - 1, AND)
        ts(pb(0, 96, 192), v("AH"), odd, OP.add)
        tt(v("AT"), pb(0, 96, 192), v("AU"), OP.mult)
        ts(v("AC"), v("AT"), W - 1, AND)
        for d in range(3):
            ts(v("TL", d, 96, 3), v("AC", d, 96, 3), float(RW * d), OP.add)
        cp("V", v("RI"), pb(7, 0, 96))
        for k, b in enumerate((7, 5)):
            o = (96 * k, 96 * k + 96)
            tt(v("VM", *o), pb(b, 0, 96), v("MASK", 0, 96), OP.mult)
            scan(v("ZV", *o), v("KEEP", 0, 96), v("VM", *o), OP.mult, OP.add)
            cp("V", v("WI", 6 * k, 6 * k + 6), v("ZV", o[0] + 15, o[1], 16))
        ts(v("H6", 0, 6), v("WI", 6, 12), 5, SHR, 127, AND)
        ts(v("U6", 0, 6), v("WI", 6, 12), W - 1, AND)
        ts(v("Q6", 0, 6), v("WI", 0, 6), 2, SHR)
        ts(v("R6", 0, 6), v("WI", 0, 6), 3, AND)
        tt(v("QT", 0, 6), v("Q6", 0, 6), v("TN", 0, 6), OP.subtract)
        ts(v("R4", 0, 6), v("R6", 0, 6), 0.25, OP.mult)
        ts(v("RJ"), v("RI"), 3, AND)
        ts(v("VA"), v("RJ"), p3, OP.is_le)
        ts(v("VB"), v("RJ"), p3, OP.is_gt)
        ky = pb(2, 0, 96)
        mm(ky, v("IDN"), v("MK"), True, False)
        for k, (a0, a1) in enumerate(ASKED):
            lo, hi = 96 * a0, 96 * a1
            o, win = v("AD", lo, hi), ind(v("XR%d" % rd), v("TL", 6 * a0, 6 * a1))
            sums = [("EX", "AD", 0)]
            if k == 2:
                mm(pb(1, 0, hi - lo), v("NID"), v("AR", lo, hi), True, False)
                cp("A", v("GB", 0, hi - lo), win)
                mm(pb(1, 0, hi - lo), v("IDN"), v("GB", 0, hi - lo), False, True)
                act(o, pb(1, 0, hi - lo), AF.Abs)
            else:
                tt(o, win, v("AR", lo, hi), OP.subtract)
                if k == 0:
                    act(o, o, AF.Abs)
                else:
                    ts(v("DP", 0, hi - lo), o, 0.0, OP.max)
                    sums = [("EXN", "AD", 0), ("EX2", "DP", -lo)]
            for e, x, o in sums:
                add_to((rd, "key"), [(ky, ez(e, a), v(x, o + 96 * a, o + 96 * a + 96)) for a in range(a0, a1)])
        scan(v("KM"), v("RS"), ky, OP.add, OP.min)
        km, fd = v("KM", 15, 96, 16), v("FD", 0, 6)
        tt(fd, km, v("THR", 0, 6), OP.is_lt)
        group([(pb(5, 0, 6), v("LT"), fd)] + [(pb(5, 3 * e + k, 3 * e + 3), v("BB"), v("FD", 3 * f, 3 * f + 3 - k))
                                              for e in range(2) for f in range(2) for k in range(0 if e > f else 1, 3)])
        tt(v("QQ", 0, 6), fd, v("QT", 0, 6), OP.mult)
        tt(v("QQ", 0, 6), v("QQ", 0, 6), v("TN", 0, 6), OP.add)
        tt(v("SS", 0, 6), pb(5, 0, 6), v("QQ", 0, 6), OP.add)
        cp("V", v("SL", 0, 6), v("SS", 0, 6))
        cp("V", v("K6", 0, 6), km)
        ts(v("S6", 0, 6), v("K6", 0, 6), 255, AND)
        tt(v("S6", 0, 6), v("S6", 0, 6), v("H6", 0, 6), OP.add)
        tt(v("T6", 0, 6), v("S6", 0, 6), v("U6", 0, 6), OP.mult)
        ts(v("C6", 0, 6), v("T6", 0, 6), W - 1, AND)
        tt(v("CQ", 0, 6), v("C6", 0, 6), v("OF", 0, 6), OP.add)
        for c in range(6):
            act(v("FIF", 4 * c, 4 * c + 4), v("FQ", 4, 8), AF.Identity, bias=v("CQ", c, c + 1))
        cp("V", v("FL", 0, 24), v("FIF", 0, 24))
        cp("A", v("FB"), ind(v("XR%d" % rd), v("FL", 0, 24)))
        tt(v("PQ", 0, 6), v("SS", 0, 6), v("R4", 0, 6), OP.add)
        for c in range(6):
            act(v("FPF", 4 * c, 4 * c + 4), v("FQ", 0, 4), AF.Identity, bias=v("PQ", c, c + 1))
        ts(v("FP", 0, 24), v("FPF", 0, 24), 4.0, OP.mult)
        cp("V", ind(v("WA"), v("SL", 0, 6)), v("VA"))
        cp("V", ind(v("WB", 16, 1424), v("SL", 0, 6)), v("VB"))
        for s, (lo, hi) in enumerate(((0, CUT), (CUT, 256))):
            init = 0.0 if s == 0 else v("ZS", 4 * lo - 1, 4 * lo)
            scan(v("ZS", 4 * lo, 4 * hi), v("WA", 4 * lo, 4 * hi), v("WB", 4 * lo + 15, 4 * hi + 15), OP.add, OP.add, init)
            o = pb(6 + s, 0, hi - lo)
            group([(o, v("IDN"), v("K16", lo, hi))] + [(o, v("DM", 128 * q, 128 * q + 128), v("ZS", 4 * lo + q, 4 * hi, 4)) for q in range(4)])
            ts(v("SRL", lo, hi), o, p15, OP.add)
            if rd < RO - 1:
                cp("AV"[s], v(Xn, 16 * lo, 16 * hi), ind(v("Y0"), v("SRL", lo, hi)))
        if rd < RO - 1:
            cp("V", ind(v(Xn), v("FP", 0, 24)), v("FB"))
            continue
        for x, pieces in zip((Xn, X), LAST):
            for q, lo, hi in pieces:
                cp(q, v(x, 16 * lo, 16 * hi), ind(v("Y0"), v("SRL", lo, hi)))
            cp("V", ind(v(x), v("FP", 0, 24)), v("FB"))
            lo, hi = 16 * pieces[0][1], 16 * pieces[-1][2]
            dma("S", T.y[:, lo:hi], ap(v(x, lo, hi)), [v(x, lo, hi)], [], 2.1 + 0.0008 * (hi - lo))
    if not PLAN:
        PLAN.extend(plan())
    for i in PLAN:
        now[0] = i
        ops[i][5]()
    for s in SEMAPHORES:
        if count.get(s, 0):
            wait("G", s, count[s])
